import numpy as np
import ml_dtypes


def mxq(x, axis, fmt="e4m3"):
    dtype, down = {"e4m3": (ml_dtypes.float8_e4m3fn, 7), "e5m2": (ml_dtypes.float8_e5m2, 14)}[fmt]
    v = np.moveaxis(np.asarray(x, np.float32).astype(ml_dtypes.bfloat16).astype(np.float64), axis, -1)
    blocks = v.reshape(v.shape[:-1] + (-1, 32))
    amax = np.abs(blocks).max(-1, keepdims=True)
    byte = np.maximum(np.where(amax > 0, np.frexp(amax)[1] - 1 + 127, 0) - down, 1)
    scale = np.exp2(byte - 127.0)
    codes = (blocks / scale).astype(np.float32).astype(dtype).astype(np.float64)
    return np.moveaxis((codes * scale).reshape(v.shape), -1, axis)


WIDE = False


def mx_kscale(k):
    if not WIDE:
        return np.ones(k)
    levels = np.array([10, -10, 5, -5, 0])
    if k % 512:
        return np.exp2(np.random.permutation(np.resize(levels, k // 32))).repeat(32)
    a = np.empty((k // 512, 16))
    for p in range(k // 512):
        a[p, :8] = np.random.permutation(np.resize(levels, 8))
        for g in range(8):
            far = levels[np.abs(levels - a[p, g]) >= 10]
            a[p, g + 8] = far[np.random.randint(len(far))]
    return np.exp2(a.ravel()).repeat(32)


def f64(x):
    return np.asarray(x).astype(np.float64)


def striped(idx):
    return np.tile(idx.reshape(-1, 16).T, (8, 1)).astype(np.uint16)


def unstriped(offs):
    return offs[:16].T.reshape(-1).astype(np.int64)


E2M1 = np.array([0.0, 0.5, 1.0, 1.5, 2.0, 3.0, 4.0, 6.0, -0.0, -0.5, -1.0, -1.5, -2.0, -3.0, -4.0, -6.0])


def pack_weight(w, fmt):
    k, n = w.shape
    w = f64(np.asarray(w, np.float32).astype(ml_dtypes.bfloat16)).reshape(k // 32, 32, n)
    amax = np.abs(w).max(1)
    if fmt == "e4m3":
        byte = np.frexp(amax)[1] - 1 + 127 - 7
    else:
        mant, ex = np.frexp(amax / 6.0)
        byte = np.where(mant > 0.5, ex, ex - 1) + 127
    byte = np.clip(np.where(amax > 0, byte, 1), 1, 254)
    scaled = (w * np.exp2(127.0 - byte)[:, None, :]).reshape(k, n).astype(np.float32)
    by_word = np.ascontiguousarray(scaled.reshape(k // 512, 128, 4, n).transpose(0, 1, 3, 2))
    if fmt == "e4m3":
        words = by_word.astype(ml_dtypes.float8_e4m3fn).view(np.uint8)
    else:
        c = by_word.astype(ml_dtypes.float4_e2m1fn).view(np.uint8) & 0xF
        words = (c[..., 0::2] | (c[..., 1::2] << 4)).reshape(k // 512, 128, 2 * n)
    return np.ascontiguousarray(words), np.ascontiguousarray(byte.astype(np.uint8).reshape(k // 512, 16, n))


def unpack_weight(words, scales, fmt):
    g, _, n = scales.shape
    words = np.ascontiguousarray(words).reshape(g, 128, n, -1)
    if fmt == "e4m3":
        vals = words.view(ml_dtypes.float8_e4m3fn).astype(np.float64)
    else:
        nib = np.empty((g, 128, n, 4), np.uint8)
        nib[..., 0::2] = words & 0xF
        nib[..., 1::2] = words >> 4
        vals = E2M1[nib]
    vals = vals * np.repeat(np.exp2(scales.astype(np.float64) - 127.0), 8, axis=1)[..., None]
    return vals.transpose(0, 1, 3, 2).reshape(g * 512, n)


def gelu(v):
    return 0.5 * v * (1.0 + np.tanh(np.sqrt(2.0 / np.pi) * (v + 0.044715 * v**3)))


def striped8(idx):
    return np.concatenate([v.reshape(-1, 16).T for v in idx]).astype(np.uint16)


def unstriped8(offs):
    return np.stack([offs[16 * g:16 * g + 16].T.reshape(-1) for g in range(8)]).astype(np.int64)


def heads(xT, wgt, idx8):
    k = np.arange(xT.shape[0])
    return wgt[k // 4 % 128] * xT[k[:, None], idx8[k % 512 // 64]]


K, T, S, H, N = 1024, 2048, 1024, 1024, 512


def setup_inputs():
    n = np.random.standard_normal
    s = mx_kscale(K)[:, None]
    u = mx_kscale(H)[:, None]
    xT = (n((K, T)) * s).astype(np.float32)
    wgt = np.repeat(np.random.uniform(0.5, 2.0, (8, S)), 16, axis=0).astype(np.float32)
    offs = striped8(np.stack([np.random.permutation(T)[:S] for _ in range(8)]))
    wa_words, wa_scales = pack_weight(n((K, H)) / np.sqrt(K) / s * u.T, "e2m1")
    ba = (0.5 * n(H) * u[:, 0]).astype(np.float32)
    wb = (n((K, H)) / np.sqrt(K) / s).astype(np.float32)
    bb = (0.5 * n(H)).astype(np.float32)
    wo = (n((H, N)) / np.sqrt(H) / u).astype(np.float32)
    bo = (0.5 * n(N)).astype(np.float32)
    return {"xT": xT, "wgt": wgt, "offs": offs, "wa_words": wa_words, "wa_scales": wa_scales,
            "ba": ba, "wb": wb, "bb": bb, "wo": wo, "bo": bo}


def reference(xT, wgt, offs, wa_words, wa_scales, ba, wb, bb, wo, bo):
    xg = heads(f64(xT), f64(wgt), unstriped8(offs))
    xq = mxq(xg, 0, "e4m3")
    wa = unpack_weight(wa_words, wa_scales, "e2m1")
    a = (wa.T @ xq) + f64(ba)[:, None]
    b = (mxq(f64(wb), 0, "e4m3").T @ xq) + f64(bb)[:, None]
    h = a * b
    y = mxq(f64(wo), 0, "e4m3").T @ mxq(h, 0, "e4m3")
    return y + f64(bo)[:, None]

@@ -1,0 +1,291 @@
+from contextlib import ExitStack
+
+import concourse.mybir as mybir
+from concourse.masks import make_identity
+
+K, T, S, H, N = 1024, 2048, 1024, 1024, 512
+FLOPS = 2 * S * (2 * K * H + H * N)
+
+F32 = mybir.dt.float32
+BF16 = mybir.dt.bfloat16
+I32 = mybir.dt.int32
+U32 = mybir.dt.uint32
+U16 = mybir.dt.uint16
+U8 = mybir.dt.uint8
+FP8X4 = mybir.dt.float8_e4m3fn_x4
+FP4X4 = mybir.dt.float4_e2m1fn_x4
+MULT = mybir.AluOpType.mult
+ADD = mybir.AluOpType.add
+IDENTITY = mybir.ActivationFunctionType.Identity
+
+P = 128
+PACK = 4
+W = 512
+PASSES = K // W
+BLOCKS = H // W
+HALVES = S // W
+OUT_TILES = N // P
+BA_COL, BB_COL, BO_COL = 0, 4, 8
+BIAS_COLS = 12
+
+
+def tile_list_hashed_click_logits_kernel(tc, xT, wgt, offs, wa_words, wa_scales, ba, wb, bb, wo, bo, out):
+    nc = tc.nc
+    with ExitStack() as ctx:
+        keep = ctx.enter_context(tc.tile_pool(name="keep", bufs=1))
+        psum = ctx.enter_context(tc.psum_pool(name="psum", bufs=1))
+
+        def f32_quad(tag):
+            return keep.tile([P, PACK, W], F32, name=tag, tag=tag)
+
+        def bf16_words(tag):
+            return keep.tile([P, PACK * W], BF16, name=tag, tag=tag, align_bytes=64)
+
+        def mx_operand(tag):
+            codes = keep.tile([P, W], U32, name=tag + "_codes", align_bytes=64)
+            scales = keep.tile([P, W], U8, name=tag + "_scales", align_bytes=64)
+            return codes, scales
+
+        def copy_on(engine, dst, src):
+            if engine == "vector":
+                nc.vector.tensor_copy(out=dst, in_=src)
+            else:
+                nc.scalar.copy(out=dst, in_=src)
+
+        def slots_walk(quad):
+            return quad.rearrange("p t (c e) -> p c t e", e=PACK)
+
+        def words_walk(words):
+            return words.rearrange("p (c e t) -> p c t e", e=PACK, t=PACK)
+
+        def quantize(operand, words):
+            codes, scales = operand
+            nc.vector.quantize_mx(out=codes[:].bitcast(FP8X4), scales=scales[:], in_=words[:])
+
+        banks = [psum.tile([P, W], F32, name="bank%d" % n) for n in range(8)]
+
+        offsets = keep.tile([P, S // 16], U16, name="offsets")
+        weights = [keep.tile([P, W], F32, name="wgt%d" % h) for h in range(HALVES)]
+        planes = [keep.tile([P, T], F32, name="plane%d" % n) for n in range(PASSES * PACK)]
+        wa_raw = keep.tile([P, PASSES * 2 * H], U8, name="wa_raw")
+        wa_scale_raw = keep.tile([P, PASSES * H], U8, name="wa_scale_raw")
+        wa_codes = keep.tile([P, PASSES * 2 * H], U8, name="wa_codes", align_bytes=64)
+        wa_scale = keep.tile([P, PASSES * H], U8, name="wa_scale", align_bytes=64)
+        bias_rows = keep.tile([P, BLOCKS * P], F32, name="bias_rows")
+        identity = keep.tile([P, P], F32, name="identity")
+        bias = keep.tile([P, BLOCKS * BIAS_COLS], F32, name="bias")
+
+        def load_plane(a, i):
+            rows = xT[a * W : (a + 1) * W, :].rearrange("(p i) t -> i p t", i=PACK)
+            nc.sync.dma_start(out=planes[a * PACK + i][:], in_=rows[i])
+
+        def load_wa_scales(q):
+            nc.sync.dma_start(
+                out=wa_scale_raw[32 * q : 32 * q + 4, :].bitcast(I32).rearrange("p (a n) -> p a n", a=PASSES),
+                in_=wa_scales.bitcast(I32)[:, 4 * q : 4 * q + 4, :].rearrange("a r n -> r a n"),
+            )
+
+        def load_bias(vec, row):
+            nc.sync.dma_start(
+                out=bias_rows[row : row + PACK, :].rearrange("t (g i) -> t g i", i=PACK),
+                in_=vec.rearrange("(g t i) -> t g i", t=PACK, i=PACK),
+            )
+
+        wb_raw, wo_raw = {}, {}
+
+        def load_wb(a, b):
+            wb_raw[a, b] = f32_quad("wb_raw%d%d" % (a, b))
+            nc.sync.dma_start(
+                out=wb_raw[a, b][:],
+                in_=wb[a * W : (a + 1) * W, b * W : (b + 1) * W].rearrange("(p j) r -> p j r", j=PACK),
+            )
+
+        def load_wo(b):
+            wo_raw[b] = f32_quad("wo_raw%d" % b)
+            rows = wo[b * W : (b + 1) * W, :].rearrange("(g t i) n -> i g t n", t=PACK, i=PACK)
+            for i in range(PACK):
+                nc.sync.dma_start(out=wo_raw[b][i:P:PACK, :, :], in_=rows[i])
+
+        nc.gpsimd.memset(bias_rows[:], 0.0)
+        nc.gpsimd.memset(wa_scale_raw[:].bitcast(I32), 0)
+        make_identity(nc, identity[:])
+        nc.sync.dma_start(offsets[:], offs)
+        load_plane(0, 0)
+        nc.sync.dma_start(out=weights[0][:], in_=wgt[:, 0:W])
+        nc.sync.dma_start(out=weights[1][:], in_=wgt[:, W : 2 * W])
+        load_plane(0, 1)
+        load_bias(ba, BA_COL)
+        load_plane(0, 2)
+        load_bias(bb, BB_COL)
+        load_plane(0, 3)
+        nc.sync.dma_start(out=bias_rows[BO_COL : BO_COL + OUT_TILES, 0:P], in_=bo.rearrange("(c p) -> c p", p=P))
+        nc.sync.dma_start(
+            out=wa_raw[:].bitcast(I32).rearrange("p (a n) -> p a n", a=PASSES),
+            in_=wa_words.bitcast(I32).rearrange("a p n -> p a n"),
+        )
+        load_wa_scales(0)
+        load_wa_scales(1)
+        load_plane(1, 0)
+        load_wa_scales(2)
+        load_wa_scales(3)
+        for i in range(1, PACK):
+            load_plane(1, i)
+        for b in range(BLOCKS):
+            for a in range(PASSES):
+                load_wb(a, b)
+        for b in range(BLOCKS):
+            load_wo(b)
+
+        for b in range(BLOCKS):
+            nc.tensor.transpose(banks[7][:, b * P : (b + 1) * P], bias_rows[:, b * P : (b + 1) * P], identity[:])
+        nc.scalar.activation(
+            out=bias[:].rearrange("p (b c) -> p b c", b=BLOCKS),
+            in_=banks[7][:, 0 : BLOCKS * P].rearrange("p (b c) -> p b c", b=BLOCKS)[:, :, 0:BIAS_COLS],
+            func=IDENTITY,
+        )
+
+        picked, xq, wbq, woq, hq, a_sb = {}, {}, {}, {}, {}, {}
+
+        def gather(a, i, h):
+            if i == 0:
+                picked[a, h] = f32_quad("quad%d%d" % (a, h))
+            window = planes[a * PACK + i][:].indirect(offsets[:, h * (W // 16) : (h + 1) * (W // 16)])
+            nc.vector.tensor_tensor(picked[a, h][:, i, :], window, weights[h][:], MULT)
+
+        def quantize_x(a, h):
+            words = bf16_words("words%d" % h)
+            copy_on("scalar", words_walk(words[:]), slots_walk(picked[a, h][:]))
+            xq[a, h] = mx_operand("xq%d%d" % (a, h))
+            quantize(xq[a, h], words)
+
+        def permute_wa():
+            nc.vector.tensor_copy(
+                out=wa_codes[:].bitcast(I32).rearrange("p (c t g u) -> p c t g u", t=PACK, g=32, u=2),
+                in_=wa_raw[:].bitcast(I32).rearrange("p (c g t u) -> p c t g u", t=PACK, g=32, u=2),
+            )
+            nc.vector.tensor_copy(
+                out=wa_scale[:].bitcast(I32).rearrange("p (c t g) -> p c t g", t=PACK, g=32),
+                in_=wa_scale_raw[:].bitcast(I32).rearrange("p (c g t) -> p c t g", t=PACK, g=32),
+            )
+
+        def quantize_wb(a, b, engine):
+            words = bf16_words("wwords%d" % a)
+            copy_on(
+                engine,
+                words[:].rearrange("p (t g i j) -> p t g j i", t=PACK, i=PACK, j=PACK),
+                wb_raw[a, b][:].rearrange("p j (g t i) -> p t g j i", t=PACK, i=PACK),
+            )
+            wbq[a, b] = mx_operand("wbq%d%d" % (a, b))
+            quantize(wbq[a, b], words)
+
+        def quantize_wo(b, engine):
+            words = bf16_words("wwords%d" % b)
+            copy_on(engine, words_walk(words[:]), slots_walk(wo_raw[b][:]))
+            woq[b] = mx_operand("woq%d" % b)
+            quantize(woq[b], words)
+
+        def a_pass(b, h, a, side):
+            for t in range(PACK):
+                col = a * H + b * W + t * P
+                nc.tensor.matmul_mx(
+                    out=banks[side + t][:],
+                    lhsT=wa_codes[:, 2 * col : 2 * (col + P)].bitcast(FP4X4),
+                    lhsT_scale=wa_scale[:, col : col + P],
+                    rhs=xq[a, h][0][:].bitcast(FP8X4),
+                    rhs_scale=xq[a, h][1][:],
+                    start=(a == 0),
+                    stop=(a == PASSES - 1),
+                )
+
+        def a_out(b, h, side, tag):
+            a_sb[b, h] = f32_quad(tag)
+            for t in range(PACK):
+                col = BIAS_COLS * b + BA_COL + t
+                nc.scalar.activation(out=a_sb[b, h][:, t, :], in_=banks[side + t][:], func=IDENTITY, bias=bias[:, col : col + 1])
+
+        def mx_group(bank, stationary, cols, moving):
+            for n in range(len(moving)):
+                nc.tensor.matmul_mx(
+                    out=bank[:],
+                    lhsT=stationary[n][0][:, cols].bitcast(FP8X4),
+                    lhsT_scale=stationary[n][1][:, cols],
+                    rhs=moving[n][0][:].bitcast(FP8X4),
+                    rhs_scale=moving[n][1][:],
+                    start=(n == 0),
+                    stop=(n == len(moving) - 1),
+                )
+
+        def b_product(b, h, side):
+            for t in range(PACK):
+                mx_group(banks[side + t], [wbq[a, b] for a in range(PASSES)], slice(t * P, (t + 1) * P), [xq[a, h] for a in range(PASSES)])
+
+        def h_on_vector(b, h, side):
+            slots = keep.tile([P, PACK, W], BF16, name="h_slots", tag="h_slots")
+            for t in range(PACK):
+                col = BIAS_COLS * b + BB_COL + t
+                nc.vector.scalar_tensor_tensor(
+                    out=slots[:, t, :], in0=banks[side + t][:], scalar=bias[:, col : col + 1], in1=a_sb[b, h][:, t, :], op0=ADD, op1=MULT
+                )
+            words = bf16_words("words%d" % h)
+            nc.vector.tensor_copy(out=words_walk(words[:]), in_=slots_walk(slots[:]))
+            hq[b, h] = mx_operand("hq%d%d" % (b, h))
+            quantize(hq[b, h], words)
+
+        def h_shared(b, h, side):
+            b_sb = f32_quad("wb_raw%d0" % h)
+            for t in range(PACK):
+                col = BIAS_COLS * b + BB_COL + t
+                nc.scalar.activation(out=b_sb[:, t, :], in_=banks[side + t][:], func=IDENTITY, bias=bias[:, col : col + 1])
+            words = bf16_words("words%d" % h)
+            nc.vector.tensor_tensor(words_walk(words[:]), slots_walk(a_sb[b, h][:]), slots_walk(b_sb[:]), MULT)
+            hq[b, h] = mx_operand("hq%d%d" % (b, h))
+            quantize(hq[b, h], words)
+
+        def logits(h, side):
+            result = f32_quad("wo_raw%d" % h)
+            for c in range(OUT_TILES):
+                mx_group(banks[side + c], [woq[b] for b in range(BLOCKS)], slice(c * P, (c + 1) * P), [hq[b, h] for b in range(BLOCKS)])
+                nc.scalar.activation(out=result[:, c, :], in_=banks[side + c][:], func=IDENTITY, bias=bias[:, BO_COL + c : BO_COL + c + 1])
+                nc.sync.dma_start(out=out[c * P : (c + 1) * P, h * W : (h + 1) * W], in_=result[:, c, :])
+
+        for i in range(PACK):
+            for h in range(HALVES):
+                gather(0, i, h)
+        quantize_x(0, 0)
+        gather(1, 0, 0)
+        permute_wa()
+        a_pass(0, 0, 0, 0)
+        a_pass(1, 0, 0, 4)
+        quantize_x(0, 1)
+        gather(1, 0, 1)
+        for i in range(1, PACK):
+            for h in range(HALVES):
+                gather(1, i, h)
+        quantize_x(1, 0)
+        a_pass(0, 0, 1, 0)
+        a_pass(1, 0, 1, 4)
+        quantize_wb(0, 0, "vector")
+        quantize_x(1, 1)
+        a_out(0, 0, 0, "quad00")
+        quantize_wb(1, 0, "vector")
+        b_product(0, 0, 0)
+        a_out(1, 0, 4, "quad01")
+        for a in range(PASSES):
+            a_pass(0, 1, a, 4)
+        h_on_vector(0, 0, 0)
+        a_out(0, 1, 4, "quad10")
+        quantize_wb(0, 1, "vector")
+        b_product(0, 1, 0)
+        for a in range(PASSES):
+            a_pass(1, 1, a, 4)
+        quantize_wb(1, 1, "vector")
+        h_on_vector(0, 1, 0)
+        a_out(1, 1, 4, "quad11")
+        quantize_wo(0, "scalar")
+        b_product(1, 0, 0)
+        h_shared(1, 0, 0)
+        quantize_wo(1, "scalar")
+        b_product(1, 1, 4)
+        h_shared(1, 1, 4)
+        logits(0, 0)
+        logits(1, 4)

@@ -27,6 +27,8 @@ HALVES = S // W
 OUT_TILES = N // P
 BA_COL, BB_COL, BO_COL = 0, 4, 8
 BIAS_COLS = 12
+B_SIDE = 4
+PICK_TAG = {(0, 0): "quad00", (0, 1): "quad01", (1, 0): "quad10", (1, 1): "quad11"}
 
 
 def tile_list_hashed_click_logits_kernel(tc, xT, wgt, offs, wa_words, wa_scales, ba, wb, bb, wo, bo, out):
@@ -65,7 +67,7 @@ def tile_list_hashed_click_logits_kernel(tc, xT, wgt, offs, wa_words, wa_scales,
         banks = [psum.tile([P, W], F32, name="bank%d" % n) for n in range(8)]
 
         offsets = keep.tile([P, S // 16], U16, name="offsets")
-        weights = [keep.tile([P, W], F32, name="wgt%d" % h) for h in range(HALVES)]
+        weights = [keep.tile([P, W], F32, name="wgt%d" % h, tag="wgt%d" % h) for h in range(HALVES)]
         planes = [keep.tile([P, T], F32, name="plane%d" % n) for n in range(PASSES * PACK)]
         wa_raw = keep.tile([P, PASSES * 2 * H], U8, name="wa_raw")
         wa_scale_raw = keep.tile([P, PASSES * H], U8, name="wa_scale_raw")
@@ -119,20 +121,22 @@ def tile_list_hashed_click_logits_kernel(tc, xT, wgt, offs, wa_words, wa_scales,
         load_bias(bb, BB_COL)
         load_plane(0, 3)
         nc.sync.dma_start(out=bias_rows[BO_COL : BO_COL + OUT_TILES, 0:P], in_=bo.rearrange("(c p) -> c p", p=P))
+        load_plane(1, 0)
+        load_wa_scales(0)
+        load_wb(0, 0)
+        load_wa_scales(1)
+        load_plane(1, 1)
+        load_wa_scales(2)
+        load_wb(1, 0)
+        load_wa_scales(3)
+        load_plane(1, 2)
         nc.sync.dma_start(
             out=wa_raw[:].bitcast(I32).rearrange("p (a n) -> p a n", a=PASSES),
             in_=wa_words.bitcast(I32).rearrange("a p n -> p a n"),
         )
-        load_wa_scales(0)
-        load_wa_scales(1)
-        load_plane(1, 0)
-        load_wa_scales(2)
-        load_wa_scales(3)
-        for i in range(1, PACK):
-            load_plane(1, i)
-        for b in range(BLOCKS):
-            for a in range(PASSES):
-                load_wb(a, b)
+        load_plane(1, 3)
+        load_wb(0, 1)
+        load_wb(1, 1)
         for b in range(BLOCKS):
             load_wo(b)
 
@@ -148,13 +152,15 @@ def tile_list_hashed_click_logits_kernel(tc, xT, wgt, offs, wa_words, wa_scales,
 
         def gather(a, i, h):
             if i == 0:
-                picked[a, h] = f32_quad("quad%d%d" % (a, h))
+                picked[a, h] = f32_quad(PICK_TAG[a, h])
             window = planes[a * PACK + i][:].indirect(offsets[:, h * (W // 16) : (h + 1) * (W // 16)])
             nc.vector.tensor_tensor(picked[a, h][:, i, :], window, weights[h][:], MULT)
 
-        def quantize_x(a, h):
+        def quantize_x(a, h, on_scalar=W):
             words = bf16_words("words%d" % h)
-            copy_on("scalar", words_walk(words[:]), slots_walk(picked[a, h][:]))
+            copy_on("scalar", words_walk(words[:, 0 : on_scalar * PACK]), slots_walk(picked[a, h][:, :, 0:on_scalar]))
+            if on_scalar < W:
+                copy_on("vector", words_walk(words[:, on_scalar * PACK :]), slots_walk(picked[a, h][:, :, on_scalar:]))
             xq[a, h] = mx_operand("xq%d%d" % (a, h))
             quantize(xq[a, h], words)
 
@@ -219,73 +225,120 @@ def tile_list_hashed_click_logits_kernel(tc, xT, wgt, offs, wa_words, wa_scales,
             for t in range(PACK):
                 mx_group(banks[side + t], [wbq[a, b] for a in range(PASSES)], slice(t * P, (t + 1) * P), [xq[a, h] for a in range(PASSES)])
 
-        def h_on_vector(b, h, side):
-            slots = keep.tile([P, PACK, W], BF16, name="h_slots", tag="h_slots")
+        h_slots, h_words = {}, {}
+
+        def h_product(b, h, side, cols=slice(0, W)):
+            if cols.start == 0:
+                h_slots[b, h] = keep.tile([P, PACK, W], BF16, name="h_slots%d" % b, tag="h_slots%d" % b)
             for t in range(PACK):
                 col = BIAS_COLS * b + BB_COL + t
                 nc.vector.scalar_tensor_tensor(
-                    out=slots[:, t, :], in0=banks[side + t][:], scalar=bias[:, col : col + 1], in1=a_sb[b, h][:, t, :], op0=ADD, op1=MULT
+                    out=h_slots[b, h][:, t, cols],
+                    in0=banks[side + t][:, cols],
+                    scalar=bias[:, col : col + 1],
+                    in1=a_sb[b, h][:, t, cols],
+                    op0=ADD,
+                    op1=MULT,
                 )
-            words = bf16_words("words%d" % h)
-            nc.vector.tensor_copy(out=words_walk(words[:]), in_=slots_walk(slots[:]))
-            hq[b, h] = mx_operand("hq%d%d" % (b, h))
-            quantize(hq[b, h], words)
 
-        def h_shared(b, h, side):
-            b_sb = f32_quad("wb_raw%d0" % h)
-            for t in range(PACK):
-                col = BIAS_COLS * b + BB_COL + t
-                nc.scalar.activation(out=b_sb[:, t, :], in_=banks[side + t][:], func=IDENTITY, bias=bias[:, col : col + 1])
-            words = bf16_words("words%d" % h)
-            nc.vector.tensor_tensor(words_walk(words[:]), slots_walk(a_sb[b, h][:]), slots_walk(b_sb[:]), MULT)
-            hq[b, h] = mx_operand("hq%d%d" % (b, h))
-            quantize(hq[b, h], words)
+        def quantize_h(b, h, engine, cols=slice(0, W)):
+            if cols.start == 0:
+                h_words[b, h] = bf16_words("words%d" % b)
+                hq[b, h] = mx_operand("hq%d%d" % (b, h))
+            piece = h_words[b, h][:, cols.start * PACK : cols.stop * PACK]
+            copy_on(engine, words_walk(piece), slots_walk(h_slots[b, h][:, :, cols]))
+            nc.vector.quantize_mx(out=hq[b, h][0][:, cols].bitcast(FP8X4), scales=hq[b, h][1][:, cols], in_=piece)
 
-        def logits(h, side):
-            result = f32_quad("wo_raw%d" % h)
+        def logit_pass(b, h, side, cols=slice(0, W)):
             for c in range(OUT_TILES):
-                mx_group(banks[side + c], [woq[b] for b in range(BLOCKS)], slice(c * P, (c + 1) * P), [hq[b, h] for b in range(BLOCKS)])
-                nc.scalar.activation(out=result[:, c, :], in_=banks[side + c][:], func=IDENTITY, bias=bias[:, BO_COL + c : BO_COL + c + 1])
-                nc.sync.dma_start(out=out[c * P : (c + 1) * P, h * W : (h + 1) * W], in_=result[:, c, :])
+                nc.tensor.matmul_mx(
+                    out=banks[side + c][:, cols],
+                    lhsT=woq[b][0][:, c * P : (c + 1) * P].bitcast(FP8X4),
+                    lhsT_scale=woq[b][1][:, c * P : (c + 1) * P],
+                    rhs=hq[b, h][0][:, cols].bitcast(FP8X4),
+                    rhs_scale=hq[b, h][1][:, cols],
+                    start=(b == 0),
+                    stop=(b == BLOCKS - 1),
+                )
 
+        def logits_out(h, side, on_vector, cols=slice(0, W)):
+            for c in range(OUT_TILES):
+                tag = "result%d%d" % (c, side)
+                result = keep.tile([P, W], F32, name=tag, tag=tag)
+                bo_col = bias[:, BO_COL + c : BO_COL + c + 1]
+                if c in on_vector:
+                    nc.vector.tensor_scalar(out=result[:, cols], in0=banks[side + c][:, cols], scalar1=bo_col, scalar2=None, op0=ADD)
+                else:
+                    nc.scalar.activation(out=result[:, cols], in_=banks[side + c][:, cols], func=IDENTITY, bias=bo_col)
+                nc.sync.dma_start(
+                    out=out[c * P : (c + 1) * P, h * W + cols.start : h * W + cols.stop], in_=result[:, cols]
+                )
+
+        def b_pass(b, h, a):
+            for t in range(PACK):
+                nc.tensor.matmul_mx(
+                    out=banks[B_SIDE + t][:],
+                    lhsT=wbq[a, b][0][:, t * P : (t + 1) * P].bitcast(FP8X4),
+                    lhsT_scale=wbq[a, b][1][:, t * P : (t + 1) * P],
+                    rhs=xq[a, h][0][:].bitcast(FP8X4),
+                    rhs_scale=xq[a, h][1][:],
+                    start=(a == 0),
+                    stop=(a == PASSES - 1),
+                )
+
+        left, right = slice(0, W // 2), slice(W // 2, W)
         for i in range(PACK):
             for h in range(HALVES):
                 gather(0, i, h)
         quantize_x(0, 0)
-        gather(1, 0, 0)
-        permute_wa()
-        a_pass(0, 0, 0, 0)
-        a_pass(1, 0, 0, 4)
         quantize_x(0, 1)
-        gather(1, 0, 1)
-        for i in range(1, PACK):
+        quantize_wb(0, 0, "scalar")
+        quantize_wb(1, 0, "scalar")
+        for i in range(PACK - 1):
             for h in range(HALVES):
                 gather(1, i, h)
-        quantize_x(1, 0)
+        permute_wa()
+        gather(1, PACK - 1, 0)
+        a_pass(0, 0, 0, 0)
+        b_pass(0, 0, 0)
+        quantize_x(1, 0, 512)
+        gather(1, PACK - 1, 1)
         a_pass(0, 0, 1, 0)
-        a_pass(1, 0, 1, 4)
-        quantize_wb(0, 0, "vector")
-        quantize_x(1, 1)
-        a_out(0, 0, 0, "quad00")
-        quantize_wb(1, 0, "vector")
-        b_product(0, 0, 0)
-        a_out(1, 0, 4, "quad01")
-        for a in range(PASSES):
-            a_pass(0, 1, a, 4)
-        h_on_vector(0, 0, 0)
-        a_out(0, 1, 4, "quad10")
+        b_pass(0, 0, 1)
         quantize_wb(0, 1, "vector")
-        b_product(0, 1, 0)
-        for a in range(PASSES):
-            a_pass(1, 1, a, 4)
+        quantize_x(1, 1, 512)
         quantize_wb(1, 1, "vector")
-        h_on_vector(0, 1, 0)
-        a_out(1, 1, 4, "quad11")
+        a_out(0, 0, 0, "quad00")
+        h_product(0, 0, 4)
+        for a in range(PASSES):
+            a_pass(1, 0, a, 0)
+        b_product(1, 0, 4)
+        a_out(1, 0, 0, "quad01")
+        quantize_h(0, 0, "vector")
+        h_product(1, 0, 4)
+        for a in range(PASSES):
+            a_pass(0, 1, a, 0)
+        b_product(0, 1, 4)
+        a_out(0, 1, 0, "quad10")
         quantize_wo(0, "scalar")
-        b_product(1, 0, 0)
-        h_shared(1, 0, 0)
-        quantize_wo(1, "scalar")
+        quantize_h(1, 0, "vector")
+        h_product(0, 1, 4)
+        for a in range(PASSES):
+            a_pass(1, 1, a, 0)
         b_product(1, 1, 4)
-        h_shared(1, 1, 4)
-        logits(0, 0)
-        logits(1, 4)
+        a_out(1, 1, 0, "quad11")
+        quantize_wo(1, "scalar")
+        logit_pass(0, 0, 0)
+        logit_pass(1, 0, 0)
+        quantize_h(0, 1, "scalar")
+        h_product(1, 1, 4, left)
+        logits_out(0, 0, ())
+        quantize_h(1, 1, "vector", left)
+        h_product(1, 1, 4, right)
+        logit_pass(0, 1, 0, left)
+        logit_pass(1, 1, 0, left)
+        quantize_h(1, 1, "vector", right)
+        logit_pass(0, 1, 4, right)
+        logits_out(1, 0, (), left)
+        logit_pass(1, 1, 4, right)
+        logits_out(1, 4, (1, 3), right)

@@ -25,8 +25,7 @@ PASSES = K // W
 BLOCKS = H // W
 HALVES = S // W
 OUT_TILES = N // P
-BA_COL, BB_COL, BO_COL = 0, 4, 8
-BIAS_COLS = 12
+BA, BB = 0, 1
 B_SIDE = 4
 PICK_TAG = {(0, 0): "quad00", (0, 1): "quad01", (1, 0): "quad10", (1, 1): "quad11"}
 
@@ -55,10 +54,10 @@ def tile_list_hashed_click_logits_kernel(tc, xT, wgt, offs, wa_words, wa_scales,
                 nc.scalar.copy(out=dst, in_=src)
 
         def slots_walk(quad):
-            return quad.rearrange("p t (c e) -> p c t e", e=PACK)
+            return quad.rearrange("p t (c e) -> p c t e", e=2)
 
         def words_walk(words):
-            return words.rearrange("p (c e t) -> p c t e", e=PACK, t=PACK)
+            return words.rearrange("p (c e t) -> p c t e", e=2, t=PACK)
 
         def quantize(operand, words):
             codes, scales = operand
@@ -68,14 +67,18 @@ def tile_list_hashed_click_logits_kernel(tc, xT, wgt, offs, wa_words, wa_scales,
 
         offsets = keep.tile([P, S // 16], U16, name="offsets")
         weights = [keep.tile([P, W], F32, name="wgt%d" % h, tag="wgt%d" % h) for h in range(HALVES)]
-        planes = [keep.tile([P, T], F32, name="plane%d" % n) for n in range(PASSES * PACK)]
+        planes = [keep.tile([P, T], F32, name="plane%d" % n, tag="plane%d" % n) for n in range(PASSES * PACK)]
         wa_raw = keep.tile([P, PASSES * 2 * H], U8, name="wa_raw")
         wa_scale_raw = keep.tile([P, PASSES * H], U8, name="wa_scale_raw")
         wa_codes = keep.tile([P, PASSES * 2 * H], U8, name="wa_codes", align_bytes=64)
         wa_scale = keep.tile([P, PASSES * H], U8, name="wa_scale", align_bytes=64)
-        bias_rows = keep.tile([P, BLOCKS * P], F32, name="bias_rows")
+        bias_rows = keep.tile([2, H], F32, name="bias_rows")
+        bo_raw = keep.tile([OUT_TILES, P], F32, name="bo_raw")
+        bias_tiles = keep.tile([P, H], F32, name="bias_tiles")
+        bo_rows = keep.tile([P, P], F32, name="bo_rows")
+        bo_cols = keep.tile([P, OUT_TILES], F32, name="bo_cols")
         identity = keep.tile([P, P], F32, name="identity")
-        bias = keep.tile([P, BLOCKS * BIAS_COLS], F32, name="bias")
+        bias = keep.tile([P, BLOCKS * PACK, 2], F32, name="bias")
 
         def load_plane(a, i):
             rows = xT[a * W : (a + 1) * W, :].rearrange("(p i) t -> i p t", i=PACK)
@@ -88,10 +91,7 @@ def tile_list_hashed_click_logits_kernel(tc, xT, wgt, offs, wa_words, wa_scales,
             )
 
         def load_bias(vec, row):
-            nc.sync.dma_start(
-                out=bias_rows[row : row + PACK, :].rearrange("t (g i) -> t g i", i=PACK),
-                in_=vec.rearrange("(g t i) -> t g i", t=PACK, i=PACK),
-            )
+            nc.sync.dma_start(out=bias_rows[row : row + 1, :], in_=vec.rearrange("(o r) -> o r", o=1))
 
         wb_raw, wo_raw = {}, {}
 
@@ -108,19 +108,20 @@ def tile_list_hashed_click_logits_kernel(tc, xT, wgt, offs, wa_words, wa_scales,
             for i in range(PACK):
                 nc.sync.dma_start(out=wo_raw[b][i:P:PACK, :, :], in_=rows[i])
 
-        nc.gpsimd.memset(bias_rows[:], 0.0)
+        nc.vector.memset(bias_tiles[:], 0.0)
+        nc.vector.memset(bo_rows[:], 0.0)
         nc.gpsimd.memset(wa_scale_raw[:].bitcast(I32), 0)
         make_identity(nc, identity[:])
         nc.sync.dma_start(offsets[:], offs)
+        load_bias(ba, BA)
+        load_bias(bb, BB)
+        nc.sync.dma_start(out=bo_raw[:], in_=bo.rearrange("(c p) -> c p", p=P))
         load_plane(0, 0)
         nc.sync.dma_start(out=weights[0][:], in_=wgt[:, 0:W])
         nc.sync.dma_start(out=weights[1][:], in_=wgt[:, W : 2 * W])
         load_plane(0, 1)
-        load_bias(ba, BA_COL)
         load_plane(0, 2)
-        load_bias(bb, BB_COL)
         load_plane(0, 3)
-        nc.sync.dma_start(out=bias_rows[BO_COL : BO_COL + OUT_TILES, 0:P], in_=bo.rearrange("(c p) -> c p", p=P))
         load_plane(1, 0)
         load_wa_scales(0)
         load_wb(0, 0)
@@ -130,23 +131,32 @@ def tile_list_hashed_click_logits_kernel(tc, xT, wgt, offs, wa_words, wa_scales,
         load_wb(1, 0)
         load_wa_scales(3)
         load_plane(1, 2)
+        load_plane(1, 3)
         nc.sync.dma_start(
             out=wa_raw[:].bitcast(I32).rearrange("p (a n) -> p a n", a=PASSES),
             in_=wa_words.bitcast(I32).rearrange("a p n -> p a n"),
         )
-        load_plane(1, 3)
         load_wb(0, 1)
         load_wb(1, 1)
         for b in range(BLOCKS):
             load_wo(b)
 
-        for b in range(BLOCKS):
-            nc.tensor.transpose(banks[7][:, b * P : (b + 1) * P], bias_rows[:, b * P : (b + 1) * P], identity[:])
-        nc.scalar.activation(
-            out=bias[:].rearrange("p (b c) -> p b c", b=BLOCKS),
-            in_=banks[7][:, 0 : BLOCKS * P].rearrange("p (b c) -> p b c", b=BLOCKS)[:, :, 0:BIAS_COLS],
-            func=IDENTITY,
+        nc.scalar.copy(
+            out=bias_tiles[0:2, :].rearrange("p (b t g i) -> p b t g i", t=PACK, g=32, i=PACK),
+            in_=bias_rows[:].rearrange("p (b g t i) -> p b t g i", t=PACK, g=32, i=PACK),
         )
+        for b in range(BLOCKS):
+            for t in range(PACK):
+                tile_cols = slice((PACK * b + t) * P, (PACK * b + t + 1) * P)
+                nc.tensor.transpose(banks[b][:, t * P : (t + 1) * P], bias_tiles[:, tile_cols], identity[:])
+            nc.scalar.activation(
+                out=bias[:, PACK * b : PACK * (b + 1), :],
+                in_=banks[b][:].rearrange("p (t c) -> p t c", t=PACK)[:, :, 0:2],
+                func=IDENTITY,
+            )
+        nc.scalar.copy(out=bo_rows[0:OUT_TILES, :], in_=bo_raw[:])
+        nc.tensor.transpose(banks[2][:, 0:P], bo_rows[:], identity[:])
+        nc.scalar.activation(out=bo_cols[:], in_=banks[2][:, 0:OUT_TILES], func=IDENTITY)
 
         picked, xq, wbq, woq, hq, a_sb = {}, {}, {}, {}, {}, {}
 
@@ -176,11 +186,10 @@ def tile_list_hashed_click_logits_kernel(tc, xT, wgt, offs, wa_words, wa_scales,
 
         def quantize_wb(a, b, engine):
             words = bf16_words("wwords%d" % a)
-            copy_on(
-                engine,
-                words[:].rearrange("p (t g i j) -> p t g j i", t=PACK, i=PACK, j=PACK),
-                wb_raw[a, b][:].rearrange("p j (g t i) -> p t g j i", t=PACK, i=PACK),
-            )
+            dst = words[:].rearrange("p (t g u e j) -> p u t g j e", t=PACK, u=2, e=2, j=PACK)
+            src = wb_raw[a, b][:].rearrange("p j (g t u e) -> p u t g j e", t=PACK, u=2, e=2)
+            for u in range(2):
+                copy_on(engine, dst[:, u], src[:, u])
             wbq[a, b] = mx_operand("wbq%d%d" % (a, b))
             quantize(wbq[a, b], words)
 
@@ -206,8 +215,7 @@ def tile_list_hashed_click_logits_kernel(tc, xT, wgt, offs, wa_words, wa_scales,
         def a_out(b, h, side, tag):
             a_sb[b, h] = f32_quad(tag)
             for t in range(PACK):
-                col = BIAS_COLS * b + BA_COL + t
-                nc.scalar.activation(out=a_sb[b, h][:, t, :], in_=banks[side + t][:], func=IDENTITY, bias=bias[:, col : col + 1])
+                nc.scalar.activation(out=a_sb[b, h][:, t, :], in_=banks[side + t][:], func=IDENTITY, bias=bias[:, PACK * b + t, BA : BA + 1])
 
         def mx_group(bank, stationary, cols, moving):
             for n in range(len(moving)):
@@ -229,13 +237,12 @@ def tile_list_hashed_click_logits_kernel(tc, xT, wgt, offs, wa_words, wa_scales,
 
         def h_product(b, h, side, cols=slice(0, W)):
             if cols.start == 0:
-                h_slots[b, h] = keep.tile([P, PACK, W], BF16, name="h_slots%d" % b, tag="h_slots%d" % b)
+                h_slots[b, h] = f32_quad("plane%d" % b)
             for t in range(PACK):
-                col = BIAS_COLS * b + BB_COL + t
                 nc.vector.scalar_tensor_tensor(
                     out=h_slots[b, h][:, t, cols],
                     in0=banks[side + t][:, cols],
-                    scalar=bias[:, col : col + 1],
+                    scalar=bias[:, PACK * b + t, BB : BB + 1],
                     in1=a_sb[b, h][:, t, cols],
                     op0=ADD,
                     op1=MULT,
@@ -265,7 +272,7 @@ def tile_list_hashed_click_logits_kernel(tc, xT, wgt, offs, wa_words, wa_scales,
             for c in range(OUT_TILES):
                 tag = "result%d%d" % (c, side)
                 result = keep.tile([P, W], F32, name=tag, tag=tag)
-                bo_col = bias[:, BO_COL + c : BO_COL + c + 1]
+                bo_col = bo_cols[:, c : c + 1]
                 if c in on_vector:
                     nc.vector.tensor_scalar(out=result[:, cols], in0=banks[side + c][:, cols], scalar1=bo_col, scalar2=None, op0=ADD)
                 else:
@@ -301,7 +308,7 @@ def tile_list_hashed_click_logits_kernel(tc, xT, wgt, offs, wa_words, wa_scales,
         gather(1, PACK - 1, 0)
         a_pass(0, 0, 0, 0)
         b_pass(0, 0, 0)
-        quantize_x(1, 0, 512)
+        quantize_x(1, 0, 384)
         gather(1, PACK - 1, 1)
         a_pass(0, 0, 1, 0)
         b_pass(0, 0, 1)

@@ -104,33 +104,31 @@ def tile_list_hashed_click_logits_kernel(tc, xT, wgt, offs, wa_words, wa_scales,
 
         def load_wo(b):
             wo_raw[b] = f32_quad("wo_raw%d" % b)
-            rows = wo[b * W : (b + 1) * W, :].rearrange("(g t i) n -> i g t n", t=PACK, i=PACK)
-            for i in range(PACK):
-                nc.sync.dma_start(out=wo_raw[b][i:P:PACK, :, :], in_=rows[i])
+            rows = wo[b * W : (b + 1) * W, :].rearrange("(g t i) n -> i g t n", t=PACK, i=2)
+            for i in range(2):
+                nc.sync.dma_start(out=wo_raw[b][i:P:2, :, :], in_=rows[i])
 
+        nc.vector.memset(wa_scale_raw[:].bitcast(I32), 0)
         nc.vector.memset(bias_tiles[:], 0.0)
         nc.vector.memset(bo_rows[:], 0.0)
-        nc.gpsimd.memset(wa_scale_raw[:].bitcast(I32), 0)
         make_identity(nc, identity[:])
         nc.sync.dma_start(offsets[:], offs)
-        load_bias(ba, BA)
-        load_bias(bb, BB)
-        nc.sync.dma_start(out=bo_raw[:], in_=bo.rearrange("(c p) -> c p", p=P))
         load_plane(0, 0)
         nc.sync.dma_start(out=weights[0][:], in_=wgt[:, 0:W])
         nc.sync.dma_start(out=weights[1][:], in_=wgt[:, W : 2 * W])
         load_plane(0, 1)
+        load_bias(ba, BA)
+        load_bias(bb, BB)
+        nc.sync.dma_start(out=bo_raw[:], in_=bo.rearrange("(c p) -> c p", p=P))
         load_plane(0, 2)
         load_plane(0, 3)
+        for q in range(4):
+            load_wa_scales(q)
         load_plane(1, 0)
-        load_wa_scales(0)
-        load_wb(0, 0)
-        load_wa_scales(1)
         load_plane(1, 1)
-        load_wa_scales(2)
-        load_wb(1, 0)
-        load_wa_scales(3)
+        load_wb(0, 0)
         load_plane(1, 2)
+        load_wb(1, 0)
         load_plane(1, 3)
         nc.sync.dma_start(
             out=wa_raw[:].bitcast(I32).rearrange("p (a n) -> p a n", a=PASSES),
@@ -142,8 +140,8 @@ def tile_list_hashed_click_logits_kernel(tc, xT, wgt, offs, wa_words, wa_scales,
             load_wo(b)
 
         nc.scalar.copy(
-            out=bias_tiles[0:2, :].rearrange("p (b t g i) -> p b t g i", t=PACK, g=32, i=PACK),
-            in_=bias_rows[:].rearrange("p (b g t i) -> p b t g i", t=PACK, g=32, i=PACK),
+            out=bias_tiles[0:2, :].rearrange("p (b t g i) -> p b t g i", t=PACK, g=64, i=2),
+            in_=bias_rows[:].rearrange("p (b g t i) -> p b t g i", t=PACK, g=64, i=2),
         )
         for b in range(BLOCKS):
             for t in range(PACK):
@@ -174,22 +172,25 @@ def tile_list_hashed_click_logits_kernel(tc, xT, wgt, offs, wa_words, wa_scales,
             xq[a, h] = mx_operand("xq%d%d" % (a, h))
             quantize(xq[a, h], words)
 
-        def permute_wa():
+        def permute_wa_codes():
             nc.vector.tensor_copy(
-                out=wa_codes[:].bitcast(I32).rearrange("p (c t g u) -> p c t g u", t=PACK, g=32, u=2),
-                in_=wa_raw[:].bitcast(I32).rearrange("p (c g t u) -> p c t g u", t=PACK, g=32, u=2),
+                out=wa_codes[:].bitcast(I32).rearrange("p (c t g e) -> p c g t e", t=PACK, g=16, e=4),
+                in_=wa_raw[:].bitcast(I32).rearrange("p (c g e t) -> p c g t e", t=PACK, g=16, e=4),
             )
+
+        def permute_wa_scales():
             nc.vector.tensor_copy(
-                out=wa_scale[:].bitcast(I32).rearrange("p (c t g) -> p c t g", t=PACK, g=32),
-                in_=wa_scale_raw[:].bitcast(I32).rearrange("p (c g t) -> p c t g", t=PACK, g=32),
+                out=wa_scale[:].bitcast(U16).rearrange("p (c t g e) -> p c g t e", t=PACK, g=8, e=8),
+                in_=wa_scale_raw[:].bitcast(U16).rearrange("p (c g e t) -> p c g t e", t=PACK, g=8, e=8),
             )
 
         def quantize_wb(a, b, engine):
             words = bf16_words("wwords%d" % a)
-            dst = words[:].rearrange("p (t g u e j) -> p u t g j e", t=PACK, u=2, e=2, j=PACK)
-            src = wb_raw[a, b][:].rearrange("p j (g t u e) -> p u t g j e", t=PACK, u=2, e=2)
-            for u in range(2):
-                copy_on(engine, dst[:, u], src[:, u])
+            copy_on(
+                engine,
+                words[:].rearrange("p (t g i j) -> p t g j i", t=PACK, i=2, j=PACK),
+                wb_raw[a, b][:].rearrange("p j (g t i) -> p t g j i", t=PACK, i=2),
+            )
             wbq[a, b] = mx_operand("wbq%d%d" % (a, b))
             quantize(wbq[a, b], words)
 
@@ -304,7 +305,8 @@ def tile_list_hashed_click_logits_kernel(tc, xT, wgt, offs, wa_words, wa_scales,
         for i in range(PACK - 1):
             for h in range(HALVES):
                 gather(1, i, h)
-        permute_wa()
+        permute_wa_scales()
+        permute_wa_codes()
         gather(1, PACK - 1, 0)
         a_pass(0, 0, 0, 0)
         b_pass(0, 0, 0)
@@ -321,23 +323,23 @@ def tile_list_hashed_click_logits_kernel(tc, xT, wgt, offs, wa_words, wa_scales,
             a_pass(1, 0, a, 0)
         b_product(1, 0, 4)
         a_out(1, 0, 0, "quad01")
+        quantize_wo(0, "scalar")
         quantize_h(0, 0, "vector")
         h_product(1, 0, 4)
         for a in range(PASSES):
             a_pass(0, 1, a, 0)
         b_product(0, 1, 4)
         a_out(0, 1, 0, "quad10")
-        quantize_wo(0, "scalar")
-        quantize_h(1, 0, "vector")
+        quantize_wo(1, "scalar")
+        quantize_h(1, 0, "scalar")
         h_product(0, 1, 4)
         for a in range(PASSES):
             a_pass(1, 1, a, 0)
         b_product(1, 1, 4)
         a_out(1, 1, 0, "quad11")
-        quantize_wo(1, "scalar")
         logit_pass(0, 0, 0)
         logit_pass(1, 0, 0)
-        quantize_h(0, 1, "scalar")
+        quantize_h(0, 1, "vector")
         h_product(1, 1, 4, left)
         logits_out(0, 0, ())
         quantize_h(1, 1, "vector", left)

@@ -54,10 +54,10 @@ def tile_list_hashed_click_logits_kernel(tc, xT, wgt, offs, wa_words, wa_scales,
                 nc.scalar.copy(out=dst, in_=src)
 
         def slots_walk(quad):
-            return quad.rearrange("p t (c e) -> p c t e", e=2)
+            return quad.rearrange("p t (c e) -> p c t e", e=PACK)
 
         def words_walk(words):
-            return words.rearrange("p (c e t) -> p c t e", e=2, t=PACK)
+            return words.rearrange("p (c e t) -> p c t e", e=PACK, t=PACK)
 
         def quantize(operand, words):
             codes, scales = operand

@@ -25,9 +25,8 @@ PASSES = K // W
 BLOCKS = H // W
 HALVES = S // W
 OUT_TILES = N // P
-BA, BB = 0, 1
-B_SIDE = 4
-PICK_TAG = {(0, 0): "quad00", (0, 1): "quad01", (1, 0): "quad10", (1, 1): "quad11"}
+BA, BB, BO = 0, 2, 4
+WGT0_AT = 2 * W
 
 
 def tile_list_hashed_click_logits_kernel(tc, xT, wgt, offs, wa_words, wa_scales, ba, wb, bb, wo, bo, out):
@@ -37,7 +36,10 @@ def tile_list_hashed_click_logits_kernel(tc, xT, wgt, offs, wa_words, wa_scales,
         psum = ctx.enter_context(tc.psum_pool(name="psum", bufs=1))
 
         def f32_quad(tag):
-            return keep.tile([P, PACK, W], F32, name=tag, tag=tag)
+            return keep.tile([P, PACK * W], F32, name=tag, tag=tag)
+
+        def slots(quad):
+            return quad[:, :].rearrange("p (t c) -> p t c", t=PACK)
 
         def bf16_words(tag):
             return keep.tile([P, PACK * W], BF16, name=tag, tag=tag, align_bytes=64)
@@ -53,52 +55,46 @@ def tile_list_hashed_click_logits_kernel(tc, xT, wgt, offs, wa_words, wa_scales,
             else:
                 nc.scalar.copy(out=dst, in_=src)
 
-        def slots_walk(quad):
-            return quad.rearrange("p t (c e) -> p c t e", e=PACK)
+        def slots_walk(quad, cols=slice(0, W)):
+            return slots(quad)[:, :, cols].rearrange("p t (c e) -> p c t e", e=PACK)
 
-        def words_walk(words):
-            return words.rearrange("p (c e t) -> p c t e", e=PACK, t=PACK)
+        def words_walk(words, cols=slice(0, W)):
+            return words[:, cols.start * PACK : cols.stop * PACK].rearrange("p (c e t) -> p c t e", e=PACK, t=PACK)
 
-        def quantize(operand, words):
+        def quantize(operand, words, cols=slice(0, W)):
             codes, scales = operand
-            nc.vector.quantize_mx(out=codes[:].bitcast(FP8X4), scales=scales[:], in_=words[:])
+            nc.vector.quantize_mx(
+                out=codes[:, cols].bitcast(FP8X4), scales=scales[:, cols], in_=words[:, cols.start * PACK : cols.stop * PACK]
+            )
 
         banks = [psum.tile([P, W], F32, name="bank%d" % n) for n in range(8)]
 
         offsets = keep.tile([P, S // 16], U16, name="offsets")
-        weights = [keep.tile([P, W], F32, name="wgt%d" % h, tag="wgt%d" % h) for h in range(HALVES)]
-        planes = [keep.tile([P, T], F32, name="plane%d" % n, tag="plane%d" % n) for n in range(PASSES * PACK)]
+        planes = [f32_quad("plane%d" % n) for n in range(PASSES * PACK)]
+        picked = {(a, h): f32_quad("picked%d%d" % (a, h)) for a, h in ((0, 0), (0, 1), (1, 0))}
+        late = keep.tile([P, (PACK + 1) * W], F32, name="late", align_bytes=64)
+        picked[1, 1] = late[:, 0 : PACK * W]
+        wgt1 = keep.tile([P, W], F32, name="wgt1")
+        weights = [late[:, WGT0_AT : WGT0_AT + W], wgt1[:]]
         wa_raw = keep.tile([P, PASSES * 2 * H], U8, name="wa_raw")
         wa_scale_raw = keep.tile([P, PASSES * H], U8, name="wa_scale_raw")
         wa_codes = keep.tile([P, PASSES * 2 * H], U8, name="wa_codes", align_bytes=64)
         wa_scale = keep.tile([P, PASSES * H], U8, name="wa_scale", align_bytes=64)
-        bias_rows = keep.tile([2, H], F32, name="bias_rows")
-        bo_raw = keep.tile([OUT_TILES, P], F32, name="bo_raw")
-        bias_tiles = keep.tile([P, H], F32, name="bias_tiles")
-        bo_rows = keep.tile([P, P], F32, name="bo_rows")
-        bo_cols = keep.tile([P, OUT_TILES], F32, name="bo_cols")
+        bias_raw = keep.tile([4, W], F32, name="bias_raw")
+        bias_rows = keep.tile([P, W], F32, name="bias_rows")
         identity = keep.tile([P, P], F32, name="identity")
-        bias = keep.tile([P, BLOCKS * PACK, 2], F32, name="bias")
+        bias = keep.tile([P, PACK, 8], F32, name="bias")
 
         def load_plane(a, i):
             rows = xT[a * W : (a + 1) * W, :].rearrange("(p i) t -> i p t", i=PACK)
             nc.sync.dma_start(out=planes[a * PACK + i][:], in_=rows[i])
-
-        def load_wa_scales(q):
-            nc.sync.dma_start(
-                out=wa_scale_raw[32 * q : 32 * q + 4, :].bitcast(I32).rearrange("p (a n) -> p a n", a=PASSES),
-                in_=wa_scales.bitcast(I32)[:, 4 * q : 4 * q + 4, :].rearrange("a r n -> r a n"),
-            )
-
-        def load_bias(vec, row):
-            nc.sync.dma_start(out=bias_rows[row : row + 1, :], in_=vec.rearrange("(o r) -> o r", o=1))
 
         wb_raw, wo_raw = {}, {}
 
         def load_wb(a, b):
             wb_raw[a, b] = f32_quad("wb_raw%d%d" % (a, b))
             nc.sync.dma_start(
-                out=wb_raw[a, b][:],
+                out=slots(wb_raw[a, b]),
                 in_=wb[a * W : (a + 1) * W, b * W : (b + 1) * W].rearrange("(p j) r -> p j r", j=PACK),
             )
 
@@ -106,71 +102,63 @@ def tile_list_hashed_click_logits_kernel(tc, xT, wgt, offs, wa_words, wa_scales,
             wo_raw[b] = f32_quad("wo_raw%d" % b)
             rows = wo[b * W : (b + 1) * W, :].rearrange("(g t i) n -> i g t n", t=PACK, i=2)
             for i in range(2):
-                nc.sync.dma_start(out=wo_raw[b][i:P:2, :, :], in_=rows[i])
+                nc.sync.dma_start(out=slots(wo_raw[b])[i:P:2, :, :], in_=rows[i])
 
         nc.vector.memset(wa_scale_raw[:].bitcast(I32), 0)
-        nc.vector.memset(bias_tiles[:], 0.0)
-        nc.vector.memset(bo_rows[:], 0.0)
+        nc.vector.memset(bias_rows[:], 0.0)
         make_identity(nc, identity[:])
         nc.sync.dma_start(offsets[:], offs)
+        nc.sync.dma_start(out=weights[0], in_=wgt[:, 0:W])
         load_plane(0, 0)
-        nc.sync.dma_start(out=weights[0][:], in_=wgt[:, 0:W])
-        nc.sync.dma_start(out=weights[1][:], in_=wgt[:, W : 2 * W])
-        load_plane(0, 1)
-        load_bias(ba, BA)
-        load_bias(bb, BB)
-        nc.sync.dma_start(out=bo_raw[:], in_=bo.rearrange("(c p) -> c p", p=P))
-        load_plane(0, 2)
-        load_plane(0, 3)
+        nc.sync.dma_start(out=weights[1], in_=wgt[:, W : 2 * W])
+        nc.scalar.dma_start(out=bias_raw[BA : BA + BLOCKS, :], in_=ba.rearrange("(b r) -> b r", b=BLOCKS))
+        nc.scalar.dma_start(out=bias_raw[BB : BB + BLOCKS, :], in_=bb.rearrange("(b r) -> b r", b=BLOCKS))
+        nc.scalar.dma_start(out=bias_rows[BO : BO + OUT_TILES, 0:P], in_=bo.rearrange("(c p) -> c p", p=P))
         for q in range(4):
-            load_wa_scales(q)
-        load_plane(1, 0)
-        load_plane(1, 1)
-        load_wb(0, 0)
-        load_plane(1, 2)
-        load_wb(1, 0)
-        load_plane(1, 3)
+            nc.scalar.dma_start(
+                out=wa_scale_raw[32 * q : 32 * q + 4, :].bitcast(I32).rearrange("p (a n) -> p a n", a=PASSES),
+                in_=wa_scales.bitcast(I32)[:, 4 * q : 4 * q + 4, :].rearrange("a r n -> r a n"),
+            )
+        for i in range(1, PACK):
+            load_plane(0, i)
         nc.sync.dma_start(
             out=wa_raw[:].bitcast(I32).rearrange("p (a n) -> p a n", a=PASSES),
             in_=wa_words.bitcast(I32).rearrange("a p n -> p a n"),
         )
-        load_wb(0, 1)
-        load_wb(1, 1)
+        for i in range(PACK):
+            load_plane(1, i)
+        for b in range(BLOCKS):
+            for a in range(PASSES):
+                load_wb(a, b)
         for b in range(BLOCKS):
             load_wo(b)
 
         nc.scalar.copy(
-            out=bias_tiles[0:2, :].rearrange("p (b t g i) -> p b t g i", t=PACK, g=64, i=2),
-            in_=bias_rows[:].rearrange("p (b g t i) -> p b t g i", t=PACK, g=64, i=2),
+            out=bias_rows[0:4, :].rearrange("p (t g i) -> p t g i", t=PACK, i=2),
+            in_=bias_raw[:].rearrange("p (g t i) -> p t g i", t=PACK, i=2),
         )
-        for b in range(BLOCKS):
-            for t in range(PACK):
-                tile_cols = slice((PACK * b + t) * P, (PACK * b + t + 1) * P)
-                nc.tensor.transpose(banks[b][:, t * P : (t + 1) * P], bias_tiles[:, tile_cols], identity[:])
-            nc.scalar.activation(
-                out=bias[:, PACK * b : PACK * (b + 1), :],
-                in_=banks[b][:].rearrange("p (t c) -> p t c", t=PACK)[:, :, 0:2],
-                func=IDENTITY,
-            )
-        nc.scalar.copy(out=bo_rows[0:OUT_TILES, :], in_=bo_raw[:])
-        nc.tensor.transpose(banks[2][:, 0:P], bo_rows[:], identity[:])
-        nc.scalar.activation(out=bo_cols[:], in_=banks[2][:, 0:OUT_TILES], func=IDENTITY)
+        for t in range(PACK):
+            nc.tensor.transpose(banks[0][:, t * P : (t + 1) * P], bias_rows[:, t * P : (t + 1) * P], identity[:])
+        nc.scalar.activation(out=bias[:], in_=banks[0][:].rearrange("p (t c) -> p t c", t=PACK)[:, :, 0:8], func=IDENTITY)
 
-        picked, xq, wbq, woq, hq, a_sb = {}, {}, {}, {}, {}, {}
+        xq, wbq, woq, hq, words, views = {}, {}, {}, {}, {}, {}
 
         def gather(a, i, h):
-            if i == 0:
-                picked[a, h] = f32_quad(PICK_TAG[a, h])
             window = planes[a * PACK + i][:].indirect(offsets[:, h * (W // 16) : (h + 1) * (W // 16)])
-            nc.vector.tensor_tensor(picked[a, h][:, i, :], window, weights[h][:], MULT)
+            nc.vector.tensor_tensor(picked[a, h][:, i * W : (i + 1) * W], window, weights[h], MULT)
 
-        def quantize_x(a, h, on_scalar=W):
-            words = bf16_words("words%d" % h)
-            copy_on("scalar", words_walk(words[:, 0 : on_scalar * PACK]), slots_walk(picked[a, h][:, :, 0:on_scalar]))
-            if on_scalar < W:
-                copy_on("vector", words_walk(words[:, on_scalar * PACK :]), slots_walk(picked[a, h][:, :, on_scalar:]))
+        def round_x(a, h, on_scalar):
+            if (a, h) == (1, 0):
+                words["x", a, h] = late[:, (PACK - 1) * W : (PACK + 1) * W].bitcast(BF16)
+            else:
+                words["x", a, h] = bf16_words("words%d" % h)
+            for engine, cols in (("scalar", slice(0, on_scalar)), ("vector", slice(on_scalar, W))):
+                if cols.stop > cols.start:
+                    copy_on(engine, words_walk(words["x", a, h], cols), slots_walk(picked[a, h], cols))
+
+        def quantize_x(a, h):
             xq[a, h] = mx_operand("xq%d%d" % (a, h))
-            quantize(xq[a, h], words)
+            quantize(xq[a, h], words["x", a, h])
 
         def permute_wa_codes():
             nc.vector.tensor_copy(
@@ -184,170 +172,177 @@ def tile_list_hashed_click_logits_kernel(tc, xT, wgt, offs, wa_words, wa_scales,
                 in_=wa_scale_raw[:].bitcast(U16).rearrange("p (c g e t) -> p c g t e", t=PACK, g=8, e=8),
             )
 
-        def quantize_wb(a, b, engine):
-            words = bf16_words("wwords%d" % a)
-            copy_on(
-                engine,
-                words[:].rearrange("p (t g i j) -> p t g j i", t=PACK, i=2, j=PACK),
-                wb_raw[a, b][:].rearrange("p j (g t i) -> p t g j i", t=PACK, i=2),
-            )
+        def round_wb(a, b, on_scalar, tag):
+            words["wb", a, b] = bf16_words(tag)
+            dst = words["wb", a, b][:].rearrange("p (t g i j) -> p t g j i", t=PACK, i=2, j=PACK)
+            src = wb_raw[a, b][:].rearrange("p (j g t i) -> p t g j i", j=PACK, t=PACK, i=2)
+            for engine, tiles in (("scalar", slice(0, on_scalar)), ("vector", slice(on_scalar, PACK))):
+                if tiles.stop > tiles.start:
+                    copy_on(engine, dst[:, tiles], src[:, tiles])
+
+        def quantize_wb(a, b):
             wbq[a, b] = mx_operand("wbq%d%d" % (a, b))
-            quantize(wbq[a, b], words)
+            quantize(wbq[a, b], words["wb", a, b])
 
-        def quantize_wo(b, engine):
-            words = bf16_words("wwords%d" % b)
-            copy_on(engine, words_walk(words[:]), slots_walk(wo_raw[b][:]))
+        def round_wo(b, engine, tag):
+            words["wo", b] = bf16_words(tag)
+            copy_on(engine, words_walk(words["wo", b]), slots_walk(wo_raw[b]))
+
+        def quantize_wo(b):
             woq[b] = mx_operand("woq%d" % b)
-            quantize(woq[b], words)
+            quantize(woq[b], words["wo", b])
 
-        def a_pass(b, h, a, side):
-            for t in range(PACK):
+        def view_pass(kind, b, h, t, a, acc, cols):
+            if kind == BA:
                 col = a * H + b * W + t * P
-                nc.tensor.matmul_mx(
-                    out=banks[side + t][:],
-                    lhsT=wa_codes[:, 2 * col : 2 * (col + P)].bitcast(FP4X4),
-                    lhsT_scale=wa_scale[:, col : col + P],
-                    rhs=xq[a, h][0][:].bitcast(FP8X4),
-                    rhs_scale=xq[a, h][1][:],
-                    start=(a == 0),
-                    stop=(a == PASSES - 1),
-                )
+                codes, scales = wa_codes[:, 2 * col : 2 * (col + P)].bitcast(FP4X4), wa_scale[:, col : col + P]
+            else:
+                codes, scales = wbq[a, b][0][:, t * P : (t + 1) * P].bitcast(FP8X4), wbq[a, b][1][:, t * P : (t + 1) * P]
+            nc.tensor.matmul_mx(
+                out=acc,
+                lhsT=codes,
+                lhsT_scale=scales,
+                rhs=xq[a, h][0][:, cols].bitcast(FP8X4),
+                rhs_scale=xq[a, h][1][:, cols],
+                start=(a == 0),
+                stop=(a == PASSES - 1),
+            )
 
-        def a_out(b, h, side, tag):
-            a_sb[b, h] = f32_quad(tag)
+        def view_out(kind, b, h, t, acc, cols):
+            if (kind, b, h) not in views:
+                views[kind, b, h] = f32_quad("plane%d" % (4 * h + 2 * b + kind // 2))
+            nc.scalar.activation(
+                out=slots(views[kind, b, h])[:, t, cols], in_=acc, func=IDENTITY, bias=bias[:, t, kind + b : kind + b + 1]
+            )
+
+        def view(kind, b, h, side, passes=range(PASSES)):
             for t in range(PACK):
-                nc.scalar.activation(out=a_sb[b, h][:, t, :], in_=banks[side + t][:], func=IDENTITY, bias=bias[:, PACK * b + t, BA : BA + 1])
+                for a in passes:
+                    view_pass(kind, b, h, t, a, banks[side + t][:], slice(0, W))
+            if passes[-1] == PASSES - 1:
+                for t in range(PACK):
+                    view_out(kind, b, h, t, banks[side + t][:], slice(0, W))
 
-        def mx_group(bank, stationary, cols, moving):
-            for n in range(len(moving)):
-                nc.tensor.matmul_mx(
-                    out=bank[:],
-                    lhsT=stationary[n][0][:, cols].bitcast(FP8X4),
-                    lhsT_scale=stationary[n][1][:, cols],
-                    rhs=moving[n][0][:].bitcast(FP8X4),
-                    rhs_scale=moving[n][1][:],
-                    start=(n == 0),
-                    stop=(n == len(moving) - 1),
-                )
+        def side_by_side(first_bank, width, per_bank=2):
+            return [banks[first_bank + n // per_bank][:, (n % per_bank) * width : (n % per_bank + 1) * width] for n in range(4)]
 
-        def b_product(b, h, side):
+        def view_part(kind, b, h, cols, accs):
             for t in range(PACK):
-                mx_group(banks[side + t], [wbq[a, b] for a in range(PASSES)], slice(t * P, (t + 1) * P), [xq[a, h] for a in range(PASSES)])
+                for a in range(PASSES):
+                    view_pass(kind, b, h, t, a, accs[t], cols)
+            for t in range(PACK):
+                view_out(kind, b, h, t, accs[t], cols)
 
-        h_slots, h_words = {}, {}
-
-        def h_product(b, h, side, cols=slice(0, W)):
+        def product(b, h, cols=slice(0, W)):
             if cols.start == 0:
-                h_slots[b, h] = f32_quad("plane%d" % b)
-            for t in range(PACK):
-                nc.vector.scalar_tensor_tensor(
-                    out=h_slots[b, h][:, t, cols],
-                    in0=banks[side + t][:, cols],
-                    scalar=bias[:, PACK * b + t, BB : BB + 1],
-                    in1=a_sb[b, h][:, t, cols],
-                    op0=ADD,
-                    op1=MULT,
-                )
-
-        def quantize_h(b, h, engine, cols=slice(0, W)):
-            if cols.start == 0:
-                h_words[b, h] = bf16_words("words%d" % b)
+                words["h", b, h] = bf16_words("words%d" % b)
                 hq[b, h] = mx_operand("hq%d%d" % (b, h))
-            piece = h_words[b, h][:, cols.start * PACK : cols.stop * PACK]
-            copy_on(engine, words_walk(piece), slots_walk(h_slots[b, h][:, :, cols]))
-            nc.vector.quantize_mx(out=hq[b, h][0][:, cols].bitcast(FP8X4), scales=hq[b, h][1][:, cols], in_=piece)
+            nc.vector.tensor_tensor(
+                words_walk(words["h", b, h], cols), slots_walk(views[BA, b, h], cols), slots_walk(views[BB, b, h], cols), MULT
+            )
 
-        def logit_pass(b, h, side, cols=slice(0, W)):
+        def quantize_h(b, h, cols=slice(0, W)):
+            quantize(hq[b, h], words["h", b, h], cols)
+
+        results = {}
+
+        def logit_passes(b, h, accs, cols=slice(0, W), per_bank=1):
             for c in range(OUT_TILES):
                 nc.tensor.matmul_mx(
-                    out=banks[side + c][:, cols],
+                    out=accs[c],
                     lhsT=woq[b][0][:, c * P : (c + 1) * P].bitcast(FP8X4),
                     lhsT_scale=woq[b][1][:, c * P : (c + 1) * P],
                     rhs=hq[b, h][0][:, cols].bitcast(FP8X4),
                     rhs_scale=hq[b, h][1][:, cols],
-                    start=(b == 0),
-                    stop=(b == BLOCKS - 1),
+                    start=(b == 0 and c % per_bank == 0),
+                    stop=(b == BLOCKS - 1 and c % per_bank == per_bank - 1),
                 )
 
-        def logits_out(h, side, on_vector, cols=slice(0, W)):
+        def logits_out(h, accs, on_vector, cols=slice(0, W), per_store=1):
+            if h not in results:
+                results[h] = f32_quad("picked0%d" % h)
+            rows = out[:, h * W + cols.start : h * W + cols.stop].rearrange("(c p) j -> p c j", p=P)
             for c in range(OUT_TILES):
-                tag = "result%d%d" % (c, side)
-                result = keep.tile([P, W], F32, name=tag, tag=tag)
-                bo_col = bo_cols[:, c : c + 1]
+                result = slots(results[h])[:, c, cols]
+                bo_col = bias[:, 0, BO + c : BO + c + 1]
                 if c in on_vector:
-                    nc.vector.tensor_scalar(out=result[:, cols], in0=banks[side + c][:, cols], scalar1=bo_col, scalar2=None, op0=ADD)
+                    nc.vector.tensor_scalar(out=result, in0=accs[c], scalar1=bo_col, scalar2=None, op0=ADD)
                 else:
-                    nc.scalar.activation(out=result[:, cols], in_=banks[side + c][:, cols], func=IDENTITY, bias=bo_col)
-                nc.sync.dma_start(
-                    out=out[c * P : (c + 1) * P, h * W + cols.start : h * W + cols.stop], in_=result[:, cols]
-                )
+                    nc.scalar.activation(out=result, in_=accs[c], func=IDENTITY, bias=bo_col)
+                if (c + 1) % per_store == 0:
+                    tiles = slice(c + 1 - per_store, c + 1)
+                    nc.sync.dma_start(out=rows[:, tiles, :], in_=slots(results[h])[:, tiles, cols])
 
-        def b_pass(b, h, a):
-            for t in range(PACK):
-                nc.tensor.matmul_mx(
-                    out=banks[B_SIDE + t][:],
-                    lhsT=wbq[a, b][0][:, t * P : (t + 1) * P].bitcast(FP8X4),
-                    lhsT_scale=wbq[a, b][1][:, t * P : (t + 1) * P],
-                    rhs=xq[a, h][0][:].bitcast(FP8X4),
-                    rhs_scale=xq[a, h][1][:],
-                    start=(a == 0),
-                    stop=(a == PASSES - 1),
-                )
-
-        left, right = slice(0, W // 2), slice(W // 2, W)
+        half = W // 2
+        left, right = slice(0, half), slice(half, W)
         for i in range(PACK):
             for h in range(HALVES):
                 gather(0, i, h)
-        quantize_x(0, 0)
-        quantize_x(0, 1)
-        quantize_wb(0, 0, "scalar")
-        quantize_wb(1, 0, "scalar")
-        for i in range(PACK - 1):
-            for h in range(HALVES):
-                gather(1, i, h)
+        round_x(0, 0, W)
+        round_x(0, 1, W)
+        gather(1, 0, 0)
         permute_wa_scales()
         permute_wa_codes()
-        gather(1, PACK - 1, 0)
-        a_pass(0, 0, 0, 0)
-        b_pass(0, 0, 0)
-        quantize_x(1, 0, 384)
-        gather(1, PACK - 1, 1)
-        a_pass(0, 0, 1, 0)
-        b_pass(0, 0, 1)
-        quantize_wb(0, 1, "vector")
-        quantize_x(1, 1, 512)
-        quantize_wb(1, 1, "vector")
-        a_out(0, 0, 0, "quad00")
-        h_product(0, 0, 4)
-        for a in range(PASSES):
-            a_pass(1, 0, a, 0)
-        b_product(1, 0, 4)
-        a_out(1, 0, 0, "quad01")
-        quantize_wo(0, "scalar")
-        quantize_h(0, 0, "vector")
-        h_product(1, 0, 4)
-        for a in range(PASSES):
-            a_pass(0, 1, a, 0)
-        b_product(0, 1, 4)
-        a_out(0, 1, 0, "quad10")
-        quantize_wo(1, "scalar")
-        quantize_h(1, 0, "scalar")
-        h_product(0, 1, 4)
-        for a in range(PASSES):
-            a_pass(1, 1, a, 0)
-        b_product(1, 1, 4)
-        a_out(1, 1, 0, "quad11")
-        logit_pass(0, 0, 0)
-        logit_pass(1, 0, 0)
-        quantize_h(0, 1, "vector")
-        h_product(1, 1, 4, left)
-        logits_out(0, 0, ())
-        quantize_h(1, 1, "vector", left)
-        h_product(1, 1, 4, right)
-        logit_pass(0, 1, 0, left)
-        logit_pass(1, 1, 0, left)
-        quantize_h(1, 1, "vector", right)
-        logit_pass(0, 1, 4, right)
-        logits_out(1, 0, (), left)
-        logit_pass(1, 1, 4, right)
-        logits_out(1, 4, (1, 3), right)
+        gather(1, 0, 1)
+        quantize_x(0, 0)
+        gather(1, 1, 0)
+        quantize_x(0, 1)
+        gather(1, 1, 1)
+        gather(1, 2, 0)
+        view(BA, 0, 0, 0, range(0, 1))
+        view(BA, 1, 0, 4, range(0, 1))
+        gather(1, 3, 0)
+        round_x(1, 0, 352)
+        gather(1, 2, 1)
+        quantize_x(1, 0)
+        gather(1, 3, 1)
+        round_wb(0, 0, PACK, "wwords0")
+        view(BA, 0, 0, 0, range(1, 2))
+        view(BA, 1, 0, 4, range(1, 2))
+        round_wb(1, 0, 0, "wwords1")
+        quantize_wb(0, 0)
+        round_x(1, 1, 0)
+        quantize_wb(1, 0)
+        view(BB, 0, 0, 0)
+        round_wb(0, 1, 0, "wwords0")
+        quantize_x(1, 1)
+        view(BA, 0, 1, 4)
+        round_wb(1, 1, 0, "wwords1")
+        quantize_wb(0, 1)
+        product(0, 0)
+        quantize_wb(1, 1)
+        view(BB, 1, 0, 0)
+        round_wo(0, "vector", "wwords0")
+        quantize_h(0, 0)
+        view(BB, 0, 1, 4)
+        round_wo(1, "vector", "wwords1")
+        quantize_wo(0)
+        product(1, 0)
+        quantize_wo(1)
+        view(BA, 1, 1, 0)
+        product(0, 1)
+        quantize_h(1, 0)
+        quantize_h(0, 1)
+        q3, q4 = slice(half, half + P), slice(half + P, W)
+        view_part(BB, 1, 1, left, side_by_side(4, half))
+        view_part(BB, 1, 1, q3, side_by_side(6, P, 4))
+        view_part(BB, 1, 1, q4, side_by_side(7, P, 4))
+        whole = [banks[c][:] for c in range(OUT_TILES)]
+        for b in range(BLOCKS):
+            logit_passes(b, 0, whole)
+        logits_out(0, whole, ())
+        product(1, 1, left)
+        product(1, 1, q3)
+        logit_passes(0, 1, side_by_side(4, half), left, 2)
+        quantize_h(1, 1, left)
+        product(1, 1, q4)
+        logit_passes(1, 1, side_by_side(4, half), left, 2)
+        quantize_h(1, 1, q3)
+        logit_passes(0, 1, side_by_side(6, P, 4), q3, 4)
+        logit_passes(1, 1, side_by_side(6, P, 4), q3, 4)
+        logit_passes(0, 1, side_by_side(7, P, 4), q4, 4)
+        quantize_h(1, 1, q4)
+        logit_passes(1, 1, side_by_side(7, P, 4), q4, 4)
+        logits_out(1, side_by_side(4, half), (2, 3), left, 2)
+        logits_out(1, side_by_side(6, P, 4), (), q3, 4)
+        logits_out(1, side_by_side(7, P, 4), (0, 1, 2, 3), q4, 4)

@@ -111,20 +111,27 @@ def tile_list_hashed_click_logits_kernel(tc, xT, wgt, offs, wa_words, wa_scales,
         nc.sync.dma_start(out=weights[0], in_=wgt[:, 0:W])
         load_plane(0, 0)
         nc.sync.dma_start(out=weights[1], in_=wgt[:, W : 2 * W])
-        nc.scalar.dma_start(out=bias_raw[BA : BA + BLOCKS, :], in_=ba.rearrange("(b r) -> b r", b=BLOCKS))
-        nc.scalar.dma_start(out=bias_raw[BB : BB + BLOCKS, :], in_=bb.rearrange("(b r) -> b r", b=BLOCKS))
-        nc.scalar.dma_start(out=bias_rows[BO : BO + OUT_TILES, 0:P], in_=bo.rearrange("(c p) -> c p", p=P))
-        for q in range(4):
-            nc.scalar.dma_start(
-                out=wa_scale_raw[32 * q : 32 * q + 4, :].bitcast(I32).rearrange("p (a n) -> p a n", a=PASSES),
-                in_=wa_scales.bitcast(I32)[:, 4 * q : 4 * q + 4, :].rearrange("a r n -> r a n"),
+
+        def load_wa_scales(r):
+            nc.sync.dma_start(
+                out=wa_scale_raw[r:P:32, :].bitcast(I32).rearrange("p (a n) -> p a n", a=PASSES),
+                in_=wa_scales.bitcast(I32)[:, r:16:4, :].rearrange("a q n -> q a n"),
             )
-        for i in range(1, PACK):
-            load_plane(0, i)
+
+        load_plane(0, 1)
+        nc.sync.dma_start(out=bias_raw[BA : BA + BLOCKS, :], in_=ba.rearrange("(b r) -> b r", b=BLOCKS))
+        nc.sync.dma_start(out=bias_raw[BB : BB + BLOCKS, :], in_=bb.rearrange("(b r) -> b r", b=BLOCKS))
+        load_plane(0, 2)
+        nc.sync.dma_start(out=bias_rows[BO : BO + OUT_TILES, 0:P], in_=bo.rearrange("(c p) -> c p", p=P))
+        load_wa_scales(0)
+        load_wa_scales(1)
         nc.sync.dma_start(
             out=wa_raw[:].bitcast(I32).rearrange("p (a n) -> p a n", a=PASSES),
             in_=wa_words.bitcast(I32).rearrange("a p n -> p a n"),
         )
+        load_wa_scales(2)
+        load_wa_scales(3)
+        load_plane(0, 3)
         for i in range(PACK):
             load_plane(1, i)
         for b in range(BLOCKS):

@@ -107,10 +107,6 @@ def tile_list_hashed_click_logits_kernel(tc, xT, wgt, offs, wa_words, wa_scales,
         nc.vector.memset(wa_scale_raw[:].bitcast(I32), 0)
         nc.vector.memset(bias_rows[:], 0.0)
         make_identity(nc, identity[:])
-        nc.sync.dma_start(offsets[:], offs)
-        nc.sync.dma_start(out=weights[0], in_=wgt[:, 0:W])
-        load_plane(0, 0)
-        nc.sync.dma_start(out=weights[1], in_=wgt[:, W : 2 * W])
 
         def load_wa_scales(r):
             nc.sync.dma_start(
@@ -118,10 +114,16 @@ def tile_list_hashed_click_logits_kernel(tc, xT, wgt, offs, wa_words, wa_scales,
                 in_=wa_scales.bitcast(I32)[:, r:16:4, :].rearrange("a q n -> q a n"),
             )
 
-        load_plane(0, 1)
+        load_plane(0, 0)
+        nc.sync.dma_start(out=weights[0], in_=wgt[:, 0:W])
+        nc.sync.dma_start(offsets[:], offs)
+        nc.sync.dma_start(out=weights[1], in_=wgt[:, W : 2 * W])
+        for i in range(1, PACK):
+            load_plane(0, i)
+        load_plane(1, 0)
         nc.sync.dma_start(out=bias_raw[BA : BA + BLOCKS, :], in_=ba.rearrange("(b r) -> b r", b=BLOCKS))
         nc.sync.dma_start(out=bias_raw[BB : BB + BLOCKS, :], in_=bb.rearrange("(b r) -> b r", b=BLOCKS))
-        load_plane(0, 2)
+        load_plane(1, 1)
         nc.sync.dma_start(out=bias_rows[BO : BO + OUT_TILES, 0:P], in_=bo.rearrange("(c p) -> c p", p=P))
         load_wa_scales(0)
         load_wa_scales(1)
@@ -131,9 +133,8 @@ def tile_list_hashed_click_logits_kernel(tc, xT, wgt, offs, wa_words, wa_scales,
         )
         load_wa_scales(2)
         load_wa_scales(3)
-        load_plane(0, 3)
-        for i in range(PACK):
-            load_plane(1, i)
+        load_plane(1, 2)
+        load_plane(1, 3)
         for b in range(BLOCKS):
             for a in range(PASSES):
                 load_wb(a, b)
@@ -288,13 +289,13 @@ def tile_list_hashed_click_logits_kernel(tc, xT, wgt, offs, wa_words, wa_scales,
         round_x(0, 0, W)
         round_x(0, 1, W)
         gather(1, 0, 0)
-        permute_wa_scales()
-        permute_wa_codes()
         gather(1, 0, 1)
         quantize_x(0, 0)
         gather(1, 1, 0)
-        quantize_x(0, 1)
         gather(1, 1, 1)
+        quantize_x(0, 1)
+        permute_wa_scales()
+        permute_wa_codes()
         gather(1, 2, 0)
         view(BA, 0, 0, 0, range(0, 1))
         view(BA, 1, 0, 4, range(0, 1))

@@ -159,7 +159,7 @@ def tile_list_hashed_click_logits_kernel(tc, xT, wgt, offs, wa_words, wa_scales,
             if (a, h) == (1, 0):
                 words["x", a, h] = late[:, (PACK - 1) * W : (PACK + 1) * W].bitcast(BF16)
             else:
-                words["x", a, h] = bf16_words("words%d" % h)
+                words["x", a, h] = bf16_words("words%d" % h if a == 0 else "wwords0")
             for engine, cols in (("scalar", slice(0, on_scalar)), ("vector", slice(on_scalar, W))):
                 if cols.stop > cols.start:
                     copy_on(engine, words_walk(words["x", a, h], cols), slots_walk(picked[a, h], cols))
@@ -309,25 +309,26 @@ def tile_list_hashed_click_logits_kernel(tc, xT, wgt, offs, wa_words, wa_scales,
         view(BA, 1, 0, 4, range(1, 2))
         round_wb(1, 0, 0, "wwords1")
         quantize_wb(0, 0)
-        round_x(1, 1, 0)
+        view(BB, 0, 0, 0, range(0, 1))
         quantize_wb(1, 0)
-        view(BB, 0, 0, 0)
-        round_wb(0, 1, 0, "wwords0")
+        view(BB, 0, 0, 0, range(1, 2))
+        round_x(1, 1, 0)
+        round_wb(0, 1, 0, "wwords2")
         quantize_x(1, 1)
         view(BA, 0, 1, 4)
+        view(BB, 0, 1, 0)
         round_wb(1, 1, 0, "wwords1")
         quantize_wb(0, 1)
-        product(0, 0)
         quantize_wb(1, 1)
-        view(BB, 1, 0, 0)
+        view(BB, 1, 0, 4)
+        view(BA, 1, 1, 0)
+        product(0, 0)
         round_wo(0, "vector", "wwords0")
         quantize_h(0, 0)
-        view(BB, 0, 1, 4)
-        round_wo(1, "vector", "wwords1")
+        round_wo(1, "vector", "wwords2")
         quantize_wo(0)
         product(1, 0)
         quantize_wo(1)
-        view(BA, 1, 1, 0)
         product(0, 1)
         quantize_h(1, 0)
         quantize_h(0, 1)

@@ -27,6 +27,7 @@ HALVES = S // W
 OUT_TILES = N // P
 BA, BB, BO = 0, 2, 4
 WGT0_AT = 2 * W
+ALL = slice(0, W)
 
 
 def tile_list_hashed_click_logits_kernel(tc, xT, wgt, offs, wa_words, wa_scales, ba, wb, bb, wo, bo, out):
@@ -41,7 +42,7 @@ def tile_list_hashed_click_logits_kernel(tc, xT, wgt, offs, wa_words, wa_scales,
         def slots(quad):
             return quad[:, :].rearrange("p (t c) -> p t c", t=PACK)
 
-        def bf16_words(tag):
+        def bf16_quad(tag):
             return keep.tile([P, PACK * W], BF16, name=tag, tag=tag, align_bytes=64)
 
         def mx_operand(tag):
@@ -52,16 +53,24 @@ def tile_list_hashed_click_logits_kernel(tc, xT, wgt, offs, wa_words, wa_scales,
         def copy_on(engine, dst, src):
             if engine == "vector":
                 nc.vector.tensor_copy(out=dst, in_=src)
-            else:
+            elif engine == "scalar":
                 nc.scalar.copy(out=dst, in_=src)
+            else:
+                nc.gpsimd.tensor_scalar(out=dst, in0=src, scalar1=1.0, scalar2=0.0, op0=MULT, op1=ADD)
 
-        def slots_walk(quad, cols=slice(0, W)):
-            return slots(quad)[:, :, cols].rearrange("p t (c e) -> p c t e", e=PACK)
+        def interleave(words, quad, shares):
+            for engine, cols in shares:
+                dst, src = words[:, cols.start * PACK : cols.stop * PACK], slots(quad)[:, :, cols]
+                if engine == "gpsimd":
+                    copy_on(engine, dst.rearrange("p (c t) -> p c t", t=PACK), src.rearrange("p t c -> p c t"))
+                else:
+                    copy_on(
+                        engine,
+                        dst.rearrange("p (c e t) -> p c t e", e=PACK, t=PACK),
+                        src.rearrange("p t (c e) -> p c t e", e=PACK),
+                    )
 
-        def words_walk(words, cols=slice(0, W)):
-            return words[:, cols.start * PACK : cols.stop * PACK].rearrange("p (c e t) -> p c t e", e=PACK, t=PACK)
-
-        def quantize(operand, words, cols=slice(0, W)):
+        def quantize(operand, words, cols=ALL):
             codes, scales = operand
             nc.vector.quantize_mx(
                 out=codes[:, cols].bitcast(FP8X4), scales=scales[:, cols], in_=words[:, cols.start * PACK : cols.stop * PACK]
@@ -100,9 +109,9 @@ def tile_list_hashed_click_logits_kernel(tc, xT, wgt, offs, wa_words, wa_scales,
 
         def load_wo(b):
             wo_raw[b] = f32_quad("wo_raw%d" % b)
-            rows = wo[b * W : (b + 1) * W, :].rearrange("(g t i) n -> i g t n", t=PACK, i=2)
-            for i in range(2):
-                nc.sync.dma_start(out=slots(wo_raw[b])[i:P:2, :, :], in_=rows[i])
+            rows = wo[b * W : (b + 1) * W, :].rearrange("(g t i) n -> t g i n", t=PACK, i=PACK)
+            for t in range(PACK):
+                nc.sync.dma_start(out=slots(wo_raw[b])[:, t, :], in_=rows[t])
 
         nc.vector.memset(wa_scale_raw[:].bitcast(I32), 0)
         nc.vector.memset(bias_rows[:], 0.0)
@@ -142,27 +151,36 @@ def tile_list_hashed_click_logits_kernel(tc, xT, wgt, offs, wa_words, wa_scales,
             load_wo(b)
 
         nc.scalar.copy(
-            out=bias_rows[0:4, :].rearrange("p (t g i) -> p t g i", t=PACK, i=2),
-            in_=bias_raw[:].rearrange("p (g t i) -> p t g i", t=PACK, i=2),
+            out=bias_rows[0:4, :].rearrange("p (t g i) -> p t g i", t=PACK, i=PACK),
+            in_=bias_raw[:].rearrange("p (g t i) -> p t g i", t=PACK, i=PACK),
         )
         for t in range(PACK):
             nc.tensor.transpose(banks[0][:, t * P : (t + 1) * P], bias_rows[:, t * P : (t + 1) * P], identity[:])
         nc.scalar.activation(out=bias[:], in_=banks[0][:].rearrange("p (t c) -> p t c", t=PACK)[:, :, 0:8], func=IDENTITY)
 
-        xq, wbq, woq, hq, words, views = {}, {}, {}, {}, {}, {}
+        xq, wbq, woq, hq, words, a_view, h_rows, results = {}, {}, {}, {}, {}, {}, {}, {}
+
+        quad = PACK * W
+        shared = keep.tile([P, 3 * quad], BF16, name="shared", align_bytes=64)
+
+        def shared_quad(start):
+            return shared[:, start : start + quad]
+
+        words["h", 0, 0], words["wo", 0], words["wo", 1] = shared_quad(0), shared_quad(quad), shared_quad(2 * quad)
+        words["h", 1, 0], words["h", 0, 1] = shared_quad(quad // 2), shared_quad(5 * quad // 4)
+        words["h", 1, 1] = shared_quad(7 * quad // 4)
+        h_rows[0, 0], h_rows[1, 1] = shared_quad(2 * quad), shared_quad(quad // 4)
+        for b in range(BLOCKS):
+            for h in range(HALVES):
+                hq[b, h] = mx_operand("hq%d%d" % (b, h))
 
         def gather(a, i, h):
             window = planes[a * PACK + i][:].indirect(offsets[:, h * (W // 16) : (h + 1) * (W // 16)])
             nc.vector.tensor_tensor(picked[a, h][:, i * W : (i + 1) * W], window, weights[h], MULT)
 
-        def round_x(a, h, on_scalar):
-            if (a, h) == (1, 0):
-                words["x", a, h] = late[:, (PACK - 1) * W : (PACK + 1) * W].bitcast(BF16)
-            else:
-                words["x", a, h] = bf16_words("words%d" % h if a == 0 else "wwords0")
-            for engine, cols in (("scalar", slice(0, on_scalar)), ("vector", slice(on_scalar, W))):
-                if cols.stop > cols.start:
-                    copy_on(engine, words_walk(words["x", a, h], cols), slots_walk(picked[a, h], cols))
+        def round_x(a, h, shares, tag=None):
+            words["x", a, h] = bf16_quad(tag) if tag else late[:, (PACK - 1) * W : (PACK + 1) * W].bitcast(BF16)
+            interleave(words["x", a, h], picked[a, h], shares)
 
         def quantize_x(a, h):
             xq[a, h] = mx_operand("xq%d%d" % (a, h))
@@ -170,91 +188,78 @@ def tile_list_hashed_click_logits_kernel(tc, xT, wgt, offs, wa_words, wa_scales,
 
         def permute_wa_codes():
             nc.vector.tensor_copy(
-                out=wa_codes[:].bitcast(I32).rearrange("p (c t g e) -> p c g t e", t=PACK, g=16, e=4),
-                in_=wa_raw[:].bitcast(I32).rearrange("p (c g e t) -> p c g t e", t=PACK, g=16, e=4),
+                out=wa_codes[:].bitcast(I32).rearrange("p (c t g e) -> p c g t e", t=PACK, g=32, e=2),
+                in_=wa_raw[:].bitcast(I32).rearrange("p (c g t e) -> p c g t e", t=PACK, g=32, e=2),
             )
 
         def permute_wa_scales():
             nc.vector.tensor_copy(
-                out=wa_scale[:].bitcast(U16).rearrange("p (c t g e) -> p c g t e", t=PACK, g=8, e=8),
-                in_=wa_scale_raw[:].bitcast(U16).rearrange("p (c g e t) -> p c g t e", t=PACK, g=8, e=8),
+                out=wa_scale[:].bitcast(I32).rearrange("p (c t g e) -> p c g t e", t=PACK, g=8, e=4),
+                in_=wa_scale_raw[:].bitcast(I32).rearrange("p (c g e t) -> p c g t e", t=PACK, g=8, e=4),
             )
 
-        def round_wb(a, b, on_scalar, tag):
-            words["wb", a, b] = bf16_words(tag)
-            dst = words["wb", a, b][:].rearrange("p (t g i j) -> p t g j i", t=PACK, i=2, j=PACK)
-            src = wb_raw[a, b][:].rearrange("p (j g t i) -> p t g j i", j=PACK, t=PACK, i=2)
-            for engine, tiles in (("scalar", slice(0, on_scalar)), ("vector", slice(on_scalar, PACK))):
-                if tiles.stop > tiles.start:
-                    copy_on(engine, dst[:, tiles], src[:, tiles])
+        def round_wb(a, b, shares, tag):
+            words["wb", a, b] = bf16_quad(tag)
+            dst = words["wb", a, b][:].rearrange("p (t g i j) -> p t g j i", t=PACK, i=PACK, j=PACK)
+            src = wb_raw[a, b][:].rearrange("p (j g t i) -> p t g j i", j=PACK, t=PACK, i=PACK)
+            for engine, tiles in shares:
+                copy_on(engine, dst[:, tiles], src[:, tiles])
 
         def quantize_wb(a, b):
             wbq[a, b] = mx_operand("wbq%d%d" % (a, b))
             quantize(wbq[a, b], words["wb", a, b])
 
-        def round_wo(b, engine, tag):
-            words["wo", b] = bf16_words(tag)
-            copy_on(engine, words_walk(words["wo", b]), slots_walk(wo_raw[b]))
+        def round_wo(b, shares):
+            interleave(words["wo", b], wo_raw[b], shares)
 
         def quantize_wo(b):
             woq[b] = mx_operand("woq%d" % b)
             quantize(woq[b], words["wo", b])
 
-        def view_pass(kind, b, h, t, a, acc, cols):
-            if kind == BA:
-                col = a * H + b * W + t * P
-                codes, scales = wa_codes[:, 2 * col : 2 * (col + P)].bitcast(FP4X4), wa_scale[:, col : col + P]
-            else:
-                codes, scales = wbq[a, b][0][:, t * P : (t + 1) * P].bitcast(FP8X4), wbq[a, b][1][:, t * P : (t + 1) * P]
-            nc.tensor.matmul_mx(
-                out=acc,
-                lhsT=codes,
-                lhsT_scale=scales,
-                rhs=xq[a, h][0][:, cols].bitcast(FP8X4),
-                rhs_scale=xq[a, h][1][:, cols],
-                start=(a == 0),
-                stop=(a == PASSES - 1),
-            )
-
-        def view_out(kind, b, h, t, acc, cols):
-            if (kind, b, h) not in views:
-                views[kind, b, h] = f32_quad("plane%d" % (4 * h + 2 * b + kind // 2))
-            nc.scalar.activation(
-                out=slots(views[kind, b, h])[:, t, cols], in_=acc, func=IDENTITY, bias=bias[:, t, kind + b : kind + b + 1]
-            )
-
-        def view(kind, b, h, side, passes=range(PASSES)):
+        def first_stage(kind, b, h, accs, passes=range(PASSES), cols=ALL):
             for t in range(PACK):
                 for a in passes:
-                    view_pass(kind, b, h, t, a, banks[side + t][:], slice(0, W))
-            if passes[-1] == PASSES - 1:
-                for t in range(PACK):
-                    view_out(kind, b, h, t, banks[side + t][:], slice(0, W))
+                    if kind == BA:
+                        col = a * H + b * W + t * P
+                        codes, scales = wa_codes[:, 2 * col : 2 * (col + P)].bitcast(FP4X4), wa_scale[:, col : col + P]
+                    else:
+                        tile = slice(t * P, (t + 1) * P)
+                        codes, scales = wbq[a, b][0][:, tile].bitcast(FP8X4), wbq[a, b][1][:, tile]
+                    nc.tensor.matmul_mx(
+                        out=accs[t],
+                        lhsT=codes,
+                        lhsT_scale=scales,
+                        rhs=xq[a, h][0][:, cols].bitcast(FP8X4),
+                        rhs_scale=xq[a, h][1][:, cols],
+                        start=(a == 0),
+                        stop=(a == PASSES - 1),
+                    )
 
-        def side_by_side(first_bank, width, per_bank=2):
-            return [banks[first_bank + n // per_bank][:, (n % per_bank) * width : (n % per_bank + 1) * width] for n in range(4)]
-
-        def view_part(kind, b, h, cols, accs):
+        def a_out(b, h, accs):
+            a_view[b, h] = f32_quad("plane%d" % (2 * h + b))
             for t in range(PACK):
-                for a in range(PASSES):
-                    view_pass(kind, b, h, t, a, accs[t], cols)
+                nc.scalar.activation(
+                    out=slots(a_view[b, h])[:, t, :], in_=accs[t], func=IDENTITY, bias=bias[:, t, BA + b : BA + b + 1]
+                )
+
+        def product(b, h, accs, cols=ALL):
             for t in range(PACK):
-                view_out(kind, b, h, t, accs[t], cols)
+                nc.vector.scalar_tensor_tensor(
+                    out=slots(h_rows[b, h])[:, t, cols],
+                    in0=accs[t],
+                    scalar=bias[:, t, BB + b : BB + b + 1],
+                    in1=slots(a_view[b, h])[:, t, cols],
+                    op0=ADD,
+                    op1=MULT,
+                )
 
-        def product(b, h, cols=slice(0, W)):
-            if cols.start == 0:
-                words["h", b, h] = bf16_words("words%d" % b)
-                hq[b, h] = mx_operand("hq%d%d" % (b, h))
-            nc.vector.tensor_tensor(
-                words_walk(words["h", b, h], cols), slots_walk(views[BA, b, h], cols), slots_walk(views[BB, b, h], cols), MULT
-            )
+        def interleave_h(b, h, shares):
+            interleave(words["h", b, h], h_rows[b, h], shares)
 
-        def quantize_h(b, h, cols=slice(0, W)):
+        def quantize_h(b, h, cols=ALL):
             quantize(hq[b, h], words["h", b, h], cols)
 
-        results = {}
-
-        def logit_passes(b, h, accs, cols=slice(0, W), per_bank=1):
+        def logit_passes(b, h, accs, cols=ALL, per_bank=1):
             for c in range(OUT_TILES):
                 nc.tensor.matmul_mx(
                     out=accs[c],
@@ -266,7 +271,7 @@ def tile_list_hashed_click_logits_kernel(tc, xT, wgt, offs, wa_words, wa_scales,
                     stop=(b == BLOCKS - 1 and c % per_bank == per_bank - 1),
                 )
 
-        def logits_out(h, accs, on_vector, cols=slice(0, W), per_store=1):
+        def logits_out(h, accs, on_vector, cols=ALL, per_store=1):
             if h not in results:
                 results[h] = f32_quad("picked0%d" % h)
             rows = out[:, h * W + cols.start : h * W + cols.stop].rearrange("(c p) j -> p c j", p=P)
@@ -281,13 +286,20 @@ def tile_list_hashed_click_logits_kernel(tc, xT, wgt, offs, wa_words, wa_scales,
                     tiles = slice(c + 1 - per_store, c + 1)
                     nc.sync.dma_start(out=rows[:, tiles, :], in_=slots(results[h])[:, tiles, cols])
 
+        def side_by_side(first_bank, width):
+            per_bank = W // width
+            return [banks[first_bank + n // per_bank][:, (n % per_bank) * width : (n % per_bank + 1) * width] for n in range(4)]
+
+        low, high = side_by_side(0, W), side_by_side(4, W)
+        scalar, vector = [("scalar", ALL)], [("vector", ALL)]
+        tiles_scalar, tiles_vector = [("scalar", slice(0, PACK))], [("vector", slice(0, PACK))]
         half = W // 2
-        left, right = slice(0, half), slice(half, W)
+        left, q3, q4 = slice(half, W), slice(0, P), slice(P, half)
         for i in range(PACK):
             for h in range(HALVES):
                 gather(0, i, h)
-        round_x(0, 0, W)
-        round_x(0, 1, W)
+        round_x(0, 0, scalar, "words0")
+        round_x(0, 1, scalar, "words1")
         gather(1, 0, 0)
         gather(1, 0, 1)
         quantize_x(0, 0)
@@ -297,61 +309,72 @@ def tile_list_hashed_click_logits_kernel(tc, xT, wgt, offs, wa_words, wa_scales,
         permute_wa_scales()
         permute_wa_codes()
         gather(1, 2, 0)
-        view(BA, 0, 0, 0, range(0, 1))
-        view(BA, 1, 0, 4, range(0, 1))
+        first_stage(BA, 0, 0, low, range(0, 1))
+        first_stage(BA, 1, 0, high, range(0, 1))
         gather(1, 3, 0)
-        round_x(1, 0, 352)
+        round_x(1, 0, [("scalar", slice(0, 352)), ("vector", slice(352, W))])
         gather(1, 2, 1)
         quantize_x(1, 0)
         gather(1, 3, 1)
-        round_wb(0, 0, PACK, "wwords0")
-        view(BA, 0, 0, 0, range(1, 2))
-        view(BA, 1, 0, 4, range(1, 2))
-        round_wb(1, 0, 0, "wwords1")
+        round_wb(0, 0, tiles_scalar, "words2")
+        first_stage(BA, 0, 0, low, range(1, 2))
+        a_out(0, 0, low)
+        first_stage(BA, 1, 0, high, range(1, 2))
+        round_wb(1, 0, tiles_vector, "words3")
         quantize_wb(0, 0)
-        view(BB, 0, 0, 0, range(0, 1))
+        first_stage(BB, 0, 0, low, range(0, 1))
+        round_x(1, 1, vector, "words0")
         quantize_wb(1, 0)
-        view(BB, 0, 0, 0, range(1, 2))
-        round_x(1, 1, 0)
-        round_wb(0, 1, 0, "wwords2")
+        first_stage(BB, 0, 0, low, range(1, 2))
+        round_wb(0, 1, tiles_scalar, "words1")
+        a_out(1, 0, high)
         quantize_x(1, 1)
-        view(BA, 0, 1, 4)
-        view(BB, 0, 1, 0)
-        round_wb(1, 1, 0, "wwords1")
+        first_stage(BA, 0, 1, high)
+        product(0, 0, low)
+        round_wb(1, 1, tiles_vector, "words2")
         quantize_wb(0, 1)
+        first_stage(BB, 1, 0, low, range(0, 1))
         quantize_wb(1, 1)
-        view(BB, 1, 0, 4)
-        view(BA, 1, 1, 0)
-        product(0, 0)
-        round_wo(0, "vector", "wwords0")
+        first_stage(BB, 1, 0, low, range(1, 2))
+        interleave_h(0, 0, vector)
+        a_out(0, 1, high)
+        round_wo(0, scalar)
+        round_wo(1, [("gpsimd", slice(0, 384)), ("scalar", slice(384, W))])
+        first_stage(BA, 1, 1, high)
+        h_rows[1, 0] = bf16_quad("words3")
+        product(1, 0, low)
+        first_stage(BB, 0, 1, low)
         quantize_h(0, 0)
-        round_wo(1, "vector", "wwords2")
         quantize_wo(0)
-        product(1, 0)
-        quantize_wo(1)
-        product(0, 1)
+        a_out(1, 1, high)
+        interleave_h(1, 0, [("gpsimd", slice(0, 352)), ("scalar", slice(352, W))])
+        h_rows[0, 1] = bf16_quad("words1")
+        product(0, 1, low)
+        first_stage(BB, 1, 1, side_by_side(4, half), cols=left)
+        first_stage(BB, 1, 1, side_by_side(6, P), cols=q3)
+        first_stage(BB, 1, 1, side_by_side(7, P), cols=q4)
         quantize_h(1, 0)
-        quantize_h(0, 1)
-        q3, q4 = slice(half, half + P), slice(half + P, W)
-        view_part(BB, 1, 1, left, side_by_side(4, half))
-        view_part(BB, 1, 1, q3, side_by_side(6, P, 4))
-        view_part(BB, 1, 1, q4, side_by_side(7, P, 4))
-        whole = [banks[c][:] for c in range(OUT_TILES)]
+        quantize_wo(1)
         for b in range(BLOCKS):
-            logit_passes(b, 0, whole)
-        logits_out(0, whole, ())
-        product(1, 1, left)
-        product(1, 1, q3)
+            logit_passes(b, 0, low)
+        interleave_h(0, 1, [("gpsimd", slice(0, 400)), ("scalar", slice(400, W))])
+        product(1, 1, side_by_side(4, half), left)
+        interleave_h(1, 1, [("scalar", left)])
+        product(1, 1, side_by_side(6, P), q3)
+        product(1, 1, side_by_side(7, P), q4)
+        logits_out(0, low, ())
+        quantize_h(0, 1)
         logit_passes(0, 1, side_by_side(4, half), left, 2)
+        interleave_h(1, 1, [("vector", q3)])
         quantize_h(1, 1, left)
-        product(1, 1, q4)
+        interleave_h(1, 1, [("vector", q4)])
         logit_passes(1, 1, side_by_side(4, half), left, 2)
         quantize_h(1, 1, q3)
-        logit_passes(0, 1, side_by_side(6, P, 4), q3, 4)
-        logit_passes(1, 1, side_by_side(6, P, 4), q3, 4)
-        logit_passes(0, 1, side_by_side(7, P, 4), q4, 4)
+        logit_passes(0, 1, side_by_side(6, P), q3, 4)
+        logit_passes(1, 1, side_by_side(6, P), q3, 4)
+        logit_passes(0, 1, side_by_side(7, P), q4, 4)
         quantize_h(1, 1, q4)
-        logit_passes(1, 1, side_by_side(7, P, 4), q4, 4)
+        logit_passes(1, 1, side_by_side(7, P), q4, 4)
         logits_out(1, side_by_side(4, half), (2, 3), left, 2)
-        logits_out(1, side_by_side(6, P, 4), (), q3, 4)
-        logits_out(1, side_by_side(7, P, 4), (0, 1, 2, 3), q4, 4)
+        logits_out(1, side_by_side(6, P), (), q3, 4)
+        logits_out(1, side_by_side(7, P), (0, 1, 2, 3), q4, 4)

@@ -161,15 +161,16 @@ def tile_list_hashed_click_logits_kernel(tc, xT, wgt, offs, wa_words, wa_scales,
         xq, wbq, woq, hq, words, a_view, h_rows, results = {}, {}, {}, {}, {}, {}, {}, {}
 
         quad = PACK * W
-        shared = keep.tile([P, 3 * quad], BF16, name="shared", align_bytes=64)
+        shared = keep.tile([P, 19 * W // 2], F32, name="shared", align_bytes=64)
 
         def shared_quad(start):
-            return shared[:, start : start + quad]
+            first = 3 * W // 2 + start // 2
+            return shared[:, first : first + quad // 2].bitcast(BF16)
 
         words["h", 0, 0], words["wo", 0], words["wo", 1] = shared_quad(0), shared_quad(quad), shared_quad(2 * quad)
         words["h", 1, 0], words["h", 0, 1] = shared_quad(quad // 2), shared_quad(5 * quad // 4)
         words["h", 1, 1] = shared_quad(7 * quad // 4)
-        h_rows[0, 0], h_rows[1, 1] = shared_quad(2 * quad), shared_quad(quad // 4)
+        h_rows[0, 0], h_rows[1, 1] = shared[:, 11 * W // 2 : 19 * W // 2], shared[:, 0:quad]
         for b in range(BLOCKS):
             for h in range(HALVES):
                 hq[b, h] = mx_operand("hq%d%d" % (b, h))
@@ -339,7 +340,7 @@ def tile_list_hashed_click_logits_kernel(tc, xT, wgt, offs, wa_words, wa_scales,
         interleave_h(0, 0, vector)
         a_out(0, 1, high)
         round_wo(0, scalar)
-        round_wo(1, [("gpsimd", slice(0, 384)), ("scalar", slice(384, W))])
+        round_wo(1, [("gpsimd", slice(0, 352)), ("scalar", slice(352, W))])
         first_stage(BA, 1, 1, high)
         h_rows[1, 0] = bf16_quad("words3")
         product(1, 0, low)

@@ -37,7 +37,7 @@ def tile_list_hashed_click_logits_kernel(tc, xT, wgt, offs, wa_words, wa_scales,
         psum = ctx.enter_context(tc.psum_pool(name="psum", bufs=1))
 
         def f32_quad(tag):
-            return keep.tile([P, PACK * W], F32, name=tag, tag=tag)
+            return keep.tile([P, PACK * W], F32, name=tag, tag=tag, align_bytes=64)
 
         def slots(quad):
             return quad[:, :].rearrange("p (t c) -> p t c", t=PACK)
@@ -45,9 +45,9 @@ def tile_list_hashed_click_logits_kernel(tc, xT, wgt, offs, wa_words, wa_scales,
         def bf16_quad(tag):
             return keep.tile([P, PACK * W], BF16, name=tag, tag=tag, align_bytes=64)
 
-        def mx_operand(tag):
-            codes = keep.tile([P, W], U32, name=tag + "_codes", align_bytes=64)
-            scales = keep.tile([P, W], U8, name=tag + "_scales", align_bytes=64)
+        def mx_operand(name, tag=None):
+            codes = keep.tile([P, W], U32, name=name + "_codes", tag=tag or name + "_codes", align_bytes=64)
+            scales = keep.tile([P, W], U8, name=name + "_scales", align_bytes=64)
             return codes, scales
 
         def copy_on(engine, dst, src):
@@ -98,23 +98,27 @@ def tile_list_hashed_click_logits_kernel(tc, xT, wgt, offs, wa_words, wa_scales,
             rows = xT[a * W : (a + 1) * W, :].rearrange("(p i) t -> i p t", i=PACK)
             nc.sync.dma_start(out=planes[a * PACK + i][:], in_=rows[i])
 
-        wb_raw, wo_raw = {}, {}
+        shared = keep.tile([P, 29 * P], F32, name="shared", align_bytes=64)
+        wb_raw = {(a, b): f32_quad("wb_raw%d%d" % (a, b)) for a, b in ((0, 0), (1, 0), (0, 1))}
+        wb_raw[1, 1] = shared[:, 13 * P : 29 * P]
+        wo_raw = {b: f32_quad("wo_raw%d" % b) for b in range(BLOCKS)}
+
+        def shared_words(start):
+            return shared[:, start * P : start * P + 2 * W].bitcast(BF16)
 
         def load_wb(a, b):
-            wb_raw[a, b] = f32_quad("wb_raw%d%d" % (a, b))
             nc.sync.dma_start(
                 out=slots(wb_raw[a, b]),
                 in_=wb[a * W : (a + 1) * W, b * W : (b + 1) * W].rearrange("(p j) r -> p j r", j=PACK),
             )
 
         def load_wo(b):
-            wo_raw[b] = f32_quad("wo_raw%d" % b)
             rows = wo[b * W : (b + 1) * W, :].rearrange("(g t i) n -> t g i n", t=PACK, i=PACK)
             for t in range(PACK):
                 nc.sync.dma_start(out=slots(wo_raw[b])[:, t, :], in_=rows[t])
 
-        nc.vector.memset(wa_scale_raw[:].bitcast(I32), 0)
-        nc.vector.memset(bias_rows[:], 0.0)
+        nc.gpsimd.memset(wa_scale_raw[:].bitcast(I32), 0)
+        nc.gpsimd.memset(bias_rows[:], 0.0)
         make_identity(nc, identity[:])
 
         def load_wa_scales(r):
@@ -160,27 +164,12 @@ def tile_list_hashed_click_logits_kernel(tc, xT, wgt, offs, wa_words, wa_scales,
 
         xq, wbq, woq, hq, words, a_view, h_rows, results = {}, {}, {}, {}, {}, {}, {}, {}
 
-        quad = PACK * W
-        shared = keep.tile([P, 19 * W // 2], F32, name="shared", align_bytes=64)
-
-        def shared_quad(start):
-            first = 3 * W // 2 + start // 2
-            return shared[:, first : first + quad // 2].bitcast(BF16)
-
-        words["h", 0, 0], words["wo", 0], words["wo", 1] = shared_quad(0), shared_quad(quad), shared_quad(2 * quad)
-        words["h", 1, 0], words["h", 0, 1] = shared_quad(quad // 2), shared_quad(5 * quad // 4)
-        words["h", 1, 1] = shared_quad(7 * quad // 4)
-        h_rows[0, 0], h_rows[1, 1] = shared[:, 11 * W // 2 : 19 * W // 2], shared[:, 0:quad]
-        for b in range(BLOCKS):
-            for h in range(HALVES):
-                hq[b, h] = mx_operand("hq%d%d" % (b, h))
-
         def gather(a, i, h):
             window = planes[a * PACK + i][:].indirect(offsets[:, h * (W // 16) : (h + 1) * (W // 16)])
             nc.vector.tensor_tensor(picked[a, h][:, i * W : (i + 1) * W], window, weights[h], MULT)
 
-        def round_x(a, h, shares, tag=None):
-            words["x", a, h] = bf16_quad(tag) if tag else late[:, (PACK - 1) * W : (PACK + 1) * W].bitcast(BF16)
+        def round_x(a, h, shares, place):
+            words["x", a, h] = place
             interleave(words["x", a, h], picked[a, h], shares)
 
         def quantize_x(a, h):
@@ -199,22 +188,27 @@ def tile_list_hashed_click_logits_kernel(tc, xT, wgt, offs, wa_words, wa_scales,
                 in_=wa_scale_raw[:].bitcast(I32).rearrange("p (c g e t) -> p c g t e", t=PACK, g=8, e=4),
             )
 
-        def round_wb(a, b, shares, tag):
-            words["wb", a, b] = bf16_quad(tag)
+        def round_wb(a, b, shares, place):
+            words["wb", a, b] = place
             dst = words["wb", a, b][:].rearrange("p (t g i j) -> p t g j i", t=PACK, i=PACK, j=PACK)
             src = wb_raw[a, b][:].rearrange("p (j g t i) -> p t g j i", j=PACK, t=PACK, i=PACK)
             for engine, tiles in shares:
-                copy_on(engine, dst[:, tiles], src[:, tiles])
+                if engine == "gpsimd":
+                    for t in range(tiles.start, tiles.stop):
+                        copy_on(engine, dst[:, t].rearrange("p g j i -> p g i j"), src[:, t].rearrange("p g j i -> p g i j"))
+                else:
+                    copy_on(engine, dst[:, tiles], src[:, tiles])
 
-        def quantize_wb(a, b):
-            wbq[a, b] = mx_operand("wbq%d%d" % (a, b))
+        def quantize_wb(a, b, tag=None):
+            wbq[a, b] = mx_operand("wbq%d%d" % (a, b), tag)
             quantize(wbq[a, b], words["wb", a, b])
 
-        def round_wo(b, shares):
+        def round_wo(b, shares, place):
+            words["wo", b] = place
             interleave(words["wo", b], wo_raw[b], shares)
 
-        def quantize_wo(b):
-            woq[b] = mx_operand("woq%d" % b)
+        def quantize_wo(b, tag=None):
+            woq[b] = mx_operand("woq%d" % b, tag)
             quantize(woq[b], words["wo", b])
 
         def first_stage(kind, b, h, accs, passes=range(PASSES), cols=ALL):
@@ -243,7 +237,9 @@ def tile_list_hashed_click_logits_kernel(tc, xT, wgt, offs, wa_words, wa_scales,
                     out=slots(a_view[b, h])[:, t, :], in_=accs[t], func=IDENTITY, bias=bias[:, t, BA + b : BA + b + 1]
                 )
 
-        def product(b, h, accs, cols=ALL):
+        def product(b, h, accs, cols=ALL, place=None):
+            if place is not None:
+                h_rows[b, h] = place
             for t in range(PACK):
                 nc.vector.scalar_tensor_tensor(
                     out=slots(h_rows[b, h])[:, t, cols],
@@ -254,14 +250,17 @@ def tile_list_hashed_click_logits_kernel(tc, xT, wgt, offs, wa_words, wa_scales,
                     op1=MULT,
                 )
 
-        def interleave_h(b, h, shares):
+        def interleave_h(b, h, shares, place=None):
+            if ("h", b, h) not in words:
+                words["h", b, h] = place
+                hq[b, h] = mx_operand("hq%d%d" % (b, h))
             interleave(words["h", b, h], h_rows[b, h], shares)
 
         def quantize_h(b, h, cols=ALL):
             quantize(hq[b, h], words["h", b, h], cols)
 
-        def logit_passes(b, h, accs, cols=ALL, per_bank=1):
-            for c in range(OUT_TILES):
+        def logit_passes(b, h, accs, cols=ALL, per_bank=1, tiles=range(OUT_TILES)):
+            for c in tiles:
                 nc.tensor.matmul_mx(
                     out=accs[c],
                     lhsT=woq[b][0][:, c * P : (c + 1) * P].bitcast(FP8X4),
@@ -293,14 +292,18 @@ def tile_list_hashed_click_logits_kernel(tc, xT, wgt, offs, wa_words, wa_scales,
 
         low, high = side_by_side(0, W), side_by_side(4, W)
         scalar, vector = [("scalar", ALL)], [("vector", ALL)]
-        tiles_scalar, tiles_vector = [("scalar", slice(0, PACK))], [("vector", slice(0, PACK))]
+
+        def split(first, second, at, total=W):
+            return [(first, slice(0, at)), (second, slice(at, total))]
+
         half = W // 2
-        left, q3, q4 = slice(half, W), slice(0, P), slice(P, half)
+        left, q3, q4 = slice(0, half), slice(half, half + P), slice(half + P, W)
+        tiles_scalar, tiles_vector = [("scalar", slice(0, PACK))], [("vector", slice(0, PACK))]
         for i in range(PACK):
             for h in range(HALVES):
                 gather(0, i, h)
-        round_x(0, 0, scalar, "words0")
-        round_x(0, 1, scalar, "words1")
+        round_x(0, 0, scalar, bf16_quad("words0"))
+        round_x(0, 1, scalar, bf16_quad("words1"))
         gather(1, 0, 0)
         gather(1, 0, 1)
         quantize_x(0, 0)
@@ -313,67 +316,66 @@ def tile_list_hashed_click_logits_kernel(tc, xT, wgt, offs, wa_words, wa_scales,
         first_stage(BA, 0, 0, low, range(0, 1))
         first_stage(BA, 1, 0, high, range(0, 1))
         gather(1, 3, 0)
-        round_x(1, 0, [("scalar", slice(0, 352)), ("vector", slice(352, W))])
+        round_x(1, 0, split("scalar", "vector", 352), late[:, (PACK - 1) * W : (PACK + 1) * W].bitcast(BF16))
         gather(1, 2, 1)
         quantize_x(1, 0)
         gather(1, 3, 1)
-        round_wb(0, 0, tiles_scalar, "words2")
+        round_wb(0, 0, tiles_scalar, bf16_quad("words2"))
         first_stage(BA, 0, 0, low, range(1, 2))
         a_out(0, 0, low)
         first_stage(BA, 1, 0, high, range(1, 2))
-        round_wb(1, 0, tiles_vector, "words3")
+        a_out(1, 0, high)
+        round_wb(1, 0, tiles_vector, shared_words(1))
         quantize_wb(0, 0)
         first_stage(BB, 0, 0, low, range(0, 1))
-        round_x(1, 1, vector, "words0")
+        round_x(1, 1, vector, bf16_quad("words0"))
         quantize_wb(1, 0)
         first_stage(BB, 0, 0, low, range(1, 2))
-        round_wb(0, 1, tiles_scalar, "words1")
-        a_out(1, 0, high)
         quantize_x(1, 1)
         first_stage(BA, 0, 1, high)
-        product(0, 0, low)
-        round_wb(1, 1, tiles_vector, "words2")
-        quantize_wb(0, 1)
-        first_stage(BB, 1, 0, low, range(0, 1))
-        quantize_wb(1, 1)
-        first_stage(BB, 1, 0, low, range(1, 2))
-        interleave_h(0, 0, vector)
         a_out(0, 1, high)
-        round_wo(0, scalar)
-        round_wo(1, [("gpsimd", slice(0, 352)), ("scalar", slice(352, W))])
-        first_stage(BA, 1, 1, high)
-        h_rows[1, 0] = bf16_quad("words3")
-        product(1, 0, low)
+        product(0, 0, low, place=bf16_quad("words1"))
+        round_wb(0, 1, split("gpsimd", "vector", 2, PACK), shared_words(5))
         first_stage(BB, 0, 1, low)
+        round_wb(1, 1, tiles_vector, bf16_quad("words0"))
+        quantize_wb(0, 1)
+        interleave_h(0, 0, split("gpsimd", "scalar", 384), shared_words(8))
+        round_wo(0, scalar, shared_words(0))
+        first_stage(BA, 1, 1, high)
+        product(0, 1, low, place=shared_words(16))
+        a_out(1, 1, high)
+        quantize_wb(1, 1, "plane2")
+        first_stage(BB, 1, 0, low)
         quantize_h(0, 0)
         quantize_wo(0)
-        a_out(1, 1, high)
-        interleave_h(1, 0, [("gpsimd", slice(0, 352)), ("scalar", slice(352, W))])
-        h_rows[0, 1] = bf16_quad("words1")
-        product(0, 1, low)
+        interleave_h(0, 1, [("gpsimd", slice(0, 384))], shared_words(4))
+        round_wo(1, scalar, bf16_quad("words2"))
+        product(1, 0, low, place=f32_quad("plane4"))
         first_stage(BB, 1, 1, side_by_side(4, half), cols=left)
         first_stage(BB, 1, 1, side_by_side(6, P), cols=q3)
         first_stage(BB, 1, 1, side_by_side(7, P), cols=q4)
+        interleave_h(1, 0, split("scalar", "vector", half), bf16_quad("words0"))
+        interleave_h(0, 1, [("scalar", slice(384, W))])
+        quantize_wo(1, "plane1")
         quantize_h(1, 0)
-        quantize_wo(1)
-        for b in range(BLOCKS):
-            logit_passes(b, 0, low)
-        interleave_h(0, 1, [("gpsimd", slice(0, 400)), ("scalar", slice(400, W))])
-        product(1, 1, side_by_side(4, half), left)
-        interleave_h(1, 1, [("scalar", left)])
+        for c in range(OUT_TILES):
+            for b in range(BLOCKS):
+                logit_passes(b, 0, low, tiles=[c])
+        product(1, 1, side_by_side(4, half), left, f32_quad("plane5"))
+        quantize_h(0, 1)
+        interleave_h(1, 1, split("gpsimd", "scalar", P, half), shared_words(10))
         product(1, 1, side_by_side(6, P), q3)
         product(1, 1, side_by_side(7, P), q4)
         logits_out(0, low, ())
-        quantize_h(0, 1)
         logit_passes(0, 1, side_by_side(4, half), left, 2)
-        interleave_h(1, 1, [("vector", q3)])
         quantize_h(1, 1, left)
-        interleave_h(1, 1, [("vector", q4)])
         logit_passes(1, 1, side_by_side(4, half), left, 2)
-        quantize_h(1, 1, q3)
         logit_passes(0, 1, side_by_side(6, P), q3, 4)
-        logit_passes(1, 1, side_by_side(6, P), q3, 4)
         logit_passes(0, 1, side_by_side(7, P), q4, 4)
+        interleave_h(1, 1, [("vector", q3)])
+        interleave_h(1, 1, [("vector", q4)])
+        quantize_h(1, 1, q3)
+        logit_passes(1, 1, side_by_side(6, P), q3, 4)
         quantize_h(1, 1, q4)
         logit_passes(1, 1, side_by_side(7, P), q4, 4)
         logits_out(1, side_by_side(4, half), (2, 3), left, 2)

@@ -98,13 +98,11 @@ def tile_list_hashed_click_logits_kernel(tc, xT, wgt, offs, wa_words, wa_scales,
             rows = xT[a * W : (a + 1) * W, :].rearrange("(p i) t -> i p t", i=PACK)
             nc.sync.dma_start(out=planes[a * PACK + i][:], in_=rows[i])
 
-        shared = keep.tile([P, 29 * P], F32, name="shared", align_bytes=64)
-        wb_raw = {(a, b): f32_quad("wb_raw%d%d" % (a, b)) for a, b in ((0, 0), (1, 0), (0, 1))}
-        wb_raw[1, 1] = shared[:, 13 * P : 29 * P]
+        wb_raw = {(a, b): f32_quad("wb_raw%d%d" % (a, b)) for a in range(PASSES) for b in range(BLOCKS)}
         wo_raw = {b: f32_quad("wo_raw%d" % b) for b in range(BLOCKS)}
 
-        def shared_words(start):
-            return shared[:, start * P : start * P + 2 * W].bitcast(BF16)
+        def late_words(start):
+            return late[:, start : start + 2 * W].bitcast(BF16)
 
         def load_wb(a, b):
             nc.sync.dma_start(
@@ -298,7 +296,7 @@ def tile_list_hashed_click_logits_kernel(tc, xT, wgt, offs, wa_words, wa_scales,
 
         half = W // 2
         left, q3, q4 = slice(0, half), slice(half, half + P), slice(half + P, W)
-        tiles_scalar, tiles_vector = [("scalar", slice(0, PACK))], [("vector", slice(0, PACK))]
+        tiles_vector = [("vector", slice(0, PACK))]
         for i in range(PACK):
             for h in range(HALVES):
                 gather(0, i, h)
@@ -316,68 +314,67 @@ def tile_list_hashed_click_logits_kernel(tc, xT, wgt, offs, wa_words, wa_scales,
         first_stage(BA, 0, 0, low, range(0, 1))
         first_stage(BA, 1, 0, high, range(0, 1))
         gather(1, 3, 0)
-        round_x(1, 0, split("scalar", "vector", 352), late[:, (PACK - 1) * W : (PACK + 1) * W].bitcast(BF16))
+        round_x(1, 0, split("scalar", "vector", 352), late_words(3 * W))
         gather(1, 2, 1)
         quantize_x(1, 0)
+        round_wb(0, 0, split("scalar", "vector", 2, PACK), bf16_quad("words2"))
         gather(1, 3, 1)
-        round_wb(0, 0, tiles_scalar, bf16_quad("words2"))
         first_stage(BA, 0, 0, low, range(1, 2))
         a_out(0, 0, low)
         first_stage(BA, 1, 0, high, range(1, 2))
         a_out(1, 0, high)
-        round_wb(1, 0, tiles_vector, shared_words(1))
         quantize_wb(0, 0)
         first_stage(BB, 0, 0, low, range(0, 1))
         round_x(1, 1, vector, bf16_quad("words0"))
+        quantize_x(1, 1)
+        round_wb(1, 0, tiles_vector, late_words(0))
+        round_wb(0, 1, tiles_vector, late_words(2 * W))
         quantize_wb(1, 0)
         first_stage(BB, 0, 0, low, range(1, 2))
-        quantize_x(1, 1)
         first_stage(BA, 0, 1, high)
         a_out(0, 1, high)
-        product(0, 0, low, place=bf16_quad("words1"))
-        round_wb(0, 1, split("gpsimd", "vector", 2, PACK), shared_words(5))
-        first_stage(BB, 0, 1, low)
-        round_wb(1, 1, tiles_vector, bf16_quad("words0"))
         quantize_wb(0, 1)
-        interleave_h(0, 0, split("gpsimd", "scalar", 384), shared_words(8))
-        round_wo(0, scalar, shared_words(0))
+        round_wb(1, 1, split("gpsimd", "scalar", 2, PACK), late_words(2 * W - P))
+        product(0, 0, low, place=bf16_quad("words1"))
         first_stage(BA, 1, 1, high)
-        product(0, 1, low, place=shared_words(16))
         a_out(1, 1, high)
-        quantize_wb(1, 1, "plane2")
-        first_stage(BB, 1, 0, low)
+        first_stage(BB, 0, 1, low)
+        quantize_wb(1, 1)
+        interleave_h(0, 0, split("gpsimd", "scalar", 384), late_words(2 * W))
+        round_wo(0, scalar, late_words(0))
+        product(0, 1, low, place=bf16_quad("words2"))
+        first_stage(BB, 1, 0, high)
         quantize_h(0, 0)
-        quantize_wo(0)
-        interleave_h(0, 1, [("gpsimd", slice(0, 384))], shared_words(4))
-        round_wo(1, scalar, bf16_quad("words2"))
-        product(1, 0, low, place=f32_quad("plane4"))
-        first_stage(BB, 1, 1, side_by_side(4, half), cols=left)
-        first_stage(BB, 1, 1, side_by_side(6, P), cols=q3)
-        first_stage(BB, 1, 1, side_by_side(7, P), cols=q4)
-        interleave_h(1, 0, split("scalar", "vector", half), bf16_quad("words0"))
+        quantize_wo(0, "plane2")
+        interleave_h(0, 1, [("gpsimd", slice(0, 384))], late_words(W))
+        round_wo(1, scalar, bf16_quad("words0"))
         interleave_h(0, 1, [("scalar", slice(384, W))])
+        product(1, 0, high, place=f32_quad("plane4"))
+        first_stage(BB, 1, 1, side_by_side(0, half), cols=left)
+        first_stage(BB, 1, 1, side_by_side(2, P), cols=q3)
+        first_stage(BB, 1, 1, side_by_side(3, P), cols=q4)
+        interleave_h(1, 0, split("scalar", "vector", 320), bf16_quad("words1"))
         quantize_wo(1, "plane1")
+        logit_passes(0, 0, high)
         quantize_h(1, 0)
-        for c in range(OUT_TILES):
-            for b in range(BLOCKS):
-                logit_passes(b, 0, low, tiles=[c])
-        product(1, 1, side_by_side(4, half), left, f32_quad("plane5"))
+        logit_passes(1, 0, high)
+        product(1, 1, side_by_side(0, half), left, f32_quad("plane5"))
         quantize_h(0, 1)
-        interleave_h(1, 1, split("gpsimd", "scalar", P, half), shared_words(10))
-        product(1, 1, side_by_side(6, P), q3)
-        product(1, 1, side_by_side(7, P), q4)
-        logits_out(0, low, ())
-        logit_passes(0, 1, side_by_side(4, half), left, 2)
+        interleave_h(1, 1, split("gpsimd", "scalar", P, half), late_words(3 * W - half))
+        product(1, 1, side_by_side(2, P), q3)
+        product(1, 1, side_by_side(3, P), q4)
+        logits_out(0, high, ())
+        logit_passes(0, 1, side_by_side(0, half), left, 2)
         quantize_h(1, 1, left)
-        logit_passes(1, 1, side_by_side(4, half), left, 2)
-        logit_passes(0, 1, side_by_side(6, P), q3, 4)
-        logit_passes(0, 1, side_by_side(7, P), q4, 4)
+        logit_passes(1, 1, side_by_side(0, half), left, 2)
+        logit_passes(0, 1, side_by_side(2, P), q3, 4)
+        logit_passes(0, 1, side_by_side(3, P), q4, 4)
         interleave_h(1, 1, [("vector", q3)])
         interleave_h(1, 1, [("vector", q4)])
         quantize_h(1, 1, q3)
-        logit_passes(1, 1, side_by_side(6, P), q3, 4)
+        logit_passes(1, 1, side_by_side(2, P), q3, 4)
         quantize_h(1, 1, q4)
-        logit_passes(1, 1, side_by_side(7, P), q4, 4)
-        logits_out(1, side_by_side(4, half), (2, 3), left, 2)
-        logits_out(1, side_by_side(6, P), (), q3, 4)
-        logits_out(1, side_by_side(7, P), (0, 1, 2, 3), q4, 4)
+        logit_passes(1, 1, side_by_side(3, P), q4, 4)
+        logits_out(1, side_by_side(0, half), (2, 3), left, 2)
+        logits_out(1, side_by_side(2, P), (), q3, 4)
+        logits_out(1, side_by_side(3, P), (0, 1, 2, 3), q4, 4)

@@ -209,8 +209,8 @@ def tile_list_hashed_click_logits_kernel(tc, xT, wgt, offs, wa_words, wa_scales,
             woq[b] = mx_operand("woq%d" % b, tag)
             quantize(woq[b], words["wo", b])
 
-        def first_stage(kind, b, h, accs, passes=range(PASSES), cols=ALL):
-            for t in range(PACK):
+        def first_stage(kind, b, h, accs, passes=range(PASSES), cols=ALL, order=range(PACK)):
+            for t in order:
                 for a in passes:
                     if kind == BA:
                         col = a * H + b * W + t * P
@@ -235,10 +235,10 @@ def tile_list_hashed_click_logits_kernel(tc, xT, wgt, offs, wa_words, wa_scales,
                     out=slots(a_view[b, h])[:, t, :], in_=accs[t], func=IDENTITY, bias=bias[:, t, BA + b : BA + b + 1]
                 )
 
-        def product(b, h, accs, cols=ALL, place=None):
+        def product(b, h, accs, cols=ALL, place=None, order=range(PACK)):
             if place is not None:
                 h_rows[b, h] = place
-            for t in range(PACK):
+            for t in order:
                 nc.vector.scalar_tensor_tensor(
                     out=slots(h_rows[b, h])[:, t, cols],
                     in0=accs[t],
@@ -295,7 +295,9 @@ def tile_list_hashed_click_logits_kernel(tc, xT, wgt, offs, wa_words, wa_scales,
             return [(first, slice(0, at)), (second, slice(at, total))]
 
         half = W // 2
-        left, q3, q4 = slice(0, half), slice(half, half + P), slice(half + P, W)
+        left, right = slice(0, half), slice(half, W)
+        q3, q4 = slice(half, half + P), slice(half + P, W)
+        backwards = range(PACK - 1, -1, -1)
         tiles_vector = [("vector", slice(0, PACK))]
         for i in range(PACK):
             for h in range(HALVES):
@@ -330,19 +332,19 @@ def tile_list_hashed_click_logits_kernel(tc, xT, wgt, offs, wa_words, wa_scales,
         round_wb(1, 0, tiles_vector, late_words(0))
         round_wb(0, 1, tiles_vector, late_words(2 * W))
         quantize_wb(1, 0)
-        first_stage(BB, 0, 0, low, range(1, 2))
+        first_stage(BB, 0, 0, low, range(1, 2), order=backwards)
         first_stage(BA, 0, 1, high)
         a_out(0, 1, high)
         quantize_wb(0, 1)
         round_wb(1, 1, split("gpsimd", "scalar", 2, PACK), late_words(2 * W - P))
-        product(0, 0, low, place=bf16_quad("words1"))
+        product(0, 0, low, place=bf16_quad("words1"), order=backwards)
         first_stage(BA, 1, 1, high)
         a_out(1, 1, high)
-        first_stage(BB, 0, 1, low)
+        first_stage(BB, 0, 1, low, order=backwards)
         quantize_wb(1, 1)
         interleave_h(0, 0, split("gpsimd", "scalar", 384), late_words(2 * W))
         round_wo(0, scalar, late_words(0))
-        product(0, 1, low, place=bf16_quad("words2"))
+        product(0, 1, low, place=bf16_quad("words2"), order=backwards)
         first_stage(BB, 1, 0, high)
         quantize_h(0, 0)
         quantize_wo(0, "plane2")
@@ -351,18 +353,16 @@ def tile_list_hashed_click_logits_kernel(tc, xT, wgt, offs, wa_words, wa_scales,
         interleave_h(0, 1, [("scalar", slice(384, W))])
         product(1, 0, high, place=f32_quad("plane4"))
         first_stage(BB, 1, 1, side_by_side(0, half), cols=left)
-        first_stage(BB, 1, 1, side_by_side(2, P), cols=q3)
-        first_stage(BB, 1, 1, side_by_side(3, P), cols=q4)
+        first_stage(BB, 1, 1, side_by_side(2, half), cols=right)
         interleave_h(1, 0, split("scalar", "vector", 320), bf16_quad("words1"))
         quantize_wo(1, "plane1")
         logit_passes(0, 0, high)
         quantize_h(1, 0)
         logit_passes(1, 0, high)
-        product(1, 1, side_by_side(0, half), left, f32_quad("plane5"))
+        product(1, 1, side_by_side(0, half), left, f32_quad("plane5"), backwards)
         quantize_h(0, 1)
         interleave_h(1, 1, split("gpsimd", "scalar", P, half), late_words(3 * W - half))
-        product(1, 1, side_by_side(2, P), q3)
-        product(1, 1, side_by_side(3, P), q4)
+        product(1, 1, side_by_side(2, half), right, order=backwards)
         logits_out(0, high, ())
         logit_passes(0, 1, side_by_side(0, half), left, 2)
         quantize_h(1, 1, left)

@@ -338,17 +338,18 @@ def tile_list_hashed_click_logits_kernel(tc, xT, wgt, offs, wa_words, wa_scales,
         quantize_wb(0, 1)
         round_wb(1, 1, split("gpsimd", "scalar", 2, PACK), late_words(2 * W - P))
         product(0, 0, low, place=bf16_quad("words1"), order=backwards)
-        first_stage(BA, 1, 1, high)
-        a_out(1, 1, high)
         first_stage(BB, 0, 1, low, order=backwards)
-        quantize_wb(1, 1)
-        interleave_h(0, 0, split("gpsimd", "scalar", 384), late_words(2 * W))
-        round_wo(0, scalar, late_words(0))
+        first_stage(BA, 1, 1, high)
+        mid = keep.tile([P, 2 * PACK * W], BF16, name="mid", tag="wb_raw00", align_bytes=64)
+        round_wo(0, scalar, mid[:, 0 : 4 * W])
+        interleave_h(0, 0, split("gpsimd", "scalar", 416), mid[:, 4 * W : 8 * W])
+        a_out(1, 1, high)
         product(0, 1, low, place=bf16_quad("words2"), order=backwards)
+        quantize_wb(1, 1)
         first_stage(BB, 1, 0, high)
         quantize_h(0, 0)
         quantize_wo(0, "plane2")
-        interleave_h(0, 1, [("gpsimd", slice(0, 384))], late_words(W))
+        interleave_h(0, 1, [("gpsimd", slice(0, 384))], mid[:, 2 * W : 6 * W])
         round_wo(1, scalar, bf16_quad("words0"))
         interleave_h(0, 1, [("scalar", slice(384, W))])
         product(1, 0, high, place=f32_quad("plane4"))
@@ -361,7 +362,7 @@ def tile_list_hashed_click_logits_kernel(tc, xT, wgt, offs, wa_words, wa_scales,
         logit_passes(1, 0, high)
         product(1, 1, side_by_side(0, half), left, f32_quad("plane5"), backwards)
         quantize_h(0, 1)
-        interleave_h(1, 1, split("gpsimd", "scalar", P, half), late_words(3 * W - half))
+        interleave_h(1, 1, split("scalar", "gpsimd", P, half), mid[:, W : 5 * W])
         product(1, 1, side_by_side(2, half), right, order=backwards)
         logits_out(0, high, ())
         logit_passes(0, 1, side_by_side(0, half), left, 2)

@@ -248,6 +248,20 @@ def tile_list_hashed_click_logits_kernel(tc, xT, wgt, offs, wa_words, wa_scales,
                     op1=MULT,
                 )
 
+        def b_out(b, h, accs, cols, rows):
+            for t in range(PACK):
+                nc.scalar.activation(
+                    out=slots(rows)[:, t, cols], in_=accs[t], func=IDENTITY, bias=bias[:, t, BB + b : BB + b + 1]
+                )
+
+        def product_in_words(b, h, rows, cols):
+            nc.vector.tensor_tensor(
+                words["h", b, h][:, cols.start * PACK : cols.stop * PACK].rearrange("p (c e t) -> p c t e", e=PACK, t=PACK),
+                slots(a_view[b, h])[:, :, cols].rearrange("p t (c e) -> p c t e", e=PACK),
+                slots(rows)[:, :, cols].rearrange("p t (c e) -> p c t e", e=PACK),
+                MULT,
+            )
+
         def interleave_h(b, h, shares, place=None):
             if ("h", b, h) not in words:
                 words["h", b, h] = place
@@ -356,26 +370,24 @@ def tile_list_hashed_click_logits_kernel(tc, xT, wgt, offs, wa_words, wa_scales,
         first_stage(BB, 1, 1, side_by_side(0, half), cols=left)
         first_stage(BB, 1, 1, side_by_side(2, half), cols=right)
         interleave_h(1, 0, split("scalar", "vector", 320), bf16_quad("words1"))
+        b_rows = f32_quad("plane6")
+        b_out(1, 1, side_by_side(2, half), right, b_rows)
         quantize_wo(1, "plane1")
         logit_passes(0, 0, high)
         quantize_h(1, 0)
         logit_passes(1, 0, high)
         product(1, 1, side_by_side(0, half), left, f32_quad("plane5"), backwards)
         quantize_h(0, 1)
-        interleave_h(1, 1, split("scalar", "gpsimd", P, half), mid[:, W : 5 * W])
-        product(1, 1, side_by_side(2, half), right, order=backwards)
+        interleave_h(1, 1, split("scalar", "vector", P, half), bf16_quad("words0"))
+        product_in_words(1, 1, b_rows, q3)
         logits_out(0, high, ())
         logit_passes(0, 1, side_by_side(0, half), left, 2)
         quantize_h(1, 1, left)
         logit_passes(1, 1, side_by_side(0, half), left, 2)
-        logit_passes(0, 1, side_by_side(2, P), q3, 4)
-        logit_passes(0, 1, side_by_side(3, P), q4, 4)
-        interleave_h(1, 1, [("vector", q3)])
-        interleave_h(1, 1, [("vector", q4)])
+        logit_passes(0, 1, side_by_side(2, half), right, 2)
+        product_in_words(1, 1, b_rows, q4)
         quantize_h(1, 1, q3)
-        logit_passes(1, 1, side_by_side(2, P), q3, 4)
         quantize_h(1, 1, q4)
-        logit_passes(1, 1, side_by_side(3, P), q4, 4)
+        logit_passes(1, 1, side_by_side(2, half), right, 2)
         logits_out(1, side_by_side(0, half), (2, 3), left, 2)
-        logits_out(1, side_by_side(2, P), (), q3, 4)
-        logits_out(1, side_by_side(3, P), (0, 1, 2, 3), q4, 4)
+        logits_out(1, side_by_side(2, half), (2, 3), right, 2)

@@ -21,34 +21,35 @@ IDENTITY = mybir.ActivationFunctionType.Identity
 P = 128
 PACK = 4
 W = 512
+HALF = W // 2
+GROUPS = 8
 PASSES = K // W
 BLOCKS = H // W
 HALVES = S // W
 OUT_TILES = N // P
-BA, BB, BO = 0, 2, 4
-WGT0_AT = 2 * W
+BA, BB, BO = 0, 2, 32
 ALL = slice(0, W)
+LEFT, RIGHT = slice(0, HALF), slice(HALF, W)
+QUAD = PACK * W * 4
+ROW = W * 4
+WGT_AT, WGT_STEP = 2 * W + HALF, W + HALF
 
 
 def tile_list_hashed_click_logits_kernel(tc, xT, wgt, offs, wa_words, wa_scales, ba, wb, bb, wo, bo, out):
     nc = tc.nc
     with ExitStack() as ctx:
         keep = ctx.enter_context(tc.tile_pool(name="keep", bufs=1))
+        arena = ctx.enter_context(tc.tile_pool(name="arena", bufs=1))
         psum = ctx.enter_context(tc.psum_pool(name="psum", bufs=1))
 
-        def f32_quad(tag):
-            return keep.tile([P, PACK * W], F32, name=tag, tag=tag, align_bytes=64)
+        def placed(name, cols, dtype, at):
+            return arena.tile([P, cols], dtype, name=name, offset=at, align_bytes=64)
 
-        def slots(quad):
-            return quad[:, :].rearrange("p (t c) -> p t c", t=PACK)
+        def quad(name, n):
+            return placed(name, PACK * W, F32, n * QUAD)
 
-        def bf16_quad(tag):
-            return keep.tile([P, PACK * W], BF16, name=tag, tag=tag, align_bytes=64)
-
-        def mx_operand(name, tag=None):
-            codes = keep.tile([P, W], U32, name=name + "_codes", tag=tag or name + "_codes", align_bytes=64)
-            scales = keep.tile([P, W], U8, name=name + "_scales", align_bytes=64)
-            return codes, scales
+        def slots(rows):
+            return rows[:, :].rearrange("p (t c) -> p t c", t=PACK)
 
         def copy_on(engine, dst, src):
             if engine == "vector":
@@ -58,158 +59,163 @@ def tile_list_hashed_click_logits_kernel(tc, xT, wgt, offs, wa_words, wa_scales,
             else:
                 nc.gpsimd.tensor_scalar(out=dst, in0=src, scalar1=1.0, scalar2=0.0, op0=MULT, op1=ADD)
 
-        def interleave(words, quad, shares):
-            for engine, cols in shares:
-                dst, src = words[:, cols.start * PACK : cols.stop * PACK], slots(quad)[:, :, cols]
-                if engine == "gpsimd":
-                    copy_on(engine, dst.rearrange("p (c t) -> p c t", t=PACK), src.rearrange("p t c -> p c t"))
-                else:
-                    copy_on(
-                        engine,
-                        dst.rearrange("p (c e t) -> p c t e", e=PACK, t=PACK),
-                        src.rearrange("p t (c e) -> p c t e", e=PACK),
-                    )
-
-        def quantize(operand, words, cols=ALL):
-            codes, scales = operand
-            nc.vector.quantize_mx(
-                out=codes[:, cols].bitcast(FP8X4), scales=scales[:, cols], in_=words[:, cols.start * PACK : cols.stop * PACK]
-            )
+        def interleave(engine, words, rows, cols=ALL):
+            dst, src = words[:, cols.start * PACK : cols.stop * PACK], slots(rows)[:, :, cols]
+            if engine == "gpsimd":
+                copy_on(engine, dst.rearrange("p (c t) -> p c t", t=PACK), src.rearrange("p t c -> p c t"))
+            else:
+                copy_on(
+                    engine,
+                    dst.rearrange("p (c e t) -> p c t e", e=PACK, t=PACK),
+                    src.rearrange("p t (c e) -> p c t e", e=PACK),
+                )
 
         banks = [psum.tile([P, W], F32, name="bank%d" % n) for n in range(8)]
+        low, high = [bank[:] for bank in banks[0:4]], [bank[:] for bank in banks[4:8]]
 
         offsets = keep.tile([P, S // 16], U16, name="offsets")
-        planes = [f32_quad("plane%d" % n) for n in range(PASSES * PACK)]
-        picked = {(a, h): f32_quad("picked%d%d" % (a, h)) for a, h in ((0, 0), (0, 1), (1, 0))}
-        late = keep.tile([P, (PACK + 1) * W], F32, name="late", align_bytes=64)
-        picked[1, 1] = late[:, 0 : PACK * W]
-        wgt1 = keep.tile([P, W], F32, name="wgt1")
-        weights = [late[:, WGT0_AT : WGT0_AT + W], wgt1[:]]
-        wa_raw = keep.tile([P, PASSES * 2 * H], U8, name="wa_raw")
-        wa_scale_raw = keep.tile([P, PASSES * H], U8, name="wa_scale_raw")
-        wa_codes = keep.tile([P, PASSES * 2 * H], U8, name="wa_codes", align_bytes=64)
-        wa_scale = keep.tile([P, PASSES * H], U8, name="wa_scale", align_bytes=64)
-        bias_raw = keep.tile([4, W], F32, name="bias_raw")
-        bias_rows = keep.tile([P, W], F32, name="bias_rows")
+        planes = [quad("plane%d" % n, n) for n in range(PASSES * PACK)]
+        picked = {(a, h): quad("picked%d%d" % (a, h), 8 + 2 * a + h) for a, h in ((0, 0), (0, 1), (1, 0))}
+        last_picked = placed("last_picked", WGT_AT + 2 * WGT_STEP, F32, 15 * QUAD)
+        picked[1, 1] = last_picked[:, 0 : PACK * W]
+        wb_raw = placed("wb_raw", PACK * PACK * W, F32, 11 * QUAD)
+        all_words = keep.tile([P, 65 * HALF], BF16, name="all_words", align_bytes=64)
+
+        def words_at(start):
+            return all_words[:, start * HALF : start * HALF + PACK * W]
+
+        words = {
+            ("x", 0, 0): words_at(40),
+            ("x", 0, 1): words_at(48),
+            ("wb", 0, 0): words_at(8),
+            ("x", 1, 0): words_at(6),
+            ("x", 1, 1): words_at(0),
+            ("wb", 1, 0): words_at(16),
+            ("wb", 0, 1): words_at(24),
+            ("wb", 1, 1): words_at(32),
+            ("wo", 0): words_at(28),
+            ("wo", 1): words_at(48),
+            ("h", 0, 0): words_at(56),
+            ("h", 1, 0): words_at(52),
+            ("h", 0, 1): words_at(57),
+            ("h", 1, 1): words_at(0),
+        }
+        wb_words = all_words[:, PACK * W : (PACK + 1) * PACK * W]
+        wgt_halves = last_picked[:, WGT_AT:].rearrange("p (h c) -> p h c", h=HALVES)
+        weights = [wgt_halves[:, h, 0:W] for h in range(HALVES)]
+        wgt_rows = keep.tile([P, 64], F32, name="wgt_rows", align_bytes=64)
+        wgt_turned = keep.tile([P, 64], F32, name="wgt_turned", align_bytes=64)
+        wgt_spread = keep.tile([P, S], F32, name="wgt_spread", align_bytes=64)
+        wa_raw = keep.tile([P, PASSES * H // 2], I32, name="wa_raw")
+        wa_scale_raw = keep.tile([P, PASSES * H // 4], I32, name="wa_scale_raw")
+        bias_raw = keep.tile([BO + OUT_TILES, W], F32, name="bias_raw")
+        bias_rows = picked[0, 0][:, 0:W]
         identity = keep.tile([P, P], F32, name="identity")
-        bias = keep.tile([P, PACK, 8], F32, name="bias")
+        bias = keep.tile([P, PACK, BO + OUT_TILES], F32, name="bias")
 
         def load_plane(a, i):
             rows = xT[a * W : (a + 1) * W, :].rearrange("(p i) t -> i p t", i=PACK)
             nc.sync.dma_start(out=planes[a * PACK + i][:], in_=rows[i])
 
-        wb_raw = {(a, b): f32_quad("wb_raw%d%d" % (a, b)) for a in range(PASSES) for b in range(BLOCKS)}
-        wo_raw = {b: f32_quad("wo_raw%d" % b) for b in range(BLOCKS)}
-
-        def late_words(start):
-            return late[:, start : start + 2 * W].bitcast(BF16)
-
-        def load_wb(a, b):
-            nc.sync.dma_start(
-                out=slots(wb_raw[a, b]),
-                in_=wb[a * W : (a + 1) * W, b * W : (b + 1) * W].rearrange("(p j) r -> p j r", j=PACK),
-            )
-
-        def load_wo(b):
-            rows = wo[b * W : (b + 1) * W, :].rearrange("(g t i) n -> t g i n", t=PACK, i=PACK)
-            for t in range(PACK):
-                nc.sync.dma_start(out=slots(wo_raw[b])[:, t, :], in_=rows[t])
-
-        nc.gpsimd.memset(wa_scale_raw[:].bitcast(I32), 0)
-        nc.gpsimd.memset(bias_rows[:], 0.0)
-        make_identity(nc, identity[:])
-
         def load_wa_scales(r):
             nc.sync.dma_start(
-                out=wa_scale_raw[r:P:32, :].bitcast(I32).rearrange("p (a n) -> p a n", a=PASSES),
+                out=wa_scale_raw[r:P:32, :].rearrange("p (a n) -> p a n", a=PASSES),
                 in_=wa_scales.bitcast(I32)[:, r:16:4, :].rearrange("a q n -> q a n"),
             )
 
-        load_plane(0, 0)
-        nc.sync.dma_start(out=weights[0], in_=wgt[:, 0:W])
+        make_identity(nc, identity[:])
+        nc.gpsimd.memset(wa_scale_raw[:], 0)
+
+        nc.sync.dma_start(out=wgt_rows[:], in_=wgt[0:P:16, :].rearrange("g (u j) -> g u j", j=64))
         nc.sync.dma_start(offsets[:], offs)
-        nc.sync.dma_start(out=weights[1], in_=wgt[:, W : 2 * W])
-        for i in range(1, PACK):
+        for i in range(PACK):
             load_plane(0, i)
         load_plane(1, 0)
         nc.sync.dma_start(out=bias_raw[BA : BA + BLOCKS, :], in_=ba.rearrange("(b r) -> b r", b=BLOCKS))
         nc.sync.dma_start(out=bias_raw[BB : BB + BLOCKS, :], in_=bb.rearrange("(b r) -> b r", b=BLOCKS))
         load_plane(1, 1)
-        nc.sync.dma_start(out=bias_rows[BO : BO + OUT_TILES, 0:P], in_=bo.rearrange("(c p) -> c p", p=P))
+        nc.sync.dma_start(out=bias_raw[BO : BO + OUT_TILES, 0:P], in_=bo.rearrange("(c p) -> c p", p=P))
         load_wa_scales(0)
         load_wa_scales(1)
-        nc.sync.dma_start(
-            out=wa_raw[:].bitcast(I32).rearrange("p (a n) -> p a n", a=PASSES),
-            in_=wa_words.bitcast(I32).rearrange("a p n -> p a n"),
-        )
+        load_plane(1, 2)
         load_wa_scales(2)
         load_wa_scales(3)
-        load_plane(1, 2)
+        nc.sync.dma_start(
+            out=wa_raw[:].rearrange("p (a n) -> p a n", a=PASSES),
+            in_=wa_words.bitcast(I32).rearrange("a p n -> p a n"),
+        )
         load_plane(1, 3)
         for b in range(BLOCKS):
             for a in range(PASSES):
-                load_wb(a, b)
-        for b in range(BLOCKS):
-            load_wo(b)
+                nc.sync.dma_start(
+                    out=slots(wb_raw[:, (2 * b + a) * PACK * W : (2 * b + a + 1) * PACK * W]),
+                    in_=wb[a * W : (a + 1) * W, b * W : (b + 1) * W].rearrange("(p j) r -> p j r", j=PACK),
+                )
 
-        nc.scalar.copy(
-            out=bias_rows[0:4, :].rearrange("p (t g i) -> p t g i", t=PACK, i=PACK),
-            in_=bias_raw[:].rearrange("p (g t i) -> p t g i", t=PACK, i=PACK),
-        )
-        for t in range(PACK):
-            nc.tensor.transpose(banks[0][:, t * P : (t + 1) * P], bias_rows[:, t * P : (t + 1) * P], identity[:])
-        nc.scalar.activation(out=bias[:], in_=banks[0][:].rearrange("p (t c) -> p t c", t=PACK)[:, :, 0:8], func=IDENTITY)
-
-        xq, wbq, woq, hq, words, a_view, h_rows, results = {}, {}, {}, {}, {}, {}, {}, {}
-
-        def gather(a, i, h):
-            window = planes[a * PACK + i][:].indirect(offsets[:, h * (W // 16) : (h + 1) * (W // 16)])
-            nc.vector.tensor_tensor(picked[a, h][:, i * W : (i + 1) * W], window, weights[h], MULT)
-
-        def round_x(a, h, shares, place):
-            words["x", a, h] = place
-            interleave(words["x", a, h], picked[a, h], shares)
-
-        def quantize_x(a, h):
-            xq[a, h] = mx_operand("xq%d%d" % (a, h))
-            quantize(xq[a, h], words["x", a, h])
-
-        def permute_wa_codes():
+        for low_bit in range(2):
+            part = slice(32 * low_bit, 32 * low_bit + 32)
+            nc.vector.transpose(wgt_turned[:, part], wgt_rows[:, part])
+        for h in range(HALVES):
+            by_group = wgt_turned[:].rearrange("y (b g u) -> y u b g", b=2, g=2)[:, 8 * h : 8 * h + 8]
             nc.vector.tensor_copy(
-                out=wa_codes[:].bitcast(I32).rearrange("p (c t g e) -> p c g t e", t=PACK, g=32, e=2),
-                in_=wa_raw[:].bitcast(I32).rearrange("p (c g t e) -> p c g t e", t=PACK, g=32, e=2),
+                out=wgt_spread[:, h * W : (h + 1) * W].rearrange("y (u b g q) -> y u b g q", b=2, g=2, q=16),
+                in_=by_group.unsqueeze(4).to_broadcast([P, 8, 2, 2, 16]),
+            )
+        for h in range(HALVES):
+            nc.vector.transpose(weights[h], wgt_spread[:, h * W : (h + 1) * W])
+
+        xq, wbq, woq, hq, a_view, h_rows = {}, {}, {}, {}, {}, {}
+
+        def gather(a, i, h, cols=ALL):
+            first = (h * W + cols.start) // 16
+            window = planes[a * PACK + i][:].indirect(offsets[:, first : first + (cols.stop - cols.start) // 16])
+            nc.vector.tensor_tensor(slots(picked[a, h])[:, i, cols], window, weights[h][:, cols], MULT)
+
+        def operand(name, scales_at=None, codes_at=None):
+            if codes_at is None:
+                codes = keep.tile([P, W], U32, name=name + "_codes", align_bytes=64)
+            else:
+                codes = placed(name + "_codes", W, U32, codes_at)
+            if scales_at is None:
+                return codes, keep.tile([P, W], U8, name=name + "_scales", align_bytes=64)
+            return codes, placed(name + "_scales", W, U8, scales_at)
+
+        def quantize(target, key, cols=ALL):
+            codes, scales = target
+            nc.vector.quantize_mx(
+                out=codes[:, cols].bitcast(FP8X4), scales=scales[:, cols], in_=words[key][:, cols.start * PACK : cols.stop * PACK]
             )
 
-        def permute_wa_scales():
-            nc.vector.tensor_copy(
-                out=wa_scale[:].bitcast(I32).rearrange("p (c t g e) -> p c g t e", t=PACK, g=8, e=4),
-                in_=wa_scale_raw[:].bitcast(I32).rearrange("p (c g e t) -> p c g t e", t=PACK, g=8, e=4),
+        def order_wa_codes(a):
+            part = slice(a * W, (a + 1) * W)
+            nc.scalar.copy(
+                out=wa_codes[:].bitcast(U32)[:, part].rearrange("p (c t g e) -> p c t g e", t=PACK, g=32, e=2),
+                in_=wa_raw[:].bitcast(U32)[:, part].rearrange("p (c g t e) -> p c t g e", t=PACK, g=32, e=2),
             )
 
-        def round_wb(a, b, shares, place):
-            words["wb", a, b] = place
-            dst = words["wb", a, b][:].rearrange("p (t g i j) -> p t g j i", t=PACK, i=PACK, j=PACK)
-            src = wb_raw[a, b][:].rearrange("p (j g t i) -> p t g j i", j=PACK, t=PACK, i=PACK)
-            for engine, tiles in shares:
-                if engine == "gpsimd":
-                    for t in range(tiles.start, tiles.stop):
-                        copy_on(engine, dst[:, t].rearrange("p g j i -> p g i j"), src[:, t].rearrange("p g j i -> p g i j"))
-                else:
-                    copy_on(engine, dst[:, tiles], src[:, tiles])
+        def order_wa_scales():
+            nc.scalar.copy(
+                out=wa_scale[:].bitcast(U32).rearrange("p (c t g e) -> p c g t e", t=PACK, g=8, e=4),
+                in_=wa_scale_raw[:].bitcast(U32).rearrange("p (c g e t) -> p c g t e", t=PACK, g=8, e=4),
+            )
 
-        def quantize_wb(a, b, tag=None):
-            wbq[a, b] = mx_operand("wbq%d%d" % (a, b), tag)
-            quantize(wbq[a, b], words["wb", a, b])
+        def round_wb(quarter, tiles):
+            dst = wb_words.rearrange("p (n t g i j) -> p n g t j i", n=PACK, t=PACK, i=PACK, j=PACK)
+            src = wb_raw[:].rearrange("p (n j g t i) -> p n g t j i", n=PACK, j=PACK, t=PACK, i=PACK)
+            nc.vector.tensor_copy(out=dst[:, quarter, :, tiles], in_=src[:, quarter, :, tiles])
 
-        def round_wo(b, shares, place):
-            words["wo", b] = place
-            interleave(words["wo", b], wo_raw[b], shares)
+        def round_wb_seam(quarter):
+            dst = wb_words[:, quarter * PACK * W + 3 * W : (quarter + 1) * PACK * W + W]
+            reach = PACK * W - 3 * PACK
+            first = quarter * PACK * W + 3 * PACK
+            src = wb_raw[:, first : first + 2 * reach].rearrange("p (n x) -> p n x", n=2)
+            src = src.rearrange("p n (y i) -> p n y i", i=PACK)
+            nc.vector.tensor_copy(
+                out=dst.rearrange("p (n g i j) -> p n g j i", n=2, i=PACK, j=PACK),
+                in_=src[:, :, 0:509:4, :].rearrange("p n (j g) i -> p n g j i", j=PACK),
+            )
 
-        def quantize_wo(b, tag=None):
-            woq[b] = mx_operand("woq%d" % b, tag)
-            quantize(woq[b], words["wo", b])
-
-        def first_stage(kind, b, h, accs, passes=range(PASSES), cols=ALL, order=range(PACK)):
+        def first_stage(kind, b, h, accs, passes=range(PASSES), order=range(PACK)):
             for t in order:
                 for a in passes:
                     if kind == BA:
@@ -222,57 +228,42 @@ def tile_list_hashed_click_logits_kernel(tc, xT, wgt, offs, wa_words, wa_scales,
                         out=accs[t],
                         lhsT=codes,
                         lhsT_scale=scales,
-                        rhs=xq[a, h][0][:, cols].bitcast(FP8X4),
-                        rhs_scale=xq[a, h][1][:, cols],
+                        rhs=xq[a, h][0][:].bitcast(FP8X4),
+                        rhs_scale=xq[a, h][1][:],
                         start=(a == 0),
                         stop=(a == PASSES - 1),
                     )
 
-        def a_out(b, h, accs):
-            a_view[b, h] = f32_quad("plane%d" % (2 * h + b))
-            for t in range(PACK):
-                nc.scalar.activation(
-                    out=slots(a_view[b, h])[:, t, :], in_=accs[t], func=IDENTITY, bias=bias[:, t, BA + b : BA + b + 1]
-                )
+        def a_at(b, h, t):
+            return (2 + 2 * h + b) * QUAD + t * ROW
 
-        def product(b, h, accs, cols=ALL, place=None, order=range(PACK)):
-            if place is not None:
-                h_rows[b, h] = place
+        def a_out(b, h, accs):
+            if (b, h) == (1, 1):
+                whole = placed("a11", PACK * W, F32, a_at(b, h, 0))
+                a_view[b, h] = [slots(whole)[:, t, :] for t in range(PACK)]
+                a_view["whole"] = whole
+            else:
+                a_view[b, h] = [placed("a%d%d_%d" % (b, h, t), W, F32, a_at(b, h, t))[:] for t in range(PACK)]
+            for t in range(PACK):
+                nc.scalar.activation(out=a_view[b, h][t], in_=accs[t], func=IDENTITY, bias=bias[:, t, BA + b : BA + b + 1])
+
+        def product(b, h, accs, rows, cols=ALL, order=range(PACK)):
+            h_rows[b, h] = rows
             for t in order:
                 nc.vector.scalar_tensor_tensor(
-                    out=slots(h_rows[b, h])[:, t, cols],
-                    in0=accs[t],
+                    out=slots(rows)[:, t, cols],
+                    in0=accs[t][:, cols],
                     scalar=bias[:, t, BB + b : BB + b + 1],
-                    in1=slots(a_view[b, h])[:, t, cols],
+                    in1=a_view[b, h][t][:, cols],
                     op0=ADD,
                     op1=MULT,
                 )
 
-        def b_out(b, h, accs, cols, rows):
-            for t in range(PACK):
-                nc.scalar.activation(
-                    out=slots(rows)[:, t, cols], in_=accs[t], func=IDENTITY, bias=bias[:, t, BB + b : BB + b + 1]
-                )
+        def interleave_h(engine, b, h, cols):
+            interleave(engine, words["h", b, h], h_rows[b, h], cols)
 
-        def product_in_words(b, h, rows, cols):
-            nc.vector.tensor_tensor(
-                words["h", b, h][:, cols.start * PACK : cols.stop * PACK].rearrange("p (c e t) -> p c t e", e=PACK, t=PACK),
-                slots(a_view[b, h])[:, :, cols].rearrange("p t (c e) -> p c t e", e=PACK),
-                slots(rows)[:, :, cols].rearrange("p t (c e) -> p c t e", e=PACK),
-                MULT,
-            )
-
-        def interleave_h(b, h, shares, place=None):
-            if ("h", b, h) not in words:
-                words["h", b, h] = place
-                hq[b, h] = mx_operand("hq%d%d" % (b, h))
-            interleave(words["h", b, h], h_rows[b, h], shares)
-
-        def quantize_h(b, h, cols=ALL):
-            quantize(hq[b, h], words["h", b, h], cols)
-
-        def logit_passes(b, h, accs, cols=ALL, per_bank=1, tiles=range(OUT_TILES)):
-            for c in tiles:
+        def logit_passes(b, h, accs, cols=ALL, per_bank=1):
+            for c in range(OUT_TILES):
                 nc.tensor.matmul_mx(
                     out=accs[c],
                     lhsT=woq[b][0][:, c * P : (c + 1) * P].bitcast(FP8X4),
@@ -283,111 +274,139 @@ def tile_list_hashed_click_logits_kernel(tc, xT, wgt, offs, wa_words, wa_scales,
                     stop=(b == BLOCKS - 1 and c % per_bank == per_bank - 1),
                 )
 
-        def logits_out(h, accs, on_vector, cols=ALL, per_store=1):
-            if h not in results:
-                results[h] = f32_quad("picked0%d" % h)
+        def logits_out(h, accs, result_rows, on_vector, cols=ALL, per_store=1, tiles=range(OUT_TILES)):
             rows = out[:, h * W + cols.start : h * W + cols.stop].rearrange("(c p) j -> p c j", p=P)
-            for c in range(OUT_TILES):
-                result = slots(results[h])[:, c, cols]
+            for c in tiles:
+                result = slots(result_rows)[:, c, cols]
                 bo_col = bias[:, 0, BO + c : BO + c + 1]
                 if c in on_vector:
                     nc.vector.tensor_scalar(out=result, in0=accs[c], scalar1=bo_col, scalar2=None, op0=ADD)
                 else:
                     nc.scalar.activation(out=result, in_=accs[c], func=IDENTITY, bias=bo_col)
                 if (c + 1) % per_store == 0:
-                    tiles = slice(c + 1 - per_store, c + 1)
-                    nc.sync.dma_start(out=rows[:, tiles, :], in_=slots(results[h])[:, tiles, cols])
+                    done = slice(c + 1 - per_store, c + 1)
+                    nc.sync.dma_start(out=rows[:, done, :], in_=slots(result_rows)[:, done, cols])
 
-        def side_by_side(first_bank, width):
-            per_bank = W // width
-            return [banks[first_bank + n // per_bank][:, (n % per_bank) * width : (n % per_bank + 1) * width] for n in range(4)]
+        def two_to_a_bank(first_bank):
+            return [banks[first_bank + n // 2][:, (n % 2) * HALF : (n % 2 + 1) * HALF] for n in range(4)]
 
-        low, high = side_by_side(0, W), side_by_side(4, W)
-        scalar, vector = [("scalar", ALL)], [("vector", ALL)]
-
-        def split(first, second, at, total=W):
-            return [(first, slice(0, at)), (second, slice(at, total))]
-
-        half = W // 2
-        left, right = slice(0, half), slice(half, W)
-        q3, q4 = slice(half, half + P), slice(half + P, W)
         backwards = range(PACK - 1, -1, -1)
-        tiles_vector = [("vector", slice(0, PACK))]
         for i in range(PACK):
             for h in range(HALVES):
                 gather(0, i, h)
-        round_x(0, 0, scalar, bf16_quad("words0"))
-        round_x(0, 1, scalar, bf16_quad("words1"))
-        gather(1, 0, 0)
-        gather(1, 0, 1)
-        quantize_x(0, 0)
-        gather(1, 1, 0)
-        gather(1, 1, 1)
-        quantize_x(0, 1)
-        permute_wa_scales()
-        permute_wa_codes()
+        wo_raw = {b: quad("wo_raw%d" % b, b) for b in range(BLOCKS)}
+        for b in range(BLOCKS):
+            wo_rows = wo[b * W : (b + 1) * W, :].rearrange("(g t i) n -> t g i n", t=PACK, i=PACK)
+            for t in range(PACK):
+                nc.sync.dma_start(out=slots(wo_raw[b])[:, t, :], in_=wo_rows[t])
+        for h in range(HALVES):
+            interleave("scalar", words["x", 0, h], picked[0, h])
+        nc.scalar.copy(
+            out=bias_rows[0:4, :].rearrange("p (t g i) -> p t g i", t=PACK, i=PACK),
+            in_=bias_raw[0:4, :].rearrange("p (g t i) -> p t g i", t=PACK, i=PACK),
+        )
+        nc.scalar.copy(out=bias_rows[BO : BO + OUT_TILES, 0:P], in_=bias_raw[BO : BO + OUT_TILES, 0:P])
+        for t in range(PACK):
+            nc.tensor.transpose(banks[0][:, t * P : (t + 1) * P], bias_rows[:, t * P : (t + 1) * P], identity[:])
+        nc.scalar.activation(out=bias[:], in_=banks[0][:].rearrange("p (t c) -> p t c", t=PACK)[:, :, 0 : BO + OUT_TILES], func=IDENTITY)
+        wa_codes = placed("wa_codes", PASSES * 2 * H, U8, 9 * QUAD)
+        wa_scale = placed("wa_scale", PASSES * H, U8, 9 * QUAD + 2 * ROW)
+        for i in range(2):
+            gather(1, i, 0)
+            gather(1, i, 1)
+            xq[0, i] = operand("xq0%d" % i)
+            quantize(xq[0, i], ("x", 0, i))
+        order_wa_scales()
+        order_wa_codes(0)
+        order_wa_codes(1)
         gather(1, 2, 0)
+        gather(1, 2, 1, LEFT)
         first_stage(BA, 0, 0, low, range(0, 1))
         first_stage(BA, 1, 0, high, range(0, 1))
-        gather(1, 3, 0)
-        round_x(1, 0, split("scalar", "vector", 352), late_words(3 * W))
-        gather(1, 2, 1)
-        quantize_x(1, 0)
-        round_wb(0, 0, split("scalar", "vector", 2, PACK), bf16_quad("words2"))
+        gather(1, 3, 0, LEFT)
+        gather(1, 3, 0, RIGHT)
+        gather(1, 2, 1, RIGHT)
         gather(1, 3, 1)
+        interleave("scalar", words["x", 1, 0], picked[1, 0], slice(0, 240))
+        interleave("scalar", words["x", 1, 0], picked[1, 0], slice(240, W))
+        interleave("scalar", words["x", 1, 1], picked[1, 1], LEFT)
+        xq[1, 0], xq[1, 1] = operand("xq10"), operand("xq11")
+        quantize(xq[1, 0], ("x", 1, 0), LEFT)
+        quantize(xq[1, 0], ("x", 1, 0), RIGHT)
         first_stage(BA, 0, 0, low, range(1, 2))
-        a_out(0, 0, low)
         first_stage(BA, 1, 0, high, range(1, 2))
+        a_out(0, 0, low)
         a_out(1, 0, high)
-        quantize_wb(0, 0)
-        first_stage(BB, 0, 0, low, range(0, 1))
-        round_x(1, 1, vector, bf16_quad("words0"))
-        quantize_x(1, 1)
-        round_wb(1, 0, tiles_vector, late_words(0))
-        round_wb(0, 1, tiles_vector, late_words(2 * W))
-        quantize_wb(1, 0)
-        first_stage(BB, 0, 0, low, range(1, 2), order=backwards)
-        first_stage(BA, 0, 1, high)
-        a_out(0, 1, high)
-        quantize_wb(0, 1)
-        round_wb(1, 1, split("gpsimd", "scalar", 2, PACK), late_words(2 * W - P))
-        product(0, 0, low, place=bf16_quad("words1"), order=backwards)
-        first_stage(BB, 0, 1, low, order=backwards)
+        for a in range(PASSES):
+            for b in range(BLOCKS):
+                wbq[a, b] = operand("wbq%d%d" % (a, b))
+        interleave("vector", words["x", 1, 1], picked[1, 1], RIGHT)
+        round_wb(0, slice(0, 3))
+        quantize(xq[1, 1], ("x", 1, 1))
+        round_wb_seam(0)
+        round_wb(1, slice(1, 3))
+        quantize(wbq[0, 0], ("wb", 0, 0))
+        round_wb_seam(1)
+        round_wb(2, slice(1, 3))
+        quantize(wbq[1, 0], ("wb", 1, 0))
+        round_wb_seam(2)
+        round_wb(3, slice(1, 4))
+        quantize(wbq[0, 1], ("wb", 0, 1))
+        quantize(wbq[1, 1], ("wb", 1, 1))
+        first_stage(BA, 0, 1, low)
+        a_out(0, 1, low)
         first_stage(BA, 1, 1, high)
-        mid = keep.tile([P, 2 * PACK * W], BF16, name="mid", tag="wb_raw00", align_bytes=64)
-        round_wo(0, scalar, mid[:, 0 : 4 * W])
-        interleave_h(0, 0, split("gpsimd", "scalar", 416), mid[:, 4 * W : 8 * W])
         a_out(1, 1, high)
-        product(0, 1, low, place=bf16_quad("words2"), order=backwards)
-        quantize_wb(1, 1)
+        first_stage(BB, 0, 0, low)
         first_stage(BB, 1, 0, high)
-        quantize_h(0, 0)
-        quantize_wo(0, "plane2")
-        interleave_h(0, 1, [("gpsimd", slice(0, 384))], mid[:, 2 * W : 6 * W])
-        round_wo(1, scalar, bf16_quad("words0"))
-        interleave_h(0, 1, [("scalar", slice(384, W))])
-        product(1, 0, high, place=f32_quad("plane4"))
-        first_stage(BB, 1, 1, side_by_side(0, half), cols=left)
-        first_stage(BB, 1, 1, side_by_side(2, half), cols=right)
-        interleave_h(1, 0, split("scalar", "vector", 320), bf16_quad("words1"))
-        b_rows = f32_quad("plane6")
-        b_out(1, 1, side_by_side(2, half), right, b_rows)
-        quantize_wo(1, "plane1")
-        logit_passes(0, 0, high)
-        quantize_h(1, 0)
-        logit_passes(1, 0, high)
-        product(1, 1, side_by_side(0, half), left, f32_quad("plane5"), backwards)
-        quantize_h(0, 1)
-        interleave_h(1, 1, split("scalar", "vector", P, half), bf16_quad("words0"))
-        product_in_words(1, 1, b_rows, q3)
-        logits_out(0, high, ())
-        logit_passes(0, 1, side_by_side(0, half), left, 2)
-        quantize_h(1, 1, left)
-        logit_passes(1, 1, side_by_side(0, half), left, 2)
-        logit_passes(0, 1, side_by_side(2, half), right, 2)
-        product_in_words(1, 1, b_rows, q4)
-        quantize_h(1, 1, q3)
-        quantize_h(1, 1, q4)
-        logit_passes(1, 1, side_by_side(2, half), right, 2)
-        logits_out(1, side_by_side(0, half), (2, 3), left, 2)
-        logits_out(1, side_by_side(2, half), (2, 3), right, 2)
+        interleave("gpsimd", words["wo", 0], wo_raw[0], slice(0, 416))
+        interleave("scalar", words["wo", 0], wo_raw[0], slice(416, W))
+        interleave("scalar", words["wo", 1], wo_raw[1])
+        product(0, 0, low, placed("h_rows00", PACK * W, BF16, 6 * QUAD))
+        first_stage(BB, 0, 1, low)
+        interleave_h("gpsimd", 0, 0, slice(0, 416))
+        interleave_h("scalar", 0, 0, slice(416, W))
+        product(1, 0, high, placed("h_rows10", PACK * W, BF16, 6 * QUAD + 2 * ROW))
+        first_stage(BB, 1, 1, high)
+        woq[0] = operand("woq0", a_at(1, 0, 2))
+        woq[1] = operand("woq1", a_at(1, 0, 3))
+        hq[0, 0] = operand("hq00", a_at(1, 0, 3) + W)
+        quantize(woq[0], ("wo", 0))
+        quantize(woq[1], ("wo", 1))
+        quantize(hq[0, 0], ("h", 0, 0))
+        interleave_h("gpsimd", 1, 0, slice(0, 416))
+        interleave_h("scalar", 1, 0, slice(416, W))
+        product(0, 1, low, words_at(44), order=backwards)
+        b_rows = placed("b_rows", PACK * W, F32, 10 * QUAD)
+        for t in range(PACK):
+            nc.scalar.activation(
+                out=slots(b_rows)[:, t, RIGHT], in_=high[t][:, RIGHT], func=IDENTITY, bias=bias[:, t, BB + 1 : BB + 2]
+            )
+        logit_passes(0, 0, low)
+        hq[1, 0] = operand("hq10", a_at(0, 1, 1), 7 * QUAD + 2 * ROW)
+        quantize(hq[1, 0], ("h", 1, 0))
+        logit_passes(1, 0, low)
+        interleave_h("gpsimd", 0, 1, slice(0, 192))
+        interleave_h("scalar", 0, 1, slice(192, W))
+        product(1, 1, high, placed("h_rows11", PACK * W, BF16, 7 * QUAD), LEFT)
+        hq[0, 1], hq[1, 1] = operand("hq01"), operand("hq11")
+        quantize(hq[0, 1], ("h", 0, 1))
+        nc.vector.tensor_tensor(
+            words["h", 1, 1][:, HALF * PACK : W * PACK].rearrange("p (c e t) -> p c t e", e=PACK, t=PACK),
+            slots(a_view["whole"])[:, :, RIGHT].rearrange("p t (c e) -> p c t e", e=PACK),
+            slots(b_rows)[:, :, RIGHT].rearrange("p t (c e) -> p c t e", e=PACK),
+            MULT,
+        )
+        results = [quad("results%d" % h, 8 + h) for h in range(HALVES)]
+        logits_out(0, low, results[0], (), tiles=range(0, 2))
+        words["h left"] = placed("h11_left", PACK * HALF, BF16, 7 * QUAD + 2 * ROW)[:]
+        interleave("scalar", words["h left"], h_rows[1, 1], LEFT)
+        logits_out(0, low, results[0], (), tiles=range(2, 4))
+        logit_passes(0, 1, two_to_a_bank(6), RIGHT, 2)
+        logit_passes(0, 1, two_to_a_bank(4), LEFT, 2)
+        quantize(hq[1, 1], ("h", 1, 1), RIGHT)
+        logit_passes(1, 1, two_to_a_bank(6), RIGHT, 2)
+        quantize(hq[1, 1], "h left", LEFT)
+        logit_passes(1, 1, two_to_a_bank(4), LEFT, 2)
+        logits_out(1, two_to_a_bank(6), results[1], (0, 1), RIGHT, 2)
+        logits_out(1, two_to_a_bank(4), results[1], (0, 1), LEFT, 2)

@@ -317,8 +317,8 @@ def tile_list_hashed_click_logits_kernel(tc, xT, wgt, offs, wa_words, wa_scales,
             xq[0, i] = operand("xq0%d" % i)
             quantize(xq[0, i], ("x", 0, i))
         order_wa_scales()
-        order_wa_codes(0)
         order_wa_codes(1)
+        order_wa_codes(0)
         gather(1, 2, 0)
         gather(1, 2, 1, LEFT)
         first_stage(BA, 0, 0, low, range(0, 1))
@@ -329,7 +329,7 @@ def tile_list_hashed_click_logits_kernel(tc, xT, wgt, offs, wa_words, wa_scales,
         gather(1, 3, 1)
         interleave("scalar", words["x", 1, 0], picked[1, 0], slice(0, 240))
         interleave("scalar", words["x", 1, 0], picked[1, 0], slice(240, W))
-        interleave("scalar", words["x", 1, 1], picked[1, 1], LEFT)
+        interleave("scalar", words["x", 1, 1], picked[1, 1], slice(0, 384))
         xq[1, 0], xq[1, 1] = operand("xq10"), operand("xq11")
         quantize(xq[1, 0], ("x", 1, 0), LEFT)
         quantize(xq[1, 0], ("x", 1, 0), RIGHT)
@@ -340,7 +340,7 @@ def tile_list_hashed_click_logits_kernel(tc, xT, wgt, offs, wa_words, wa_scales,
         for a in range(PASSES):
             for b in range(BLOCKS):
                 wbq[a, b] = operand("wbq%d%d" % (a, b))
-        interleave("vector", words["x", 1, 1], picked[1, 1], RIGHT)
+        interleave("vector", words["x", 1, 1], picked[1, 1], slice(384, W))
         round_wb(0, slice(0, 3))
         quantize(xq[1, 1], ("x", 1, 1))
         round_wb_seam(0)

@@ -43,7 +43,7 @@ def tile_list_hashed_click_logits_kernel(tc, xT, wgt, offs, wa_words, wa_scales,
         psum = ctx.enter_context(tc.psum_pool(name="psum", bufs=1))
 
         def placed(name, cols, dtype, at):
-            return arena.tile([P, cols], dtype, name=name, offset=at, align_bytes=64)
+            return arena.tile([P, cols], dtype, name=name, offset=at, align_bytes=256 if at % 256 == 0 else 64)
 
         def quad(name, n):
             return placed(name, PACK * W, F32, n * QUAD)
@@ -172,13 +172,16 @@ def tile_list_hashed_click_logits_kernel(tc, xT, wgt, offs, wa_words, wa_scales,
             nc.vector.tensor_tensor(slots(picked[a, h])[:, i, cols], window, weights[h][:, cols], MULT)
 
         def operand(name, scales_at=None, codes_at=None):
+            shift = 128 if name.startswith("w") else 0
             if codes_at is None:
-                codes = keep.tile([P, W], U32, name=name + "_codes", align_bytes=64)
+                codes = keep.tile([P, W + 64], U32, name=name + "_codes", align_bytes=256)[:, shift // 4 : shift // 4 + W]
             else:
-                codes = placed(name + "_codes", W, U32, codes_at)
+                codes = placed(name + "_codes", W, U32, codes_at)[:]
             if scales_at is None:
-                return codes, keep.tile([P, W], U8, name=name + "_scales", align_bytes=64)
-            return codes, placed(name + "_scales", W, U8, scales_at)
+                scales = keep.tile([P, W + 256], U8, name=name + "_scales", align_bytes=256)
+            else:
+                scales = placed(name + "_scales", W + 256, U8, scales_at)
+            return codes, scales[:, shift + 64 : shift + 64 + W]
 
         def quantize(target, key, cols=ALL):
             codes, scales = target
@@ -309,8 +312,8 @@ def tile_list_hashed_click_logits_kernel(tc, xT, wgt, offs, wa_words, wa_scales,
         for t in range(PACK):
             nc.tensor.transpose(banks[0][:, t * P : (t + 1) * P], bias_rows[:, t * P : (t + 1) * P], identity[:])
         nc.scalar.activation(out=bias[:], in_=banks[0][:].rearrange("p (t c) -> p t c", t=PACK)[:, :, 0 : BO + OUT_TILES], func=IDENTITY)
-        wa_codes = placed("wa_codes", PASSES * 2 * H, U8, 9 * QUAD)
-        wa_scale = placed("wa_scale", PASSES * H, U8, 9 * QUAD + 2 * ROW)
+        wa_codes = placed("wa_codes", PASSES * 2 * H, U8, 9 * QUAD + 128)
+        wa_scale = placed("wa_scale", PASSES * H, U8, 9 * QUAD + 2 * ROW + 192)
         for i in range(2):
             gather(1, i, 0)
             gather(1, i, 1)
@@ -370,7 +373,7 @@ def tile_list_hashed_click_logits_kernel(tc, xT, wgt, offs, wa_words, wa_scales,
         first_stage(BB, 1, 1, high)
         woq[0] = operand("woq0", a_at(1, 0, 2))
         woq[1] = operand("woq1", a_at(1, 0, 3))
-        hq[0, 0] = operand("hq00", a_at(1, 0, 3) + W)
+        hq[0, 0] = operand("hq00", a_at(1, 0, 3) + 2 * W)
         quantize(woq[0], ("wo", 0))
         quantize(woq[1], ("wo", 1))
         quantize(hq[0, 0], ("h", 0, 0))

@@ -79,7 +79,7 @@ def tile_list_hashed_click_logits_kernel(tc, xT, wgt, offs, wa_words, wa_scales,
         last_picked = placed("last_picked", WGT_AT + 2 * WGT_STEP, F32, 15 * QUAD)
         picked[1, 1] = last_picked[:, 0 : PACK * W]
         wb_raw = placed("wb_raw", PACK * PACK * W, F32, 11 * QUAD)
-        all_words = keep.tile([P, 65 * HALF], BF16, name="all_words", align_bytes=64)
+        all_words = keep.tile([P, 65 * HALF], BF16, name="all_words", align_bytes=256)
 
         def words_at(start):
             return all_words[:, start * HALF : start * HALF + PACK * W]
@@ -103,12 +103,12 @@ def tile_list_hashed_click_logits_kernel(tc, xT, wgt, offs, wa_words, wa_scales,
         wb_words = all_words[:, PACK * W : (PACK + 1) * PACK * W]
         wgt_halves = last_picked[:, WGT_AT:].rearrange("p (h c) -> p h c", h=HALVES)
         weights = [wgt_halves[:, h, 0:W] for h in range(HALVES)]
-        wgt_rows = keep.tile([P, 64], F32, name="wgt_rows", align_bytes=64)
+        wgt_rows = keep.tile([P, 64], F32, name="wgt_rows", align_bytes=256)
         wgt_turned = keep.tile([P, 64], F32, name="wgt_turned", align_bytes=64)
         wgt_spread = keep.tile([P, S], F32, name="wgt_spread", align_bytes=64)
-        wa_raw = keep.tile([P, PASSES * H // 2], I32, name="wa_raw")
-        wa_scale_raw = keep.tile([P, PASSES * H // 4], I32, name="wa_scale_raw")
-        bias_raw = keep.tile([BO + OUT_TILES, W], F32, name="bias_raw")
+        wa_raw = keep.tile([P, PASSES * H // 2], I32, name="wa_raw", align_bytes=256)
+        wa_scale_raw = keep.tile([P, PASSES * H // 4], I32, name="wa_scale_raw", align_bytes=256)
+        bias_raw = keep.tile([BO + OUT_TILES, W], F32, name="bias_raw", align_bytes=256)
         bias_rows = picked[0, 0][:, 0:W]
         identity = keep.tile([P, P], F32, name="identity")
         bias = keep.tile([P, PACK, BO + OUT_TILES], F32, name="bias")
@@ -367,8 +367,8 @@ def tile_list_hashed_click_logits_kernel(tc, xT, wgt, offs, wa_words, wa_scales,
         interleave("scalar", words["wo", 1], wo_raw[1])
         product(0, 0, low, placed("h_rows00", PACK * W, BF16, 6 * QUAD))
         first_stage(BB, 0, 1, low)
-        interleave_h("gpsimd", 0, 0, slice(0, 416))
-        interleave_h("scalar", 0, 0, slice(416, W))
+        interleave_h("gpsimd", 0, 0, slice(0, 384))
+        interleave_h("scalar", 0, 0, slice(384, W))
         product(1, 0, high, placed("h_rows10", PACK * W, BF16, 6 * QUAD + 2 * ROW))
         first_stage(BB, 1, 1, high)
         woq[0] = operand("woq0", a_at(1, 0, 2))
@@ -377,8 +377,8 @@ def tile_list_hashed_click_logits_kernel(tc, xT, wgt, offs, wa_words, wa_scales,
         quantize(woq[0], ("wo", 0))
         quantize(woq[1], ("wo", 1))
         quantize(hq[0, 0], ("h", 0, 0))
-        interleave_h("gpsimd", 1, 0, slice(0, 416))
-        interleave_h("scalar", 1, 0, slice(416, W))
+        interleave_h("gpsimd", 1, 0, slice(0, 384))
+        interleave_h("scalar", 1, 0, slice(384, W))
         product(0, 1, low, words_at(44), order=backwards)
         b_rows = placed("b_rows", PACK * W, F32, 10 * QUAD)
         for t in range(PACK):

@@ -79,7 +79,7 @@ def tile_list_hashed_click_logits_kernel(tc, xT, wgt, offs, wa_words, wa_scales,
         last_picked = placed("last_picked", WGT_AT + 2 * WGT_STEP, F32, 15 * QUAD)
         picked[1, 1] = last_picked[:, 0 : PACK * W]
         wb_raw = placed("wb_raw", PACK * PACK * W, F32, 11 * QUAD)
-        all_words = keep.tile([P, 65 * HALF], BF16, name="all_words", align_bytes=256)
+        all_words = keep.tile([P, 68 * HALF], BF16, name="all_words", align_bytes=256)
 
         def words_at(start):
             return all_words[:, start * HALF : start * HALF + PACK * W]
@@ -96,8 +96,8 @@ def tile_list_hashed_click_logits_kernel(tc, xT, wgt, offs, wa_words, wa_scales,
             ("wo", 0): words_at(28),
             ("wo", 1): words_at(48),
             ("h", 0, 0): words_at(56),
-            ("h", 1, 0): words_at(52),
-            ("h", 0, 1): words_at(57),
+            ("h", 1, 0): words_at(60),
+            ("h", 0, 1): words_at(54),
             ("h", 1, 1): words_at(0),
         }
         wb_words = all_words[:, PACK * W : (PACK + 1) * PACK * W]
@@ -241,8 +241,8 @@ def tile_list_hashed_click_logits_kernel(tc, xT, wgt, offs, wa_words, wa_scales,
             return (2 + 2 * h + b) * QUAD + t * ROW
 
         def a_out(b, h, accs):
-            if (b, h) == (1, 1):
-                whole = placed("a11", PACK * W, F32, a_at(b, h, 0))
+            if (b, h) == (0, 1):
+                whole = placed("a01", PACK * W, F32, a_at(b, h, 0))
                 a_view[b, h] = [slots(whole)[:, t, :] for t in range(PACK)]
                 a_view["whole"] = whole
             else:
@@ -254,7 +254,7 @@ def tile_list_hashed_click_logits_kernel(tc, xT, wgt, offs, wa_words, wa_scales,
             h_rows[b, h] = rows
             for t in order:
                 nc.vector.scalar_tensor_tensor(
-                    out=slots(rows)[:, t, cols],
+                    out=slots(rows)[:, t, :],
                     in0=accs[t][:, cols],
                     scalar=bias[:, t, BB + b : BB + b + 1],
                     in1=a_view[b, h][t][:, cols],
@@ -377,39 +377,41 @@ def tile_list_hashed_click_logits_kernel(tc, xT, wgt, offs, wa_words, wa_scales,
         quantize(woq[0], ("wo", 0))
         quantize(woq[1], ("wo", 1))
         quantize(hq[0, 0], ("h", 0, 0))
-        interleave_h("gpsimd", 1, 0, slice(0, 384))
-        interleave_h("scalar", 1, 0, slice(384, W))
-        product(0, 1, low, words_at(44), order=backwards)
-        b_rows = placed("b_rows", PACK * W, F32, 10 * QUAD)
+        ours, rest = slice(0, 192), slice(192, W)
+        b_rows = placed("b_rows", PACK * ours.stop, F32, 10 * QUAD)
         for t in range(PACK):
             nc.scalar.activation(
-                out=slots(b_rows)[:, t, RIGHT], in_=high[t][:, RIGHT], func=IDENTITY, bias=bias[:, t, BB + 1 : BB + 2]
+                out=slots(b_rows)[:, t, :], in_=low[t][:, ours], func=IDENTITY, bias=bias[:, t, BB : BB + 1]
             )
-        logit_passes(0, 0, low)
-        hq[1, 0] = operand("hq10", a_at(0, 1, 1), 7 * QUAD + 2 * ROW)
-        quantize(hq[1, 0], ("h", 1, 0))
-        logit_passes(1, 0, low)
-        interleave_h("gpsimd", 0, 1, slice(0, 192))
-        interleave_h("scalar", 0, 1, slice(192, W))
-        product(1, 1, high, placed("h_rows11", PACK * W, BF16, 7 * QUAD), LEFT)
-        hq[0, 1], hq[1, 1] = operand("hq01"), operand("hq11")
-        quantize(hq[0, 1], ("h", 0, 1))
-        nc.vector.tensor_tensor(
-            words["h", 1, 1][:, HALF * PACK : W * PACK].rearrange("p (c e t) -> p c t e", e=PACK, t=PACK),
-            slots(a_view["whole"])[:, :, RIGHT].rearrange("p t (c e) -> p c t e", e=PACK),
-            slots(b_rows)[:, :, RIGHT].rearrange("p t (c e) -> p c t e", e=PACK),
+        interleave_h("scalar", 1, 0, ALL)
+        nc.gpsimd.tensor_tensor(
+            words["h", 0, 1][:, 0 : PACK * ours.stop].rearrange("p (c t) -> p c t", t=PACK),
+            slots(a_view["whole"])[:, :, ours].rearrange("p t c -> p c t"),
+            slots(b_rows).rearrange("p t c -> p c t"),
             MULT,
         )
+        rows01 = all_words[:, 48 * HALF : 53 * HALF]
+        product(0, 1, low, rows01, rest)
+        logit_passes(0, 0, low)
+        left_rows = placed("left_rows", PACK * HALF, BF16, 7 * QUAD)
+        product(1, 1, high, left_rows, LEFT)
+        hq[1, 0], hq[0, 1], hq[1, 1] = operand("hq10"), operand("hq01"), operand("hq11")
+        quantize(hq[1, 0], ("h", 1, 0))
+        logit_passes(1, 0, low)
+        interleave("scalar", words["h", 0, 1][:, PACK * ours.stop :], rows01, slice(0, P))
+        interleave("gpsimd", words["h", 0, 1][:, PACK * ours.stop :], rows01, slice(P, 320))
+        interleave("scalar", words["h", 1, 1], left_rows, LEFT)
+        right_rows = all_words[:, 62 * HALF : 66 * HALF]
+        product(1, 1, high, right_rows, RIGHT)
+        quantize(hq[0, 1], ("h", 0, 1))
+        interleave("vector", words["h", 1, 1][:, PACK * HALF :], right_rows, LEFT)
         results = [quad("results%d" % h, 8 + h) for h in range(HALVES)]
-        logits_out(0, low, results[0], (), tiles=range(0, 2))
-        words["h left"] = placed("h11_left", PACK * HALF, BF16, 7 * QUAD + 2 * ROW)[:]
-        interleave("scalar", words["h left"], h_rows[1, 1], LEFT)
-        logits_out(0, low, results[0], (), tiles=range(2, 4))
-        logit_passes(0, 1, two_to_a_bank(6), RIGHT, 2)
+        logits_out(0, low, results[0], ())
         logit_passes(0, 1, two_to_a_bank(4), LEFT, 2)
+        logit_passes(0, 1, two_to_a_bank(6), RIGHT, 2)
+        quantize(hq[1, 1], ("h", 1, 1), LEFT)
+        logit_passes(1, 1, two_to_a_bank(4), LEFT, 2)
         quantize(hq[1, 1], ("h", 1, 1), RIGHT)
         logit_passes(1, 1, two_to_a_bank(6), RIGHT, 2)
-        quantize(hq[1, 1], "h left", LEFT)
-        logit_passes(1, 1, two_to_a_bank(4), LEFT, 2)
-        logits_out(1, two_to_a_bank(6), results[1], (0, 1), RIGHT, 2)
         logits_out(1, two_to_a_bank(4), results[1], (0, 1), LEFT, 2)
+        logits_out(1, two_to_a_bank(6), results[1], (0, 1), RIGHT, 2)

@@ -79,7 +79,7 @@ def tile_list_hashed_click_logits_kernel(tc, xT, wgt, offs, wa_words, wa_scales,
         last_picked = placed("last_picked", WGT_AT + 2 * WGT_STEP, F32, 15 * QUAD)
         picked[1, 1] = last_picked[:, 0 : PACK * W]
         wb_raw = placed("wb_raw", PACK * PACK * W, F32, 11 * QUAD)
-        all_words = keep.tile([P, 68 * HALF], BF16, name="all_words", align_bytes=256)
+        all_words = keep.tile([P, 70 * HALF], BF16, name="all_words", align_bytes=256)
 
         def words_at(start):
             return all_words[:, start * HALF : start * HALF + PACK * W]
@@ -96,8 +96,8 @@ def tile_list_hashed_click_logits_kernel(tc, xT, wgt, offs, wa_words, wa_scales,
             ("wo", 0): words_at(28),
             ("wo", 1): words_at(48),
             ("h", 0, 0): words_at(56),
-            ("h", 1, 0): words_at(60),
-            ("h", 0, 1): words_at(54),
+            ("h", 1, 0): words_at(62),
+            ("h", 0, 1): words_at(57),
             ("h", 1, 1): words_at(0),
         }
         wb_words = all_words[:, PACK * W : (PACK + 1) * PACK * W]
@@ -181,7 +181,7 @@ def tile_list_hashed_click_logits_kernel(tc, xT, wgt, offs, wa_words, wa_scales,
                 scales = keep.tile([P, W + 256], U8, name=name + "_scales", align_bytes=256)
             else:
                 scales = placed(name + "_scales", W + 256, U8, scales_at)
-            return codes, scales[:, shift + 64 : shift + 64 + W]
+            return codes, scales[:, 3 * shift // 2 : 3 * shift // 2 + W]
 
         def quantize(target, key, cols=ALL):
             codes, scales = target
@@ -377,20 +377,17 @@ def tile_list_hashed_click_logits_kernel(tc, xT, wgt, offs, wa_words, wa_scales,
         quantize(woq[0], ("wo", 0))
         quantize(woq[1], ("wo", 1))
         quantize(hq[0, 0], ("h", 0, 0))
-        ours, rest = slice(0, 192), slice(192, W)
+        ours, rest = slice(0, 160), slice(160, W)
         b_rows = placed("b_rows", PACK * ours.stop, F32, 10 * QUAD)
         for t in range(PACK):
             nc.scalar.activation(
                 out=slots(b_rows)[:, t, :], in_=low[t][:, ours], func=IDENTITY, bias=bias[:, t, BB : BB + 1]
             )
         interleave_h("scalar", 1, 0, ALL)
-        nc.gpsimd.tensor_tensor(
-            words["h", 0, 1][:, 0 : PACK * ours.stop].rearrange("p (c t) -> p c t", t=PACK),
-            slots(a_view["whole"])[:, :, ours].rearrange("p t c -> p c t"),
-            slots(b_rows).rearrange("p t c -> p c t"),
-            MULT,
-        )
-        rows01 = all_words[:, 48 * HALF : 53 * HALF]
+        our_rows = all_words[:, 109 * P : 114 * P]
+        nc.gpsimd.tensor_tensor(slots(our_rows), slots(a_view["whole"])[:, :, ours], slots(b_rows), MULT)
+        interleave("gpsimd", words["h", 0, 1], our_rows, ours)
+        rows01 = all_words[:, 96 * P : 107 * P]
         product(0, 1, low, rows01, rest)
         logit_passes(0, 0, low)
         left_rows = placed("left_rows", PACK * HALF, BF16, 7 * QUAD)
@@ -398,10 +395,10 @@ def tile_list_hashed_click_logits_kernel(tc, xT, wgt, offs, wa_words, wa_scales,
         hq[1, 0], hq[0, 1], hq[1, 1] = operand("hq10"), operand("hq01"), operand("hq11")
         quantize(hq[1, 0], ("h", 1, 0))
         logit_passes(1, 0, low)
-        interleave("scalar", words["h", 0, 1][:, PACK * ours.stop :], rows01, slice(0, P))
-        interleave("gpsimd", words["h", 0, 1][:, PACK * ours.stop :], rows01, slice(P, 320))
+        interleave("scalar", words["h", 0, 1][:, PACK * ours.stop :], rows01, slice(0, 160))
+        interleave("gpsimd", words["h", 0, 1][:, PACK * ours.stop :], rows01, slice(160, 352))
         interleave("scalar", words["h", 1, 1], left_rows, LEFT)
-        right_rows = all_words[:, 62 * HALF : 66 * HALF]
+        right_rows = all_words[:, 66 * HALF : 70 * HALF]
         product(1, 1, high, right_rows, RIGHT)
         quantize(hq[0, 1], ("h", 0, 1))
         interleave("vector", words["h", 1, 1][:, PACK * HALF :], right_rows, LEFT)

@@ -218,7 +218,7 @@ def tile_list_hashed_click_logits_kernel(tc, xT, wgt, offs, wa_words, wa_scales,
                 in_=src[:, :, 0:509:4, :].rearrange("p n (j g) i -> p n g j i", j=PACK),
             )
 
-        def first_stage(kind, b, h, accs, passes=range(PASSES), order=range(PACK)):
+        def first_stage(kind, b, h, accs, passes=range(PASSES), order=range(PACK), cols=ALL):
             for t in order:
                 for a in passes:
                     if kind == BA:
@@ -231,8 +231,8 @@ def tile_list_hashed_click_logits_kernel(tc, xT, wgt, offs, wa_words, wa_scales,
                         out=accs[t],
                         lhsT=codes,
                         lhsT_scale=scales,
-                        rhs=xq[a, h][0][:].bitcast(FP8X4),
-                        rhs_scale=xq[a, h][1][:],
+                        rhs=xq[a, h][0][:, cols].bitcast(FP8X4),
+                        rhs_scale=xq[a, h][1][:, cols],
                         start=(a == 0),
                         stop=(a == PASSES - 1),
                     )
@@ -255,7 +255,7 @@ def tile_list_hashed_click_logits_kernel(tc, xT, wgt, offs, wa_words, wa_scales,
             for t in order:
                 nc.vector.scalar_tensor_tensor(
                     out=slots(rows)[:, t, :],
-                    in0=accs[t][:, cols],
+                    in0=accs[t],
                     scalar=bias[:, t, BB + b : BB + b + 1],
                     in1=a_view[b, h][t][:, cols],
                     op0=ADD,
@@ -370,41 +370,43 @@ def tile_list_hashed_click_logits_kernel(tc, xT, wgt, offs, wa_words, wa_scales,
         interleave_h("gpsimd", 0, 0, slice(0, 384))
         interleave_h("scalar", 0, 0, slice(384, W))
         product(1, 0, high, placed("h_rows10", PACK * W, BF16, 6 * QUAD + 2 * ROW))
-        first_stage(BB, 1, 1, high)
+        first_stage(BB, 1, 1, two_to_a_bank(4), cols=LEFT)
+        first_stage(BB, 1, 1, two_to_a_bank(6), cols=RIGHT)
         woq[0] = operand("woq0", a_at(1, 0, 2))
         woq[1] = operand("woq1", a_at(1, 0, 3))
         hq[0, 0] = operand("hq00", a_at(1, 0, 3) + 2 * W)
         quantize(woq[0], ("wo", 0))
         quantize(woq[1], ("wo", 1))
         quantize(hq[0, 0], ("h", 0, 0))
-        ours, rest = slice(0, 160), slice(160, W)
+        ours, rest = slice(0, P), slice(P, W)
         b_rows = placed("b_rows", PACK * ours.stop, F32, 10 * QUAD)
         for t in range(PACK):
             nc.scalar.activation(
                 out=slots(b_rows)[:, t, :], in_=low[t][:, ours], func=IDENTITY, bias=bias[:, t, BB : BB + 1]
             )
         interleave_h("scalar", 1, 0, ALL)
-        our_rows = all_words[:, 109 * P : 114 * P]
+        our_rows = all_words[:, 110 * P : 114 * P]
         nc.gpsimd.tensor_tensor(slots(our_rows), slots(a_view["whole"])[:, :, ours], slots(b_rows), MULT)
         interleave("gpsimd", words["h", 0, 1], our_rows, ours)
-        rows01 = all_words[:, 96 * P : 107 * P]
-        product(0, 1, low, rows01, rest)
+        rows01 = all_words[:, 96 * P : 108 * P]
+        product(0, 1, [acc[:, rest] for acc in low], rows01, rest)
         logit_passes(0, 0, low)
         left_rows = placed("left_rows", PACK * HALF, BF16, 7 * QUAD)
-        product(1, 1, high, left_rows, LEFT)
+        product(1, 1, two_to_a_bank(4), left_rows, LEFT)
         hq[1, 0], hq[0, 1], hq[1, 1] = operand("hq10"), operand("hq01"), operand("hq11")
         quantize(hq[1, 0], ("h", 1, 0))
         logit_passes(1, 0, low)
-        interleave("scalar", words["h", 0, 1][:, PACK * ours.stop :], rows01, slice(0, 160))
-        interleave("gpsimd", words["h", 0, 1][:, PACK * ours.stop :], rows01, slice(160, 352))
+        interleave("scalar", words["h", 0, 1][:, PACK * ours.stop :], rows01, slice(0, 192))
+        interleave("gpsimd", words["h", 0, 1][:, PACK * ours.stop :], rows01, slice(192, 384))
+        quantize(hq[0, 1], ("h", 0, 1), LEFT)
+        logit_passes(0, 1, two_to_a_bank(4), LEFT, 2)
         interleave("scalar", words["h", 1, 1], left_rows, LEFT)
         right_rows = all_words[:, 66 * HALF : 70 * HALF]
-        product(1, 1, high, right_rows, RIGHT)
-        quantize(hq[0, 1], ("h", 0, 1))
+        product(1, 1, two_to_a_bank(6), right_rows, RIGHT)
+        quantize(hq[0, 1], ("h", 0, 1), RIGHT)
         interleave("vector", words["h", 1, 1][:, PACK * HALF :], right_rows, LEFT)
         results = [quad("results%d" % h, 8 + h) for h in range(HALVES)]
         logits_out(0, low, results[0], ())
-        logit_passes(0, 1, two_to_a_bank(4), LEFT, 2)
         logit_passes(0, 1, two_to_a_bank(6), RIGHT, 2)
         quantize(hq[1, 1], ("h", 1, 1), LEFT)
         logit_passes(1, 1, two_to_a_bank(4), LEFT, 2)

from contextlib import ExitStack

import concourse.mybir as mybir
from concourse.masks import make_identity

K, T, S, H, N = 1024, 2048, 1024, 1024, 512
FLOPS = 2 * S * (2 * K * H + H * N)

F32 = mybir.dt.float32
BF16 = mybir.dt.bfloat16
I32 = mybir.dt.int32
U32 = mybir.dt.uint32
U16 = mybir.dt.uint16
U8 = mybir.dt.uint8
FP8X4 = mybir.dt.float8_e4m3fn_x4
FP4X4 = mybir.dt.float4_e2m1fn_x4
MULT = mybir.AluOpType.mult
ADD = mybir.AluOpType.add
IDENTITY = mybir.ActivationFunctionType.Identity

P = 128
PACK = 4
W = 512
HALF = W // 2
GROUPS = 8
PASSES = K // W
BLOCKS = H // W
HALVES = S // W
OUT_TILES = N // P
BA, BB, BO = 0, 2, 32
ALL = slice(0, W)
LEFT, RIGHT = slice(0, HALF), slice(HALF, W)
QUAD = PACK * W * 4
ROW = W * 4
WGT_AT, WGT_STEP = 2 * W + HALF, W + HALF


def tile_list_hashed_click_logits_kernel(tc, xT, wgt, offs, wa_words, wa_scales, ba, wb, bb, wo, bo, out):
    nc = tc.nc
    with ExitStack() as ctx:
        keep = ctx.enter_context(tc.tile_pool(name="keep", bufs=1))
        arena = ctx.enter_context(tc.tile_pool(name="arena", bufs=1))
        psum = ctx.enter_context(tc.psum_pool(name="psum", bufs=1))

        def placed(name, cols, dtype, at):
            return arena.tile([P, cols], dtype, name=name, offset=at, align_bytes=256 if at % 256 == 0 else 64)

        def quad(name, n):
            return placed(name, PACK * W, F32, n * QUAD)

        def slots(rows):
            return rows[:, :].rearrange("p (t c) -> p t c", t=PACK)

        def copy_on(engine, dst, src):
            if engine == "vector":
                nc.vector.tensor_copy(out=dst, in_=src)
            elif engine == "scalar":
                nc.scalar.copy(out=dst, in_=src)
            else:
                nc.gpsimd.tensor_scalar(out=dst, in0=src, scalar1=1.0, scalar2=0.0, op0=MULT, op1=ADD)

        def interleave(engine, words, rows, cols=ALL):
            dst, src = words[:, cols.start * PACK : cols.stop * PACK], slots(rows)[:, :, cols]
            if engine == "gpsimd":
                copy_on(engine, dst.rearrange("p (c t) -> p c t", t=PACK), src.rearrange("p t c -> p c t"))
            else:
                copy_on(
                    engine,
                    dst.rearrange("p (c e t) -> p c t e", e=PACK, t=PACK),
                    src.rearrange("p t (c e) -> p c t e", e=PACK),
                )

        banks = [psum.tile([P, W], F32, name="bank%d" % n) for n in range(8)]
        low, high = [bank[:] for bank in banks[0:4]], [bank[:] for bank in banks[4:8]]

        offsets = keep.tile([P, S // 16], U16, name="offsets")
        planes = [quad("plane%d" % n, n) for n in range(PASSES * PACK)]
        picked = {(a, h): quad("picked%d%d" % (a, h), 8 + 2 * a + h) for a, h in ((0, 0), (0, 1), (1, 0))}
        last_picked = placed("last_picked", WGT_AT + 2 * WGT_STEP, F32, 15 * QUAD)
        picked[1, 1] = last_picked[:, 0 : PACK * W]
        wb_raw = placed("wb_raw", PACK * PACK * W, F32, 11 * QUAD)
        all_words = keep.tile([P, 70 * HALF], BF16, name="all_words", align_bytes=256)

        def words_at(start):
            return all_words[:, start * HALF : start * HALF + PACK * W]

        words = {
            ("x", 0, 0): words_at(40),
            ("x", 0, 1): words_at(48),
            ("wb", 0, 0): words_at(8),
            ("x", 1, 0): words_at(6),
            ("x", 1, 1): words_at(0),
            ("wb", 1, 0): words_at(16),
            ("wb", 0, 1): words_at(24),
            ("wb", 1, 1): words_at(32),
            ("wo", 0): words_at(28),
            ("wo", 1): words_at(48),
            ("h", 0, 0): words_at(56),
            ("h", 1, 0): words_at(62),
            ("h", 0, 1): words_at(57),
            ("h", 1, 1): words_at(0),
        }
        wb_words = all_words[:, PACK * W : (PACK + 1) * PACK * W]
        wgt_halves = last_picked[:, WGT_AT:].rearrange("p (h c) -> p h c", h=HALVES)
        weights = [wgt_halves[:, h, 0:W] for h in range(HALVES)]
        wgt_rows = keep.tile([P, 64], F32, name="wgt_rows", align_bytes=256)
        wgt_turned = keep.tile([P, 64], F32, name="wgt_turned", align_bytes=64)
        wgt_spread = keep.tile([P, S], F32, name="wgt_spread", align_bytes=64)
        wa_raw = keep.tile([P, PASSES * H // 2], I32, name="wa_raw", align_bytes=256)
        wa_scale_raw = keep.tile([P, PASSES * H // 4], I32, name="wa_scale_raw", align_bytes=256)
        bias_raw = keep.tile([BO + OUT_TILES, W], F32, name="bias_raw", align_bytes=256)
        bias_rows = picked[0, 0][:, 0:W]
        identity = keep.tile([P, P], F32, name="identity")
        bias = keep.tile([P, PACK, BO + OUT_TILES], F32, name="bias")

        def load_plane(a, i):
            rows = xT[a * W : (a + 1) * W, :].rearrange("(p i) t -> i p t", i=PACK)
            nc.sync.dma_start(out=planes[a * PACK + i][:], in_=rows[i])

        def load_wa_scales(r):
            nc.sync.dma_start(
                out=wa_scale_raw[r:P:32, :].rearrange("p (a n) -> p a n", a=PASSES),
                in_=wa_scales.bitcast(I32)[:, r:16:4, :].rearrange("a q n -> q a n"),
            )

        make_identity(nc, identity[:])
        nc.gpsimd.memset(wa_scale_raw[:], 0)

        nc.sync.dma_start(out=wgt_rows[:], in_=wgt[0:P:16, :].rearrange("g (u j) -> g u j", j=64))
        nc.sync.dma_start(offsets[:], offs)
        for i in range(PACK):
            load_plane(0, i)
        load_plane(1, 0)
        nc.sync.dma_start(out=bias_raw[BA : BA + BLOCKS, :], in_=ba.rearrange("(b r) -> b r", b=BLOCKS))
        nc.sync.dma_start(out=bias_raw[BB : BB + BLOCKS, :], in_=bb.rearrange("(b r) -> b r", b=BLOCKS))
        load_plane(1, 1)
        nc.sync.dma_start(out=bias_raw[BO : BO + OUT_TILES, 0:P], in_=bo.rearrange("(c p) -> c p", p=P))
        load_wa_scales(0)
        load_wa_scales(1)
        load_plane(1, 2)
        load_wa_scales(2)
        load_wa_scales(3)
        nc.sync.dma_start(
            out=wa_raw[:].rearrange("p (a n) -> p a n", a=PASSES),
            in_=wa_words.bitcast(I32).rearrange("a p n -> p a n"),
        )
        load_plane(1, 3)
        for b in range(BLOCKS):
            for a in range(PASSES):
                nc.sync.dma_start(
                    out=slots(wb_raw[:, (2 * b + a) * PACK * W : (2 * b + a + 1) * PACK * W]),
                    in_=wb[a * W : (a + 1) * W, b * W : (b + 1) * W].rearrange("(p j) r -> p j r", j=PACK),
                )

        for low_bit in range(2):
            part = slice(32 * low_bit, 32 * low_bit + 32)
            nc.vector.transpose(wgt_turned[:, part], wgt_rows[:, part])
        for h in range(HALVES):
            by_group = wgt_turned[:].rearrange("y (b g u) -> y u b g", b=2, g=2)[:, 8 * h : 8 * h + 8]
            nc.vector.tensor_copy(
                out=wgt_spread[:, h * W : (h + 1) * W].rearrange("y (u b g q) -> y u b g q", b=2, g=2, q=16),
                in_=by_group.unsqueeze(4).to_broadcast([P, 8, 2, 2, 16]),
            )
        for h in range(HALVES):
            nc.vector.transpose(weights[h], wgt_spread[:, h * W : (h + 1) * W])

        xq, wbq, woq, hq, a_view, h_rows = {}, {}, {}, {}, {}, {}

        def gather(a, i, h, cols=ALL):
            first = (h * W + cols.start) // 16
            window = planes[a * PACK + i][:].indirect(offsets[:, first : first + (cols.stop - cols.start) // 16])
            nc.vector.tensor_tensor(slots(picked[a, h])[:, i, cols], window, weights[h][:, cols], MULT)

        def operand(name, scales_at=None, codes_at=None):
            shift = 128 if name.startswith("w") else 0
            if codes_at is None:
                codes = keep.tile([P, W + 64], U32, name=name + "_codes", align_bytes=256)[:, shift // 4 : shift // 4 + W]
            else:
                codes = placed(name + "_codes", W, U32, codes_at)[:]
            if scales_at is None:
                scales = keep.tile([P, W + 256], U8, name=name + "_scales", align_bytes=256)
            else:
                scales = placed(name + "_scales", W + 256, U8, scales_at)
            return codes, scales[:, 3 * shift // 2 : 3 * shift // 2 + W]

        def quantize(target, key, cols=ALL):
            codes, scales = target
            nc.vector.quantize_mx(
                out=codes[:, cols].bitcast(FP8X4), scales=scales[:, cols], in_=words[key][:, cols.start * PACK : cols.stop * PACK]
            )

        def order_wa_codes(a):
            part = slice(a * W, (a + 1) * W)
            nc.scalar.copy(
                out=wa_codes[:].bitcast(U32)[:, part].rearrange("p (c t g e) -> p c t g e", t=PACK, g=32, e=2),
                in_=wa_raw[:].bitcast(U32)[:, part].rearrange("p (c g t e) -> p c t g e", t=PACK, g=32, e=2),
            )

        def order_wa_scales():
            nc.scalar.copy(
                out=wa_scale[:].bitcast(U32).rearrange("p (c t g e) -> p c g t e", t=PACK, g=8, e=4),
                in_=wa_scale_raw[:].bitcast(U32).rearrange("p (c g e t) -> p c g t e", t=PACK, g=8, e=4),
            )

        def round_wb(quarter, tiles):
            dst = wb_words.rearrange("p (n t g i j) -> p n g t j i", n=PACK, t=PACK, i=PACK, j=PACK)
            src = wb_raw[:].rearrange("p (n j g t i) -> p n g t j i", n=PACK, j=PACK, t=PACK, i=PACK)
            nc.vector.tensor_copy(out=dst[:, quarter, :, tiles], in_=src[:, quarter, :, tiles])

        def round_wb_seam(quarter):
            dst = wb_words[:, quarter * PACK * W + 3 * W : (quarter + 1) * PACK * W + W]
            reach = PACK * W - 3 * PACK
            first = quarter * PACK * W + 3 * PACK
            src = wb_raw[:, first : first + 2 * reach].rearrange("p (n x) -> p n x", n=2)
            src = src.rearrange("p n (y i) -> p n y i", i=PACK)
            nc.vector.tensor_copy(
                out=dst.rearrange("p (n g i j) -> p n g j i", n=2, i=PACK, j=PACK),
                in_=src[:, :, 0:509:4, :].rearrange("p n (j g) i -> p n g j i", j=PACK),
            )

        def first_stage(kind, b, h, accs, passes=range(PASSES), order=range(PACK), cols=ALL):
            for t in order:
                for a in passes:
                    if kind == BA:
                        col = a * H + b * W + t * P
                        codes, scales = wa_codes[:, 2 * col : 2 * (col + P)].bitcast(FP4X4), wa_scale[:, col : col + P]
                    else:
                        tile = slice(t * P, (t + 1) * P)
                        codes, scales = wbq[a, b][0][:, tile].bitcast(FP8X4), wbq[a, b][1][:, tile]
                    nc.tensor.matmul_mx(
                        out=accs[t],
                        lhsT=codes,
                        lhsT_scale=scales,
                        rhs=xq[a, h][0][:, cols].bitcast(FP8X4),
                        rhs_scale=xq[a, h][1][:, cols],
                        start=(a == 0),
                        stop=(a == PASSES - 1),
                    )

        def a_at(b, h, t):
            return (2 + 2 * h + b) * QUAD + t * ROW

        def a_out(b, h, accs):
            if (b, h) == (0, 1):
                whole = placed("a01", PACK * W, F32, a_at(b, h, 0))
                a_view[b, h] = [slots(whole)[:, t, :] for t in range(PACK)]
                a_view["whole"] = whole
            else:
                a_view[b, h] = [placed("a%d%d_%d" % (b, h, t), W, F32, a_at(b, h, t))[:] for t in range(PACK)]
            for t in range(PACK):
                nc.scalar.activation(out=a_view[b, h][t], in_=accs[t], func=IDENTITY, bias=bias[:, t, BA + b : BA + b + 1])

        def product(b, h, accs, rows, cols=ALL, order=range(PACK)):
            h_rows[b, h] = rows
            for t in order:
                nc.vector.scalar_tensor_tensor(
                    out=slots(rows)[:, t, :],
                    in0=accs[t],
                    scalar=bias[:, t, BB + b : BB + b + 1],
                    in1=a_view[b, h][t][:, cols],
                    op0=ADD,
                    op1=MULT,
                )

        def interleave_h(engine, b, h, cols):
            interleave(engine, words["h", b, h], h_rows[b, h], cols)

        def logit_passes(b, h, accs, cols=ALL, per_bank=1):
            for c in range(OUT_TILES):
                nc.tensor.matmul_mx(
                    out=accs[c],
                    lhsT=woq[b][0][:, c * P : (c + 1) * P].bitcast(FP8X4),
                    lhsT_scale=woq[b][1][:, c * P : (c + 1) * P],
                    rhs=hq[b, h][0][:, cols].bitcast(FP8X4),
                    rhs_scale=hq[b, h][1][:, cols],
                    start=(b == 0 and c % per_bank == 0),
                    stop=(b == BLOCKS - 1 and c % per_bank == per_bank - 1),
                )

        def logits_out(h, accs, result_rows, on_vector, cols=ALL, per_store=1, tiles=range(OUT_TILES)):
            rows = out[:, h * W + cols.start : h * W + cols.stop].rearrange("(c p) j -> p c j", p=P)
            for c in tiles:
                result = slots(result_rows)[:, c, cols]
                bo_col = bias[:, 0, BO + c : BO + c + 1]
                if c in on_vector:
                    nc.vector.tensor_scalar(out=result, in0=accs[c], scalar1=bo_col, scalar2=None, op0=ADD)
                else:
                    nc.scalar.activation(out=result, in_=accs[c], func=IDENTITY, bias=bo_col)
                if (c + 1) % per_store == 0:
                    done = slice(c + 1 - per_store, c + 1)
                    nc.sync.dma_start(out=rows[:, done, :], in_=slots(result_rows)[:, done, cols])

        def two_to_a_bank(first_bank):
            return [banks[first_bank + n // 2][:, (n % 2) * HALF : (n % 2 + 1) * HALF] for n in range(4)]

        backwards = range(PACK - 1, -1, -1)
        for i in range(PACK):
            for h in range(HALVES):
                gather(0, i, h)
        wo_raw = {b: quad("wo_raw%d" % b, b) for b in range(BLOCKS)}
        for b in range(BLOCKS):
            wo_rows = wo[b * W : (b + 1) * W, :].rearrange("(g t i) n -> t g i n", t=PACK, i=PACK)
            for t in range(PACK):
                nc.sync.dma_start(out=slots(wo_raw[b])[:, t, :], in_=wo_rows[t])
        for h in range(HALVES):
            interleave("scalar", words["x", 0, h], picked[0, h])
        nc.scalar.copy(
            out=bias_rows[0:4, :].rearrange("p (t g i) -> p t g i", t=PACK, i=PACK),
            in_=bias_raw[0:4, :].rearrange("p (g t i) -> p t g i", t=PACK, i=PACK),
        )
        nc.scalar.copy(out=bias_rows[BO : BO + OUT_TILES, 0:P], in_=bias_raw[BO : BO + OUT_TILES, 0:P])
        for t in range(PACK):
            nc.tensor.transpose(banks[0][:, t * P : (t + 1) * P], bias_rows[:, t * P : (t + 1) * P], identity[:])
        nc.scalar.activation(out=bias[:], in_=banks[0][:].rearrange("p (t c) -> p t c", t=PACK)[:, :, 0 : BO + OUT_TILES], func=IDENTITY)
        wa_codes = placed("wa_codes", PASSES * 2 * H, U8, 9 * QUAD + 128)
        wa_scale = placed("wa_scale", PASSES * H, U8, 9 * QUAD + 2 * ROW + 192)
        for i in range(2):
            gather(1, i, 0)
            gather(1, i, 1)
            xq[0, i] = operand("xq0%d" % i)
            quantize(xq[0, i], ("x", 0, i))
        order_wa_scales()
        order_wa_codes(1)
        order_wa_codes(0)
        gather(1, 2, 0)
        gather(1, 2, 1, LEFT)
        first_stage(BA, 0, 0, low, range(0, 1))
        first_stage(BA, 1, 0, high, range(0, 1))
        gather(1, 3, 0, LEFT)
        gather(1, 3, 0, RIGHT)
        gather(1, 2, 1, RIGHT)
        gather(1, 3, 1)
        interleave("scalar", words["x", 1, 0], picked[1, 0], slice(0, 240))
        interleave("scalar", words["x", 1, 0], picked[1, 0], slice(240, W))
        interleave("scalar", words["x", 1, 1], picked[1, 1], slice(0, 384))
        xq[1, 0], xq[1, 1] = operand("xq10"), operand("xq11")
        quantize(xq[1, 0], ("x", 1, 0), LEFT)
        quantize(xq[1, 0], ("x", 1, 0), RIGHT)
        first_stage(BA, 0, 0, low, range(1, 2))
        first_stage(BA, 1, 0, high, range(1, 2))
        a_out(0, 0, low)
        a_out(1, 0, high)
        for a in range(PASSES):
            for b in range(BLOCKS):
                wbq[a, b] = operand("wbq%d%d" % (a, b))
        interleave("vector", words["x", 1, 1], picked[1, 1], slice(384, W))
        round_wb(0, slice(0, 3))
        quantize(xq[1, 1], ("x", 1, 1))
        round_wb_seam(0)
        round_wb(1, slice(1, 3))
        quantize(wbq[0, 0], ("wb", 0, 0))
        round_wb_seam(1)
        round_wb(2, slice(1, 3))
        quantize(wbq[1, 0], ("wb", 1, 0))
        round_wb_seam(2)
        round_wb(3, slice(1, 4))
        quantize(wbq[0, 1], ("wb", 0, 1))
        quantize(wbq[1, 1], ("wb", 1, 1))
        first_stage(BA, 0, 1, low)
        a_out(0, 1, low)
        first_stage(BA, 1, 1, high)
        a_out(1, 1, high)
        first_stage(BB, 0, 0, low)
        first_stage(BB, 1, 0, high)
        interleave("gpsimd", words["wo", 0], wo_raw[0], slice(0, 416))
        interleave("scalar", words["wo", 0], wo_raw[0], slice(416, W))
        interleave("scalar", words["wo", 1], wo_raw[1])
        product(0, 0, low, placed("h_rows00", PACK * W, BF16, 6 * QUAD))
        first_stage(BB, 0, 1, low)
        interleave_h("gpsimd", 0, 0, slice(0, 384))
        interleave_h("scalar", 0, 0, slice(384, W))
        product(1, 0, high, placed("h_rows10", PACK * W, BF16, 6 * QUAD + 2 * ROW))
        first_stage(BB, 1, 1, two_to_a_bank(4), cols=LEFT)
        first_stage(BB, 1, 1, two_to_a_bank(6), cols=RIGHT)
        woq[0] = operand("woq0", a_at(1, 0, 2))
        woq[1] = operand("woq1", a_at(1, 0, 3))
        hq[0, 0] = operand("hq00", a_at(1, 0, 3) + 2 * W)
        quantize(woq[0], ("wo", 0))
        quantize(woq[1], ("wo", 1))
        quantize(hq[0, 0], ("h", 0, 0))
        ours, rest = slice(0, P), slice(P, W)
        b_rows = placed("b_rows", PACK * ours.stop, F32, 10 * QUAD)
        for t in range(PACK):
            nc.scalar.activation(
                out=slots(b_rows)[:, t, :], in_=low[t][:, ours], func=IDENTITY, bias=bias[:, t, BB : BB + 1]
            )
        interleave_h("scalar", 1, 0, ALL)
        our_rows = all_words[:, 110 * P : 114 * P]
        nc.gpsimd.tensor_tensor(slots(our_rows), slots(a_view["whole"])[:, :, ours], slots(b_rows), MULT)
        interleave("gpsimd", words["h", 0, 1], our_rows, ours)
        rows01 = all_words[:, 96 * P : 108 * P]
        product(0, 1, [acc[:, rest] for acc in low], rows01, rest)
        logit_passes(0, 0, low)
        left_rows = placed("left_rows", PACK * HALF, BF16, 7 * QUAD)
        product(1, 1, two_to_a_bank(4), left_rows, LEFT)
        hq[1, 0], hq[0, 1], hq[1, 1] = operand("hq10"), operand("hq01"), operand("hq11")
        quantize(hq[1, 0], ("h", 1, 0))
        logit_passes(1, 0, low)
        interleave("scalar", words["h", 0, 1][:, PACK * ours.stop :], rows01, slice(0, 192))
        interleave("gpsimd", words["h", 0, 1][:, PACK * ours.stop :], rows01, slice(192, 384))
        quantize(hq[0, 1], ("h", 0, 1), LEFT)
        logit_passes(0, 1, two_to_a_bank(4), LEFT, 2)
        interleave("scalar", words["h", 1, 1], left_rows, LEFT)
        right_rows = all_words[:, 66 * HALF : 70 * HALF]
        product(1, 1, two_to_a_bank(6), right_rows, RIGHT)
        quantize(hq[0, 1], ("h", 0, 1), RIGHT)
        interleave("vector", words["h", 1, 1][:, PACK * HALF :], right_rows, LEFT)
        results = [quad("results%d" % h, 8 + h) for h in range(HALVES)]
        logits_out(0, low, results[0], ())
        logit_passes(0, 1, two_to_a_bank(6), RIGHT, 2)
        quantize(hq[1, 1], ("h", 1, 1), LEFT)
        logit_passes(1, 1, two_to_a_bank(4), LEFT, 2)
        quantize(hq[1, 1], ("h", 1, 1), RIGHT)
        logit_passes(1, 1, two_to_a_bank(6), RIGHT, 2)
        logits_out(1, two_to_a_bank(4), results[1], (0, 1), LEFT, 2)
        logits_out(1, two_to_a_bank(6), results[1], (0, 1), RIGHT, 2)
